import numpy as np
import ml_dtypes


def mxq(x, axis, fmt="e4m3"):
    dtype, down = {"e4m3": (ml_dtypes.float8_e4m3fn, 7), "e5m2": (ml_dtypes.float8_e5m2, 14)}[fmt]
    v = np.moveaxis(np.asarray(x, np.float32).astype(ml_dtypes.bfloat16).astype(np.float64), axis, -1)
    blocks = v.reshape(v.shape[:-1] + (-1, 32))
    amax = np.abs(blocks).max(-1, keepdims=True)
    byte = np.maximum(np.where(amax > 0, np.frexp(amax)[1] - 1 + 127, 0) - down, 1)
    scale = np.exp2(byte - 127.0)
    codes = (blocks / scale).astype(np.float32).astype(dtype).astype(np.float64)
    return np.moveaxis((codes * scale).reshape(v.shape), -1, axis)


WIDE = False


def mx_kscale(k):
    if not WIDE:
        return np.ones(k)
    levels = np.array([10, -10, 5, -5, 0])
    if k % 512:
        return np.exp2(np.random.permutation(np.resize(levels, k // 32))).repeat(32)
    a = np.empty((k // 512, 16))
    for p in range(k // 512):
        a[p, :8] = np.random.permutation(np.resize(levels, 8))
        for g in range(8):
            far = levels[np.abs(levels - a[p, g]) >= 10]
            a[p, g + 8] = far[np.random.randint(len(far))]
    return np.exp2(a.ravel()).repeat(32)


def f64(x):
    return np.asarray(x).astype(np.float64)


def striped(idx):
    return np.tile(idx.reshape(-1, 16).T, (8, 1)).astype(np.uint16)


def unstriped(offs):
    return offs[:16].T.reshape(-1).astype(np.int64)


E2M1 = np.array([0.0, 0.5, 1.0, 1.5, 2.0, 3.0, 4.0, 6.0, -0.0, -0.5, -1.0, -1.5, -2.0, -3.0, -4.0, -6.0])


def pack_weight(w, fmt):
    k, n = w.shape
    w = f64(np.asarray(w, np.float32).astype(ml_dtypes.bfloat16)).reshape(k // 32, 32, n)
    amax = np.abs(w).max(1)
    if fmt == "e4m3":
        byte = np.frexp(amax)[1] - 1 + 127 - 7
    else:
        mant, ex = np.frexp(amax / 6.0)
        byte = np.where(mant > 0.5, ex, ex - 1) + 127
    byte = np.clip(np.where(amax > 0, byte, 1), 1, 254)
    scaled = (w * np.exp2(127.0 - byte)[:, None, :]).reshape(k, n).astype(np.float32)
    by_word = np.ascontiguousarray(scaled.reshape(k // 512, 128, 4, n).transpose(0, 1, 3, 2))
    if fmt == "e4m3":
        words = by_word.astype(ml_dtypes.float8_e4m3fn).view(np.uint8)
    else:
        c = by_word.astype(ml_dtypes.float4_e2m1fn).view(np.uint8) & 0xF
        words = (c[..., 0::2] | (c[..., 1::2] << 4)).reshape(k // 512, 128, 2 * n)
    return np.ascontiguousarray(words), np.ascontiguousarray(byte.astype(np.uint8).reshape(k // 512, 16, n))


def unpack_weight(words, scales, fmt):
    g, _, n = scales.shape
    words = np.ascontiguousarray(words).reshape(g, 128, n, -1)
    if fmt == "e4m3":
        vals = words.view(ml_dtypes.float8_e4m3fn).astype(np.float64)
    else:
        nib = np.empty((g, 128, n, 4), np.uint8)
        nib[..., 0::2] = words & 0xF
        nib[..., 1::2] = words >> 4
        vals = E2M1[nib]
    vals = vals * np.repeat(np.exp2(scales.astype(np.float64) - 127.0), 8, axis=1)[..., None]
    return vals.transpose(0, 1, 3, 2).reshape(g * 512, n)


def sigmoid(v):
    return 1.0 / (1.0 + np.exp(-np.maximum(v, -700.0)))


K, T, E, C, H, N, TOP = 1024, 512, 6, 256, 512, 512, 3


def by_expert(wq, xq):
    return np.concatenate([wq[e].T @ xq[:, e * C:(e + 1) * C] for e in range(E)], axis=1)


def setup_inputs():
    n = np.random.standard_normal
    s = mx_kscale(K)
    u = mx_kscale(H)
    deal = np.repeat(np.arange(E), C).reshape(TOP, T)[:, np.random.permutation(T)]
    deal = np.take_along_axis(deal, np.argsort(np.random.rand(TOP, T), axis=0), axis=0)
    for _ in range(8):
        s_, t_ = np.random.permutation(T).reshape(2, -1); r = np.random.randint(TOP, size=T // 2); x, y = deal[r, s_].copy(), deal[r, t_].copy()
        ok = ~((deal[:, s_] == y).any(0) | (deal[:, t_] == x).any(0)); deal[r[ok], s_[ok]] = y[ok]; deal[r[ok], t_[ok]] = x[ok]
    order = np.lexsort((np.random.rand(TOP * T), deal.reshape(-1)))
    slot_token = order % T; pos = np.empty(TOP * T, np.int64); pos[order] = np.arange(TOP * T); pos = pos.reshape(TOP, T)
    g = np.random.uniform(0.5, 1.5, (TOP, T)); g = g / g.sum(0)
    x = pack_weight(n((K, T)) * s[:, None], "e4m3")
    w2 = [pack_weight(m, "e2m1") for m in n((E, H, N)) / np.sqrt(H) / u[None, :, None]]
    return {
        "x_words": x[0],
        "x_scales": x[1],
        "w1": (n((K, H)) / np.sqrt(K) / s[:, None]).astype(np.float32),
        "w3": (n((K, H)) / np.sqrt(K) / s[:, None] * u).astype(np.float32),
        "w2_words": np.stack([m[0] for m in w2]),
        "w2_scales": np.stack([m[1] for m in w2]),
        "gate": np.stack([np.tile(r, (128, 1)) for r in g]).astype(np.float32),
        "offs": striped(slot_token),
        "pos1": striped(pos[0]),
        "pos2": striped(pos[1]),
        "pos3": striped(pos[2]),
    }


def reference(x_words, x_scales, w1, w3, w2_words, w2_scales, gate, offs, pos1, pos2, pos3):
    w1q = mxq(f64(w1), 0, "e4m3")
    w3q = mxq(f64(w3), 0, "e4m3")
    w2 = np.stack([unpack_weight(w2_words[e], w2_scales[e], "e2m1") for e in range(E)])
    idx = unstriped(offs)
    x = unpack_weight(x_words, x_scales, "e4m3")
    h = sigmoid(w1q.T @ x) * (w3q.T @ x)
    y = by_expert(w2, mxq(h[:, idx], 0, "e4m3"))
    out = sum(f64(gate[r, :1]) * y[:, unstriped(p)] for r, p in enumerate((pos1, pos2, pos3)))
    return out

@@ -1,0 +1,253 @@
+from contextlib import ExitStack
+
+import concourse.mybir as mybir
+from concourse.masks import make_identity
+
+K, T, E, C, H, N, TOP = 1024, 512, 6, 256, 512, 512, 3
+S = E * C
+FLOPS = 2 * (2 * K * H * T + H * N * S)
+
+F32 = mybir.dt.float32
+BF16 = mybir.dt.bfloat16
+I32 = mybir.dt.int32
+U32 = mybir.dt.uint32
+U16 = mybir.dt.uint16
+U8 = mybir.dt.uint8
+FP8X4 = mybir.dt.float8_e4m3fn_x4
+FP4X4 = mybir.dt.float4_e2m1fn_x4
+MULT = mybir.AluOpType.mult
+ADD = mybir.AluOpType.add
+SIGMOID = mybir.ActivationFunctionType.Sigmoid
+
+P = 128
+PACK = 4
+K_PASS = P * PACK
+PASSES = K // K_PASS
+N_TILES = N // P
+BANK = 512
+HALF = H // 2
+LAST_SPLIT = 104
+
+
+def tile_moe_sup_glu_sigmoid_kernel(
+    tc, x_words, x_scales, w1, w3, w2_words, w2_scales, gate, offs, pos1, pos2, pos3, out
+):
+    nc = tc.nc
+    with ExitStack() as ctx:
+        keep = ctx.enter_context(tc.tile_pool(name="keep", bufs=1))
+        ring = ctx.enter_context(tc.tile_pool(name="ring", bufs=2))
+        picks = ctx.enter_context(tc.tile_pool(name="picks", bufs=3))
+        psum = ctx.enter_context(tc.psum_pool(name="psum", bufs=1))
+
+        def bank(b):
+            return psum.tile([P, BANK], F32, name="bank%d" % b)
+
+        x_codes = keep.tile([P, PASSES, T], U32, align_bytes=64)
+        x_plane = keep.tile([P, PASSES, T], U8, align_bytes=64)
+        w2_codes = keep.tile([P, E, 2 * N], U8, align_bytes=64)
+        w2_plane = keep.tile([P, E, N], U8, align_bytes=64)
+        gates = keep.tile([P, TOP, T], F32)
+        slot_token = keep.tile([P, S // 16], U16)
+        token_slot = [keep.tile([P, T // 16], U16, name="token_slot%d" % r) for r in range(TOP)]
+        ident = keep.tile([P, P], F32)
+
+        nc.vector.memset(x_plane[:].rearrange("p s t -> p (s t)").bitcast(I32), 0)
+        nc.vector.memset(w2_plane[:].rearrange("p e n -> p (e n)").bitcast(I32), 0)
+        make_identity(nc, ident[:])
+
+        raw = {}
+
+        def load_w(name, w, s):
+            rows = w[s * K_PASS : (s + 1) * K_PASS, :].rearrange("(p j) c -> p j c", j=PACK)
+            for half in range(2):
+                raw[name, s, half] = keep.tile([P, PACK, HALF], F32, name="raw_%s%d%d" % (name, s, half))
+                nc.sync.dma_start(out=raw[name, s, half][:], in_=rows[:, :, half * HALF : (half + 1) * HALF])
+
+        def load_x(s):
+            nc.sync.dma_start(
+                out=x_codes[:, s, :].bitcast(I32),
+                in_=x_words[s].rearrange("p t d -> p (t d)").bitcast(I32),
+            )
+
+        def load_plane(plane, rows):
+            for r in range(4):
+                nc.sync.dma_start(
+                    out=plane[r:P:32, :, :].bitcast(I32),
+                    in_=rows[:, r:16:4, :].rearrange("g q w -> q g w").bitcast(I32),
+                )
+
+        load_w("w1", w1, 0)
+        load_plane(x_plane, x_scales)
+        load_x(0)
+        load_w("w1", w1, 1)
+        load_x(1)
+        load_w("w3", w3, 0)
+        load_w("w3", w3, 1)
+        nc.sync.dma_start(slot_token[:], offs)
+        load_plane(w2_plane, w2_scales.rearrange("e s b n -> (e s) b n"))
+        nc.sync.dma_start(
+            out=w2_codes[:].bitcast(I32),
+            in_=w2_words.rearrange("e s p b -> p (e s) b").bitcast(I32),
+        )
+        for r, pos in enumerate((pos1, pos2, pos3)):
+            nc.sync.dma_start(token_slot[r][:], pos)
+        nc.sync.dma_start(out=gates[:], in_=gate.rearrange("r p t -> p r t"))
+
+        def regroup(copy, grouped, name, s, m0, m1):
+            half = m0 // (HALF // PACK)
+            base = half * (HALF // PACK)
+            copy(
+                out=grouped[:, :, m0:m1, :].rearrange("p t m j -> p m j t"),
+                in_=raw[name, s, half][:].rearrange("p j (m t) -> p m j t", t=PACK)[:, m0 - base : m1 - base],
+            )
+
+        def first_layer(name, banks, shares, pieces):
+            for s in range(PASSES):
+                grouped = keep.tile([P, PACK, P, PACK], BF16, name="grouped_%s%d" % (name, s), align_bytes=64)
+                codes = keep.tile([P, H], U32, name="codes_%s%d" % (name, s), align_bytes=64)
+                plane = keep.tile([P, H], U8, name="plane_%s%d" % (name, s), align_bytes=64)
+                for copy, m0, m1 in shares[s]:
+                    regroup(copy, grouped, name, s, m0, m1)
+                width = H // pieces[s]
+                flat = grouped[:].rearrange("p t m j -> p (t m j)")
+                for c in range(0, H, width):
+                    nc.vector.quantize_mx(
+                        out=codes[:, c : c + width].bitcast(FP8X4),
+                        scales=plane[:, c : c + width],
+                        in_=flat[:, PACK * c : PACK * (c + width)],
+                    )
+                for t in range(PACK):
+                    nc.tensor.matmul_mx(
+                        out=banks[t][:],
+                        lhsT=codes[:, t * P : (t + 1) * P].bitcast(FP8X4),
+                        lhsT_scale=plane[:, t * P : (t + 1) * P],
+                        rhs=x_codes[:, s, :].bitcast(FP8X4),
+                        rhs_scale=x_plane[:, s, :],
+                        start=(s == 0),
+                        stop=(s == PASSES - 1),
+                    )
+
+        on_vector, on_scalar = nc.vector.tensor_copy, nc.scalar.copy
+        mid = P // 2
+        a_banks = [bank(t) for t in range(PACK)]
+        both = [(on_vector, 0, mid), (on_scalar, mid, P)]
+        first_layer("w1", a_banks, [both, both], [1, 1])
+        sig = keep.tile([P, PACK, T], F32)
+        for t in range(PACK):
+            nc.scalar.activation(out=sig[:, t, :], in_=a_banks[t][:], func=SIGMOID)
+        b_banks = [bank(PACK + t) for t in range(PACK)]
+        first_layer(
+            "w3",
+            b_banks,
+            [
+                [(on_vector, 0, mid), (on_vector, mid, P)],
+                [(on_vector, 0, mid), (on_vector, mid, LAST_SPLIT), (on_scalar, LAST_SPLIT, P)],
+            ],
+            [1, 2],
+        )
+
+        h_pairs = [keep.tile([P, T, 2], BF16, name="h_pairs%d" % u) for u in range(2)]
+        for t in range(PACK):
+            nc.vector.tensor_tensor(out=h_pairs[t // 2][:, :, t % 2], in0=b_banks[t][:], in1=sig[:, t, :], op=MULT)
+        h_window = [h_pairs[u][:].rearrange("p t e -> p (t e)").bitcast(U32) for u in range(2)]
+
+        h_codes = keep.tile([P, S], U32, align_bytes=64)
+        h_plane = keep.tile([P, S], U8, align_bytes=64)
+        y = [keep.tile([P, S], F32, name="y%d" % nt) for nt in range(N_TILES)]
+
+        def gather_h(e):
+            picked = picks.tile([P, 2, 2 * C], BF16)
+            for u in range(2):
+                nc.vector.tensor_copy(
+                    out=picked[:, u, :].bitcast(U32),
+                    in_=h_window[u].indirect(slot_token[:, e * C // 16 : (e + 1) * C // 16]),
+                )
+            h_slots = keep.tile([P, C, 2, 2], BF16, name="h_slots%d" % e, align_bytes=64)
+            nc.scalar.copy(out=h_slots[:], in_=picked[:].rearrange("p u (c e) -> p c u e", e=2))
+            return h_slots
+
+        def expert_product(e, nt, acc):
+            slots = slice(e * C, (e + 1) * C)
+            nc.tensor.matmul_mx(
+                out=acc[:, (e % 2) * C : (e % 2 + 1) * C],
+                lhsT=w2_codes[:, e, 2 * nt * P : 2 * (nt + 1) * P].bitcast(FP4X4),
+                lhsT_scale=w2_plane[:, e, nt * P : (nt + 1) * P],
+                rhs=h_codes[:, slots].bitcast(FP8X4),
+                rhs_scale=h_plane[:, slots],
+                start=True,
+                stop=True,
+            )
+
+        accs = {}
+
+        def finish_expert(e, h_slots):
+            slots = slice(e * C, (e + 1) * C)
+            nc.vector.quantize_mx(
+                out=h_codes[:, slots].bitcast(FP8X4),
+                scales=h_plane[:, slots],
+                in_=h_slots[:].rearrange("p c u e -> p (c u e)"),
+            )
+            if e % 2 == 0:
+                accs[e // 2] = bank(e // 2)
+            acc = accs[e // 2]
+            expert_product(e, 0, acc)
+            nc.scalar.copy(out=y[0][:, slots], in_=acc[:, (e % 2) * C : (e % 2 + 1) * C])
+
+        waiting = gather_h(0)
+        for e in range(1, E):
+            h_slots = gather_h(e)
+            finish_expert(e - 1, waiting)
+            waiting = h_slots
+        finish_expert(E - 1, waiting)
+
+        def slot_results(nt):
+            for g in range(E // 2):
+                acc = bank((nt * (E // 2) + g) % PACK)
+                expert_product(2 * g, nt, acc)
+                expert_product(2 * g + 1, nt, acc)
+                nc.scalar.copy(out=y[nt][:, g * BANK : (g + 1) * BANK], in_=acc[:])
+
+        def weighted(nt, r, product, t0, t1):
+            nc.vector.tensor_tensor(
+                out=product[:, t0:t1],
+                in0=y[nt][:].indirect(token_slot[r][:, t0 // 16 : t1 // 16]),
+                in1=gates[:, r, t0:t1],
+                op=MULT,
+            )
+
+        for nt in range(N_TILES - 1):
+            slot_results(nt + 1)
+            products = [ring.tile([P, T], F32, name="product%d" % r) for r in range(TOP)]
+            for r in range(TOP):
+                weighted(nt, r, products[r], 0, T)
+            turned = bank(PACK + nt % 2)
+            for tb in range(T // P):
+                cols = slice(tb * P, (tb + 1) * P)
+                for r in range(TOP):
+                    nc.tensor.matmul(
+                        out=turned[:, cols], lhsT=products[r][:, cols], rhs=ident[:],
+                        start=(r == 0), stop=(r == TOP - 1), is_transpose=True,
+                    )
+            summed = ring.tile([P, T], F32)
+            nc.scalar.copy(out=summed[:], in_=turned[:])
+            back = bank(PACK + 2 + nt % 2)
+            for tb in range(T // P):
+                cols = slice(tb * P, (tb + 1) * P)
+                nc.tensor.transpose(back[:, cols], summed[:, cols], ident[:])
+            result = ring.tile([P, T], F32)
+            nc.scalar.copy(out=result[:], in_=back[:])
+            nc.sync.dma_start(out=out[nt * P : (nt + 1) * P, :], in_=result[:])
+
+        nt = N_TILES - 1
+        products = [ring.tile([P, T], F32, name="product%d" % r) for r in range(TOP)]
+        summed = ring.tile([P, T], F32)
+        weighted(nt, 0, products[0], 0, T)
+        weighted(nt, 1, products[1], 0, T)
+        weighted(nt, 2, products[2], 0, T // 2)
+        nc.vector.tensor_tensor(out=summed[:], in0=products[0][:], in1=products[1][:], op=ADD)
+        weighted(nt, 2, products[2], T // 2, T)
+        result = ring.tile([P, T], F32)
+        for t0 in (0, T // 2):
+            cols = slice(t0, t0 + T // 2)
+            nc.vector.tensor_tensor(out=result[:, cols], in0=summed[:, cols], in1=products[2][:, cols], op=ADD)
+            nc.sync.dma_start(out=out[nt * P : (nt + 1) * P, cols], in_=result[:, cols])

@@ -25,8 +25,7 @@ K_PASS = P * PACK
 PASSES = K // K_PASS
 N_TILES = N // P
 BANK = 512
-HALF = H // 2
-LAST_SPLIT = 104
+SPLIT = 84
 
 
 def tile_moe_sup_glu_sigmoid_kernel(
@@ -58,10 +57,9 @@ def tile_moe_sup_glu_sigmoid_kernel(
         raw = {}
 
         def load_w(name, w, s):
+            raw[name, s] = keep.tile([P, PACK, H], F32, name="raw_%s%d" % (name, s))
             rows = w[s * K_PASS : (s + 1) * K_PASS, :].rearrange("(p j) c -> p j c", j=PACK)
-            for half in range(2):
-                raw[name, s, half] = keep.tile([P, PACK, HALF], F32, name="raw_%s%d%d" % (name, s, half))
-                nc.sync.dma_start(out=raw[name, s, half][:], in_=rows[:, :, half * HALF : (half + 1) * HALF])
+            nc.sync.dma_start(out=raw[name, s][:], in_=rows)
 
         def load_x(s):
             nc.sync.dma_start(
@@ -77,9 +75,9 @@ def tile_moe_sup_glu_sigmoid_kernel(
                 )
 
         load_w("w1", w1, 0)
+        load_w("w1", w1, 1)
         load_plane(x_plane, x_scales)
         load_x(0)
-        load_w("w1", w1, 1)
         load_x(1)
         load_w("w3", w3, 0)
         load_w("w3", w3, 1)
@@ -93,30 +91,24 @@ def tile_moe_sup_glu_sigmoid_kernel(
             nc.sync.dma_start(token_slot[r][:], pos)
         nc.sync.dma_start(out=gates[:], in_=gate.rearrange("r p t -> p r t"))
 
-        def regroup(copy, grouped, name, s, m0, m1):
-            half = m0 // (HALF // PACK)
-            base = half * (HALF // PACK)
-            copy(
-                out=grouped[:, :, m0:m1, :].rearrange("p t m j -> p m j t"),
-                in_=raw[name, s, half][:].rearrange("p j (m t) -> p m j t", t=PACK)[:, m0 - base : m1 - base],
-            )
+        on_vector, on_scalar = nc.vector.tensor_copy, nc.scalar.copy
 
-        def first_layer(name, banks, shares, pieces):
-            for s in range(PASSES):
-                grouped = keep.tile([P, PACK, P, PACK], BF16, name="grouped_%s%d" % (name, s), align_bytes=64)
-                codes = keep.tile([P, H], U32, name="codes_%s%d" % (name, s), align_bytes=64)
-                plane = keep.tile([P, H], U8, name="plane_%s%d" % (name, s), align_bytes=64)
-                for copy, m0, m1 in shares[s]:
-                    regroup(copy, grouped, name, s, m0, m1)
-                width = H // pieces[s]
-                flat = grouped[:].rearrange("p t m j -> p (t m j)")
-                for c in range(0, H, width):
-                    nc.vector.quantize_mx(
-                        out=codes[:, c : c + width].bitcast(FP8X4),
-                        scales=plane[:, c : c + width],
-                        in_=flat[:, PACK * c : PACK * (c + width)],
-                    )
-                for t in range(PACK):
+        def first_layer_pass(name, s, banks, steps):
+            grouped = keep.tile([P, PACK, P, PACK], BF16, name="grouped_%s%d" % (name, s), align_bytes=64)
+            codes = keep.tile([P, H], U32, name="codes_%s%d" % (name, s), align_bytes=64)
+            plane = keep.tile([P, H], U8, name="plane_%s%d" % (name, s), align_bytes=64)
+            source = raw[name, s][:].rearrange("p j (m t) -> p m j t", t=PACK)
+            target = grouped[:].rearrange("p t m j -> p m j t")
+            flat = grouped[:].rearrange("p t m j -> p (t m j)")
+            for t0, t1, shares in steps:
+                for copy, m0, m1 in shares:
+                    copy(out=target[:, m0:m1, :, t0:t1], in_=source[:, m0:m1, :, t0:t1])
+                nc.vector.quantize_mx(
+                    out=codes[:, t0 * P : t1 * P].bitcast(FP8X4),
+                    scales=plane[:, t0 * P : t1 * P],
+                    in_=flat[:, PACK * t0 * P : PACK * t1 * P],
+                )
+                for t in range(t0, t1):
                     nc.tensor.matmul_mx(
                         out=banks[t][:],
                         lhsT=codes[:, t * P : (t + 1) * P].bitcast(FP8X4),
@@ -127,29 +119,32 @@ def tile_moe_sup_glu_sigmoid_kernel(
                         stop=(s == PASSES - 1),
                     )
 
-        on_vector, on_scalar = nc.vector.tensor_copy, nc.scalar.copy
-        mid = P // 2
         a_banks = [bank(t) for t in range(PACK)]
-        both = [(on_vector, 0, mid), (on_scalar, mid, P)]
-        first_layer("w1", a_banks, [both, both], [1, 1])
+        for s in range(PASSES):
+            first_layer_pass("w1", s, a_banks, [(0, PACK, [(on_vector, 0, SPLIT), (on_scalar, SPLIT, P)])])
         sig = keep.tile([P, PACK, T], F32)
         for t in range(PACK):
             nc.scalar.activation(out=sig[:, t, :], in_=a_banks[t][:], func=SIGMOID)
         b_banks = [bank(PACK + t) for t in range(PACK)]
-        first_layer(
+        first_layer_pass("w3", 0, b_banks, [(0, PACK, [(on_vector, 0, P)])])
+        first_layer_pass(
             "w3",
+            1,
             b_banks,
             [
-                [(on_vector, 0, mid), (on_vector, mid, P)],
-                [(on_vector, 0, mid), (on_vector, mid, LAST_SPLIT), (on_scalar, LAST_SPLIT, P)],
+                (0, 2, [(on_vector, 0, SPLIT), (on_scalar, SPLIT, P)]),
+                (2, PACK, [(on_vector, 0, P // 2), (on_scalar, P // 2, P)]),
             ],
-            [1, 2],
         )
 
-        h_pairs = [keep.tile([P, T, 2], BF16, name="h_pairs%d" % u) for u in range(2)]
-        for t in range(PACK):
-            nc.vector.tensor_tensor(out=h_pairs[t // 2][:, :, t % 2], in0=b_banks[t][:], in1=sig[:, t, :], op=MULT)
-        h_window = [h_pairs[u][:].rearrange("p t e -> p (t e)").bitcast(U32) for u in range(2)]
+        h = keep.tile([P, PACK, T], BF16)
+        h_window = []
+        for u in range(2):
+            for t in (2 * u, 2 * u + 1):
+                nc.vector.tensor_tensor(out=h[:, t, :], in0=b_banks[t][:], in1=sig[:, t, :], op=MULT)
+            h_pairs = keep.tile([P, T, 2], BF16, name="h_pairs%d" % u)
+            nc.scalar.copy(out=h_pairs[:], in_=h[:, 2 * u : 2 * u + 2, :].rearrange("p e t -> p t e"))
+            h_window.append(h_pairs[:].rearrange("p t e -> p (t e)").bitcast(U32))
 
         h_codes = keep.tile([P, S], U32, align_bytes=64)
         h_plane = keep.tile([P, S], U8, align_bytes=64)
@@ -162,8 +157,11 @@ def tile_moe_sup_glu_sigmoid_kernel(
                     out=picked[:, u, :].bitcast(U32),
                     in_=h_window[u].indirect(slot_token[:, e * C // 16 : (e + 1) * C // 16]),
                 )
+            return picked
+
+        def join_pairs(e, picked, copy):
             h_slots = keep.tile([P, C, 2, 2], BF16, name="h_slots%d" % e, align_bytes=64)
-            nc.scalar.copy(out=h_slots[:], in_=picked[:].rearrange("p u (c e) -> p c u e", e=2))
+            copy(out=h_slots[:], in_=picked[:].rearrange("p u (c e) -> p c u e", e=2))
             return h_slots
 
         def expert_product(e, nt, acc):
@@ -193,12 +191,16 @@ def tile_moe_sup_glu_sigmoid_kernel(
             expert_product(e, 0, acc)
             nc.scalar.copy(out=y[0][:, slots], in_=acc[:, (e % 2) * C : (e % 2 + 1) * C])
 
-        waiting = gather_h(0)
-        for e in range(1, E):
-            h_slots = gather_h(e)
-            finish_expert(e - 1, waiting)
-            waiting = h_slots
-        finish_expert(E - 1, waiting)
+        joined = {}
+        for e in range(E - 1):
+            joined[e] = join_pairs(e, gather_h(e), on_scalar)
+            if e >= 2:
+                finish_expert(e - 2, joined[e - 2])
+        picked = gather_h(E - 1)
+        finish_expert(E - 3, joined[E - 3])
+        joined[E - 1] = join_pairs(E - 1, picked, on_vector)
+        finish_expert(E - 2, joined[E - 2])
+        finish_expert(E - 1, joined[E - 1])
 
         def slot_results(nt):
             for g in range(E // 2):

@@ -67,22 +67,22 @@ def tile_moe_sup_glu_sigmoid_kernel(
                 in_=x_words[s].rearrange("p t d -> p (t d)").bitcast(I32),
             )
 
-        def load_plane(plane, rows):
+        def load_plane(queue, plane, rows):
             for r in range(4):
-                nc.sync.dma_start(
+                queue.dma_start(
                     out=plane[r:P:32, :, :].bitcast(I32),
                     in_=rows[:, r:16:4, :].rearrange("g q w -> q g w").bitcast(I32),
                 )
 
         load_w("w1", w1, 0)
         load_w("w1", w1, 1)
-        load_plane(x_plane, x_scales)
+        load_plane(nc.scalar, x_plane, x_scales)
         load_x(0)
         load_x(1)
         load_w("w3", w3, 0)
         load_w("w3", w3, 1)
         nc.sync.dma_start(slot_token[:], offs)
-        load_plane(w2_plane, w2_scales.rearrange("e s b n -> (e s) b n"))
+        load_plane(nc.sync, w2_plane, w2_scales.rearrange("e s b n -> (e s) b n"))
         nc.sync.dma_start(
             out=w2_codes[:].bitcast(I32),
             in_=w2_words.rearrange("e s p b -> p (e s) b").bitcast(I32),
@@ -93,49 +93,56 @@ def tile_moe_sup_glu_sigmoid_kernel(
 
         on_vector, on_scalar = nc.vector.tensor_copy, nc.scalar.copy
 
-        def first_layer_pass(name, s, banks, steps):
+        def quantised(name, s):
             grouped = keep.tile([P, PACK, P, PACK], BF16, name="grouped_%s%d" % (name, s), align_bytes=64)
             codes = keep.tile([P, H], U32, name="codes_%s%d" % (name, s), align_bytes=64)
             plane = keep.tile([P, H], U8, name="plane_%s%d" % (name, s), align_bytes=64)
-            source = raw[name, s][:].rearrange("p j (m t) -> p m j t", t=PACK)
-            target = grouped[:].rearrange("p t m j -> p m j t")
-            flat = grouped[:].rearrange("p t m j -> p (t m j)")
-            for t0, t1, shares in steps:
-                for copy, m0, m1 in shares:
-                    copy(out=target[:, m0:m1, :, t0:t1], in_=source[:, m0:m1, :, t0:t1])
-                nc.vector.quantize_mx(
-                    out=codes[:, t0 * P : t1 * P].bitcast(FP8X4),
-                    scales=plane[:, t0 * P : t1 * P],
-                    in_=flat[:, PACK * t0 * P : PACK * t1 * P],
-                )
-                for t in range(t0, t1):
-                    nc.tensor.matmul_mx(
-                        out=banks[t][:],
-                        lhsT=codes[:, t * P : (t + 1) * P].bitcast(FP8X4),
-                        lhsT_scale=plane[:, t * P : (t + 1) * P],
-                        rhs=x_codes[:, s, :].bitcast(FP8X4),
-                        rhs_scale=x_plane[:, s, :],
-                        start=(s == 0),
-                        stop=(s == PASSES - 1),
-                    )
+            return raw[name, s], grouped, codes, plane
 
-        a_banks = [bank(t) for t in range(PACK)]
+        def quantise(tiles, t0, t1, split):
+            loaded, grouped, codes, plane = tiles
+            source = loaded[:].rearrange("p j (m t) -> p m j t", t=PACK)
+            target = grouped[:].rearrange("p t m j -> p m j t")
+            on_vector(out=target[:, 0:split, :, t0:t1], in_=source[:, 0:split, :, t0:t1])
+            if split < P:
+                on_scalar(out=target[:, split:P, :, t0:t1], in_=source[:, split:P, :, t0:t1])
+            nc.vector.quantize_mx(
+                out=codes[:, t0 * P : t1 * P].bitcast(FP8X4),
+                scales=plane[:, t0 * P : t1 * P],
+                in_=grouped[:].rearrange("p t m j -> p (t m j)")[:, PACK * t0 * P : PACK * t1 * P],
+            )
+
+        def first_product(acc, tiles, s, t):
+            codes, plane = tiles[2], tiles[3]
+            nc.tensor.matmul_mx(
+                out=acc[:],
+                lhsT=codes[:, t * P : (t + 1) * P].bitcast(FP8X4),
+                lhsT_scale=plane[:, t * P : (t + 1) * P],
+                rhs=x_codes[:, s, :].bitcast(FP8X4),
+                rhs_scale=x_plane[:, s, :],
+                start=(s == 0),
+                stop=(s == PASSES - 1),
+            )
+
+        w1q = [quantised("w1", s) for s in range(PASSES)]
         for s in range(PASSES):
-            first_layer_pass("w1", s, a_banks, [(0, PACK, [(on_vector, 0, SPLIT), (on_scalar, SPLIT, P)])])
+            quantise(w1q[s], 0, PACK, SPLIT)
         sig = keep.tile([P, PACK, T], F32)
         for t in range(PACK):
-            nc.scalar.activation(out=sig[:, t, :], in_=a_banks[t][:], func=SIGMOID)
+            acc = bank(t)
+            for s in range(PASSES):
+                first_product(acc, w1q[s], s, t)
+            nc.scalar.activation(out=sig[:, t, :], in_=acc[:], func=SIGMOID)
+
+        w3q = [quantised("w3", s) for s in range(PASSES)]
         b_banks = [bank(PACK + t) for t in range(PACK)]
-        first_layer_pass("w3", 0, b_banks, [(0, PACK, [(on_vector, 0, P)])])
-        first_layer_pass(
-            "w3",
-            1,
-            b_banks,
-            [
-                (0, 2, [(on_vector, 0, SPLIT), (on_scalar, SPLIT, P)]),
-                (2, PACK, [(on_vector, 0, P // 2), (on_scalar, P // 2, P)]),
-            ],
-        )
+        quantise(w3q[0], 0, PACK, P)
+        for t in range(PACK):
+            first_product(b_banks[t], w3q[0], 0, t)
+        for t0, split in ((0, SPLIT), (2, P // 2)):
+            quantise(w3q[1], t0, t0 + 2, split)
+            for t in (t0, t0 + 1):
+                first_product(b_banks[t], w3q[1], 1, t)
 
         h = keep.tile([P, PACK, T], BF16)
         h_window = []
@@ -164,10 +171,9 @@ def tile_moe_sup_glu_sigmoid_kernel(
             copy(out=h_slots[:], in_=picked[:].rearrange("p u (c e) -> p c u e", e=2))
             return h_slots
 
-        def expert_product(e, nt, acc):
-            slots = slice(e * C, (e + 1) * C)
+        def expert_product(e, nt, acc, slots):
             nc.tensor.matmul_mx(
-                out=acc[:, (e % 2) * C : (e % 2 + 1) * C],
+                out=acc,
                 lhsT=w2_codes[:, e, 2 * nt * P : 2 * (nt + 1) * P].bitcast(FP4X4),
                 lhsT_scale=w2_plane[:, e, nt * P : (nt + 1) * P],
                 rhs=h_codes[:, slots].bitcast(FP8X4),
@@ -176,37 +182,34 @@ def tile_moe_sup_glu_sigmoid_kernel(
                 stop=True,
             )
 
-        accs = {}
-
-        def finish_expert(e, h_slots):
-            slots = slice(e * C, (e + 1) * C)
+        def finish_slots(e, h_slots, c0, c1, b, copy):
+            slots = slice(e * C + c0, e * C + c1)
             nc.vector.quantize_mx(
                 out=h_codes[:, slots].bitcast(FP8X4),
                 scales=h_plane[:, slots],
-                in_=h_slots[:].rearrange("p c u e -> p (c u e)"),
+                in_=h_slots[:, c0:c1].rearrange("p c u e -> p (c u e)"),
             )
-            if e % 2 == 0:
-                accs[e // 2] = bank(e // 2)
-            acc = accs[e // 2]
-            expert_product(e, 0, acc)
-            nc.scalar.copy(out=y[0][:, slots], in_=acc[:, (e % 2) * C : (e % 2 + 1) * C])
+            acc = bank(b)
+            expert_product(e, 0, acc[:, 0 : c1 - c0], slots)
+            copy(out=y[0][:, slots], in_=acc[:, 0 : c1 - c0])
 
         joined = {}
         for e in range(E - 1):
             joined[e] = join_pairs(e, gather_h(e), on_scalar)
             if e >= 2:
-                finish_expert(e - 2, joined[e - 2])
+                finish_slots(e - 2, joined[e - 2], 0, C, e - 2, on_scalar)
         picked = gather_h(E - 1)
-        finish_expert(E - 3, joined[E - 3])
+        finish_slots(E - 3, joined[E - 3], 0, C, E - 3, on_scalar)
         joined[E - 1] = join_pairs(E - 1, picked, on_vector)
-        finish_expert(E - 2, joined[E - 2])
-        finish_expert(E - 1, joined[E - 1])
+        finish_slots(E - 2, joined[E - 2], 0, C, E - 2, on_scalar)
+        finish_slots(E - 1, joined[E - 1], 0, C // 2, E - 1, on_vector)
+        finish_slots(E - 1, joined[E - 1], C // 2, C, E, on_vector)
 
         def slot_results(nt):
             for g in range(E // 2):
-                acc = bank((nt * (E // 2) + g) % PACK)
-                expert_product(2 * g, nt, acc)
-                expert_product(2 * g + 1, nt, acc)
+                acc = bank(E - g)
+                for e in (2 * g, 2 * g + 1):
+                    expert_product(e, nt, acc[:, (e % 2) * C : (e % 2 + 1) * C], slice(e * C, (e + 1) * C))
                 nc.scalar.copy(out=y[nt][:, g * BANK : (g + 1) * BANK], in_=acc[:])
 
         def weighted(nt, r, product, t0, t1):
@@ -217,39 +220,42 @@ def tile_moe_sup_glu_sigmoid_kernel(
                 op=MULT,
             )
 
-        for nt in range(N_TILES - 1):
-            slot_results(nt + 1)
-            products = [ring.tile([P, T], F32, name="product%d" % r) for r in range(TOP)]
-            for r in range(TOP):
-                weighted(nt, r, products[r], 0, T)
-            turned = bank(PACK + nt % 2)
-            for tb in range(T // P):
-                cols = slice(tb * P, (tb + 1) * P)
+        def sum_on_tensor(nt, products, t0, t1):
+            turned = bank(0)
+            for c in range(t0, t1, P):
                 for r in range(TOP):
                     nc.tensor.matmul(
-                        out=turned[:, cols], lhsT=products[r][:, cols], rhs=ident[:],
+                        out=turned[:, c : c + P], lhsT=products[r][:, c : c + P], rhs=ident[:],
                         start=(r == 0), stop=(r == TOP - 1), is_transpose=True,
                     )
             summed = ring.tile([P, T], F32)
-            nc.scalar.copy(out=summed[:], in_=turned[:])
-            back = bank(PACK + 2 + nt % 2)
-            for tb in range(T // P):
-                cols = slice(tb * P, (tb + 1) * P)
-                nc.tensor.transpose(back[:, cols], summed[:, cols], ident[:])
-            result = ring.tile([P, T], F32)
-            nc.scalar.copy(out=result[:], in_=back[:])
-            nc.sync.dma_start(out=out[nt * P : (nt + 1) * P, :], in_=result[:])
+            nc.scalar.copy(out=summed[:, t0:t1], in_=turned[:, t0:t1])
+            back = bank(1 + nt % 2)
+            for c in range(t0, t1, P):
+                nc.tensor.transpose(back[:, c : c + P], summed[:, c : c + P], ident[:])
+            result = keep.tile([P, T], F32, name="result%d" % nt)
+            nc.scalar.copy(out=result[:, t0:t1], in_=back[:, t0:t1])
+            nc.scalar.dma_start(out=out[nt * P : (nt + 1) * P, t0:t1], in_=result[:, t0:t1])
+
+        for nt in range(1, N_TILES):
+            slot_results(nt)
+
+        for nt in range(N_TILES - 1):
+            products = [ring.tile([P, T], F32, name="product%d" % r) for r in range(TOP)]
+            for r in range(TOP):
+                weighted(nt, r, products[r], 0, T)
+            sum_on_tensor(nt, products, 0, T)
 
         nt = N_TILES - 1
         products = [ring.tile([P, T], F32, name="product%d" % r) for r in range(TOP)]
-        summed = ring.tile([P, T], F32)
+        partial = keep.tile([P, T], F32)
+        last = keep.tile([P, T], F32)
         weighted(nt, 0, products[0], 0, T)
         weighted(nt, 1, products[1], 0, T)
         weighted(nt, 2, products[2], 0, T // 2)
-        nc.vector.tensor_tensor(out=summed[:], in0=products[0][:], in1=products[1][:], op=ADD)
+        nc.vector.tensor_tensor(out=partial[:], in0=products[0][:], in1=products[1][:], op=ADD)
         weighted(nt, 2, products[2], T // 2, T)
-        result = ring.tile([P, T], F32)
         for t0 in (0, T // 2):
             cols = slice(t0, t0 + T // 2)
-            nc.vector.tensor_tensor(out=result[:, cols], in0=summed[:, cols], in1=products[2][:, cols], op=ADD)
-            nc.sync.dma_start(out=out[nt * P : (nt + 1) * P, cols], in_=result[:, cols])
+            nc.vector.tensor_tensor(out=last[:, cols], in0=partial[:, cols], in1=products[2][:, cols], op=ADD)
+            nc.sync.dma_start(out=out[nt * P : (nt + 1) * P, cols], in_=last[:, cols])

@@ -67,22 +67,22 @@ def tile_moe_sup_glu_sigmoid_kernel(
                 in_=x_words[s].rearrange("p t d -> p (t d)").bitcast(I32),
             )
 
-        def load_plane(queue, plane, rows):
+        def load_plane(plane, rows):
             for r in range(4):
-                queue.dma_start(
+                nc.sync.dma_start(
                     out=plane[r:P:32, :, :].bitcast(I32),
                     in_=rows[:, r:16:4, :].rearrange("g q w -> q g w").bitcast(I32),
                 )
 
         load_w("w1", w1, 0)
-        load_w("w1", w1, 1)
-        load_plane(nc.scalar, x_plane, x_scales)
+        load_plane(x_plane, x_scales)
         load_x(0)
+        load_w("w1", w1, 1)
         load_x(1)
         load_w("w3", w3, 0)
         load_w("w3", w3, 1)
         nc.sync.dma_start(slot_token[:], offs)
-        load_plane(nc.sync, w2_plane, w2_scales.rearrange("e s b n -> (e s) b n"))
+        load_plane(w2_plane, w2_scales.rearrange("e s b n -> (e s) b n"))
         nc.sync.dma_start(
             out=w2_codes[:].bitcast(I32),
             in_=w2_words.rearrange("e s p b -> p (e s) b").bitcast(I32),
@@ -101,11 +101,11 @@ def tile_moe_sup_glu_sigmoid_kernel(
 
         def quantise(tiles, t0, t1, split):
             loaded, grouped, codes, plane = tiles
-            source = loaded[:].rearrange("p j (m t) -> p m j t", t=PACK)
-            target = grouped[:].rearrange("p t m j -> p m j t")
-            on_vector(out=target[:, 0:split, :, t0:t1], in_=source[:, 0:split, :, t0:t1])
+            source = loaded[:].rearrange("p j (m t) -> p m t j", t=PACK)
+            target = grouped[:].rearrange("p t m j -> p m t j")
+            on_vector(out=target[:, 0:split, t0:t1, :], in_=source[:, 0:split, t0:t1, :])
             if split < P:
-                on_scalar(out=target[:, split:P, :, t0:t1], in_=source[:, split:P, :, t0:t1])
+                on_scalar(out=target[:, split:P, t0:t1, :], in_=source[:, split:P, t0:t1, :])
             nc.vector.quantize_mx(
                 out=codes[:, t0 * P : t1 * P].bitcast(FP8X4),
                 scales=plane[:, t0 * P : t1 * P],
@@ -125,14 +125,14 @@ def tile_moe_sup_glu_sigmoid_kernel(
             )
 
         w1q = [quantised("w1", s) for s in range(PASSES)]
+        a_banks = [bank(t) for t in range(PACK)]
         for s in range(PASSES):
-            quantise(w1q[s], 0, PACK, SPLIT)
+            quantise(w1q[s], 0, PACK, P)
+            for t in range(PACK):
+                first_product(a_banks[t], w1q[s], s, t)
         sig = keep.tile([P, PACK, T], F32)
         for t in range(PACK):
-            acc = bank(t)
-            for s in range(PASSES):
-                first_product(acc, w1q[s], s, t)
-            nc.scalar.activation(out=sig[:, t, :], in_=acc[:], func=SIGMOID)
+            nc.scalar.activation(out=sig[:, t, :], in_=a_banks[t][:], func=SIGMOID)
 
         w3q = [quantised("w3", s) for s in range(PASSES)]
         b_banks = [bank(PACK + t) for t in range(PACK)]
@@ -166,9 +166,11 @@ def tile_moe_sup_glu_sigmoid_kernel(
                 )
             return picked
 
-        def join_pairs(e, picked, copy):
-            h_slots = keep.tile([P, C, 2, 2], BF16, name="h_slots%d" % e, align_bytes=64)
-            copy(out=h_slots[:], in_=picked[:].rearrange("p u (c e) -> p c u e", e=2))
+        def join_pairs(e, picked, copy, width):
+            h_slots = keep.tile([P, C, 2, 2], BF16, name="h_slots%d" % min(e, E - 2), align_bytes=64)
+            pairs = picked[:].rearrange("p u (c e) -> p c u e", e=2)
+            for c in range(0, C, width):
+                copy(out=h_slots[:, c : c + width], in_=pairs[:, c : c + width])
             return h_slots
 
         def expert_product(e, nt, acc, slots):
@@ -195,13 +197,13 @@ def tile_moe_sup_glu_sigmoid_kernel(
 
         joined = {}
         for e in range(E - 1):
-            joined[e] = join_pairs(e, gather_h(e), on_scalar)
+            joined[e] = join_pairs(e, gather_h(e), on_scalar, C)
             if e >= 2:
                 finish_slots(e - 2, joined[e - 2], 0, C, e - 2, on_scalar)
         picked = gather_h(E - 1)
         finish_slots(E - 3, joined[E - 3], 0, C, E - 3, on_scalar)
-        joined[E - 1] = join_pairs(E - 1, picked, on_vector)
         finish_slots(E - 2, joined[E - 2], 0, C, E - 2, on_scalar)
+        joined[E - 1] = join_pairs(E - 1, picked, on_vector, C // 2)
         finish_slots(E - 1, joined[E - 1], 0, C // 2, E - 1, on_vector)
         finish_slots(E - 1, joined[E - 1], C // 2, C, E, on_vector)
 
@@ -241,13 +243,13 @@ def tile_moe_sup_glu_sigmoid_kernel(
             slot_results(nt)
 
         for nt in range(N_TILES - 1):
-            products = [ring.tile([P, T], F32, name="product%d" % r) for r in range(TOP)]
+            products = [keep.tile([P, T], F32, name="product%d_%d" % (nt, r)) for r in range(TOP)]
             for r in range(TOP):
                 weighted(nt, r, products[r], 0, T)
             sum_on_tensor(nt, products, 0, T)
 
         nt = N_TILES - 1
-        products = [ring.tile([P, T], F32, name="product%d" % r) for r in range(TOP)]
+        products = [keep.tile([P, T], F32, name="product%d_%d" % (nt, r)) for r in range(TOP)]
         partial = keep.tile([P, T], F32)
         last = keep.tile([P, T], F32)
         weighted(nt, 0, products[0], 0, T)

@@ -18,6 +18,7 @@ FP4X4 = mybir.dt.float4_e2m1fn_x4
 MULT = mybir.AluOpType.mult
 ADD = mybir.AluOpType.add
 SIGMOID = mybir.ActivationFunctionType.Sigmoid
+COPY = mybir.ActivationFunctionType.Copy
 
 P = 128
 PACK = 4
@@ -35,7 +36,7 @@ def tile_moe_sup_glu_sigmoid_kernel(
     with ExitStack() as ctx:
         keep = ctx.enter_context(tc.tile_pool(name="keep", bufs=1))
         ring = ctx.enter_context(tc.tile_pool(name="ring", bufs=2))
-        picks = ctx.enter_context(tc.tile_pool(name="picks", bufs=3))
+        picks = ctx.enter_context(tc.tile_pool(name="picks", bufs=4))
         psum = ctx.enter_context(tc.psum_pool(name="psum", bufs=1))
 
         def bank(b):
@@ -145,13 +146,12 @@ def tile_moe_sup_glu_sigmoid_kernel(
                 first_product(b_banks[t], w3q[1], 1, t)
 
         h = keep.tile([P, PACK, T], BF16)
-        h_window = []
-        for u in range(2):
-            for t in (2 * u, 2 * u + 1):
-                nc.vector.tensor_tensor(out=h[:, t, :], in0=b_banks[t][:], in1=sig[:, t, :], op=MULT)
-            h_pairs = keep.tile([P, T, 2], BF16, name="h_pairs%d" % u)
-            nc.scalar.copy(out=h_pairs[:], in_=h[:, 2 * u : 2 * u + 2, :].rearrange("p e t -> p t e"))
-            h_window.append(h_pairs[:].rearrange("p t e -> p (t e)").bitcast(U32))
+        h_pairs = keep.tile([P, T, 2], BF16)
+        for t in range(PACK):
+            nc.vector.tensor_tensor(out=h[:, t, :], in0=b_banks[t][:], in1=sig[:, t, :], op=MULT)
+            if t == 1:
+                nc.scalar.copy(out=h_pairs[:], in_=h[:, 0:2, :].rearrange("p e t -> p t e"))
+        h_words = h_pairs[:].rearrange("p t e -> p (t e)").bitcast(U32)
 
         h_codes = keep.tile([P, S], U32, align_bytes=64)
         h_plane = keep.tile([P, S], U8, align_bytes=64)
@@ -159,18 +159,17 @@ def tile_moe_sup_glu_sigmoid_kernel(
 
         def gather_h(e):
             picked = picks.tile([P, 2, 2 * C], BF16)
-            for u in range(2):
-                nc.vector.tensor_copy(
-                    out=picked[:, u, :].bitcast(U32),
-                    in_=h_window[u].indirect(slot_token[:, e * C // 16 : (e + 1) * C // 16]),
-                )
+            tokens = slot_token[:, e * C // 16 : (e + 1) * C // 16]
+            nc.vector.tensor_copy(out=picked[:, 0, :].bitcast(U32), in_=h_words.indirect(tokens))
+            for d in range(2):
+                nc.scalar.activation(out=picked[:, 1, d : 2 * C : 2], in_=h[:, 2 + d, :].indirect(tokens), func=COPY)
             return picked
 
-        def join_pairs(e, picked, copy, width):
+        def join_pairs(e, picked, width):
             h_slots = keep.tile([P, C, 2, 2], BF16, name="h_slots%d" % min(e, E - 2), align_bytes=64)
             pairs = picked[:].rearrange("p u (c e) -> p c u e", e=2)
             for c in range(0, C, width):
-                copy(out=h_slots[:, c : c + width], in_=pairs[:, c : c + width])
+                nc.vector.tensor_copy(out=h_slots[:, c : c + width], in_=pairs[:, c : c + width])
             return h_slots
 
         def expert_product(e, nt, acc, slots):
@@ -184,28 +183,31 @@ def tile_moe_sup_glu_sigmoid_kernel(
                 stop=True,
             )
 
-        def finish_slots(e, h_slots, c0, c1, b, copy):
+        def first_tile(e, h_slots, c0, c1, acc):
             slots = slice(e * C + c0, e * C + c1)
             nc.vector.quantize_mx(
                 out=h_codes[:, slots].bitcast(FP8X4),
                 scales=h_plane[:, slots],
                 in_=h_slots[:, c0:c1].rearrange("p c u e -> p (c u e)"),
             )
-            acc = bank(b)
-            expert_product(e, 0, acc[:, 0 : c1 - c0], slots)
-            copy(out=y[0][:, slots], in_=acc[:, 0 : c1 - c0])
+            expert_product(e, 0, acc, slots)
 
-        joined = {}
+        pair_banks = [bank(0), bank(1), bank(4)]
+        picked = [gather_h(0), gather_h(1)]
         for e in range(E - 1):
-            joined[e] = join_pairs(e, gather_h(e), on_scalar, C)
-            if e >= 2:
-                finish_slots(e - 2, joined[e - 2], 0, C, e - 2, on_scalar)
-        picked = gather_h(E - 1)
-        finish_slots(E - 3, joined[E - 3], 0, C, E - 3, on_scalar)
-        finish_slots(E - 2, joined[E - 2], 0, C, E - 2, on_scalar)
-        joined[E - 1] = join_pairs(E - 1, picked, on_vector, C // 2)
-        finish_slots(E - 1, joined[E - 1], 0, C // 2, E - 1, on_vector)
-        finish_slots(E - 1, joined[E - 1], C // 2, C, E, on_vector)
+            h_slots = join_pairs(e, picked[e], C)
+            if e + 2 < E:
+                picked.append(gather_h(e + 2))
+            first_tile(e, h_slots, 0, C, pair_banks[e // 2][:, (e % 2) * C : (e % 2 + 1) * C])
+        nc.scalar.copy(out=y[0][:, 0:BANK], in_=pair_banks[0][:])
+        nc.scalar.copy(out=y[0][:, BANK : 2 * BANK], in_=pair_banks[1][:])
+        nc.scalar.copy(out=y[0][:, 2 * BANK : 2 * BANK + C], in_=pair_banks[2][:, 0:C])
+        h_slots = join_pairs(E - 1, picked[E - 1], C // 2)
+        for half in range(2):
+            acc = bank(5 + half)
+            c0 = half * C // 2
+            first_tile(E - 1, h_slots, c0, c0 + C // 2, acc[:, 0 : C // 2])
+            nc.vector.tensor_copy(out=y[0][:, (E - 1) * C + c0 : (E - 1) * C + c0 + C // 2], in_=acc[:, 0 : C // 2])
 
         def slot_results(nt):
             for g in range(E // 2):

@@ -36,7 +36,6 @@ def tile_moe_sup_glu_sigmoid_kernel(
     with ExitStack() as ctx:
         keep = ctx.enter_context(tc.tile_pool(name="keep", bufs=1))
         ring = ctx.enter_context(tc.tile_pool(name="ring", bufs=2))
-        picks = ctx.enter_context(tc.tile_pool(name="picks", bufs=4))
         psum = ctx.enter_context(tc.psum_pool(name="psum", bufs=1))
 
         def bank(b):
@@ -100,27 +99,30 @@ def tile_moe_sup_glu_sigmoid_kernel(
             plane = keep.tile([P, H], U8, name="plane_%s%d" % (name, s), align_bytes=64)
             return raw[name, s], grouped, codes, plane
 
-        def quantise(tiles, t0, t1, split):
-            loaded, grouped, codes, plane = tiles
+        def regroup(tiles, t0, t1, split):
+            loaded, grouped = tiles[0], tiles[1]
             source = loaded[:].rearrange("p j (m t) -> p m t j", t=PACK)
             target = grouped[:].rearrange("p t m j -> p m t j")
             on_vector(out=target[:, 0:split, t0:t1, :], in_=source[:, 0:split, t0:t1, :])
             if split < P:
                 on_scalar(out=target[:, split:P, t0:t1, :], in_=source[:, split:P, t0:t1, :])
+
+        def quantise(tiles, t0, t1):
+            grouped, codes, plane = tiles[1], tiles[2], tiles[3]
             nc.vector.quantize_mx(
                 out=codes[:, t0 * P : t1 * P].bitcast(FP8X4),
                 scales=plane[:, t0 * P : t1 * P],
                 in_=grouped[:].rearrange("p t m j -> p (t m j)")[:, PACK * t0 * P : PACK * t1 * P],
             )
 
-        def first_product(acc, tiles, s, t):
+        def first_product(acc, tiles, s, t, tokens=slice(0, T)):
             codes, plane = tiles[2], tiles[3]
             nc.tensor.matmul_mx(
-                out=acc[:],
+                out=acc,
                 lhsT=codes[:, t * P : (t + 1) * P].bitcast(FP8X4),
                 lhsT_scale=plane[:, t * P : (t + 1) * P],
-                rhs=x_codes[:, s, :].bitcast(FP8X4),
-                rhs_scale=x_plane[:, s, :],
+                rhs=x_codes[:, s, tokens].bitcast(FP8X4),
+                rhs_scale=x_plane[:, s, tokens],
                 start=(s == 0),
                 stop=(s == PASSES - 1),
             )
@@ -128,48 +130,62 @@ def tile_moe_sup_glu_sigmoid_kernel(
         w1q = [quantised("w1", s) for s in range(PASSES)]
         a_banks = [bank(t) for t in range(PACK)]
         for s in range(PASSES):
-            quantise(w1q[s], 0, PACK, P)
-            for t in range(PACK):
-                first_product(a_banks[t], w1q[s], s, t)
+            regroup(w1q[s], 0, PACK, P)
+            quantise(w1q[s], 0, PACK)
+            for t in (2, 3, 0, 1):
+                first_product(a_banks[t][:], w1q[s], s, t)
         sig = keep.tile([P, PACK, T], F32)
-        for t in range(PACK):
+        for t in (2, 3, 0, 1):
             nc.scalar.activation(out=sig[:, t, :], in_=a_banks[t][:], func=SIGMOID)
 
         w3q = [quantised("w3", s) for s in range(PASSES)]
         b_banks = [bank(PACK + t) for t in range(PACK)]
-        quantise(w3q[0], 0, PACK, P)
-        for t in range(PACK):
-            first_product(b_banks[t], w3q[0], 0, t)
-        for t0, split in ((0, SPLIT), (2, P // 2)):
-            quantise(w3q[1], t0, t0 + 2, split)
-            for t in (t0, t0 + 1):
-                first_product(b_banks[t], w3q[1], 1, t)
-
-        h = keep.tile([P, PACK, T], BF16)
+        h = keep.tile([P, 2, T], BF16)
         h_pairs = keep.tile([P, T, 2], BF16)
-        for t in range(PACK):
-            nc.vector.tensor_tensor(out=h[:, t, :], in0=b_banks[t][:], in1=sig[:, t, :], op=MULT)
-            if t == 1:
-                nc.scalar.copy(out=h_pairs[:], in_=h[:, 0:2, :].rearrange("p e t -> p t e"))
+        regroup(w3q[0], 0, PACK, P)
+        quantise(w3q[0], 0, PACK)
+        for t in (2, 3):
+            first_product(b_banks[t - 2][:], w3q[0], 0, t)
+        regroup(w3q[1], 2, 4, SPLIT)
+        quantise(w3q[1], 2, 4)
+        for t in (2, 3):
+            first_product(b_banks[t - 2][:], w3q[1], 1, t)
+        regroup(w3q[1], 0, 2, P // 2)
+        nc.vector.tensor_tensor(out=h[:, 0, :], in0=b_banks[0][:], in1=sig[:, 2, :], op=MULT)
+        quantise(w3q[1], 0, 2)
+        nc.vector.tensor_tensor(out=h[:, 1, :], in0=b_banks[1][:], in1=sig[:, 3, :], op=MULT)
+        for half in range(2):
+            tokens = slice(half * T // 2, (half + 1) * T // 2)
+            acc = b_banks[2 + half]
+            for t in range(2):
+                for s in range(PASSES):
+                    first_product(acc[:, t * T // 2 : (t + 1) * T // 2], w3q[s], s, t, tokens)
+            nc.vector.tensor_tensor(
+                out=h_pairs[:, tokens, :],
+                in0=acc[:].rearrange("p (e t) -> p t e", e=2),
+                in1=sig[:, 0:2, tokens].rearrange("p e t -> p t e"),
+                op=MULT,
+            )
         h_words = h_pairs[:].rearrange("p t e -> p (t e)").bitcast(U32)
 
         h_codes = keep.tile([P, S], U32, align_bytes=64)
         h_plane = keep.tile([P, S], U8, align_bytes=64)
         y = [keep.tile([P, S], F32, name="y%d" % nt) for nt in range(N_TILES)]
 
-        def gather_h(e):
-            picked = picks.tile([P, 2, 2 * C], BF16)
-            tokens = slot_token[:, e * C // 16 : (e + 1) * C // 16]
-            nc.vector.tensor_copy(out=picked[:, 0, :].bitcast(U32), in_=h_words.indirect(tokens))
-            for d in range(2):
-                nc.scalar.activation(out=picked[:, 1, d : 2 * C : 2], in_=h[:, 2 + d, :].indirect(tokens), func=COPY)
-            return picked
+        picked = [keep.tile([P, 2, 2 * C], BF16, name="picked%d" % e) for e in range(E)]
 
-        def join_pairs(e, picked, width):
-            h_slots = keep.tile([P, C, 2, 2], BF16, name="h_slots%d" % min(e, E - 2), align_bytes=64)
-            pairs = picked[:].rearrange("p u (c e) -> p c u e", e=2)
-            for c in range(0, C, width):
-                nc.vector.tensor_copy(out=h_slots[:, c : c + width], in_=pairs[:, c : c + width])
+        def gather_planes(e):
+            tokens = slot_token[:, e * C // 16 : (e + 1) * C // 16]
+            for d in range(2):
+                nc.scalar.activation(out=picked[e][:, 1, d : 2 * C : 2], in_=h[:, d, :].indirect(tokens), func=COPY)
+
+        def gather_pairs(e):
+            tokens = slot_token[:, e * C // 16 : (e + 1) * C // 16]
+            nc.vector.tensor_copy(out=picked[e][:, 0, :].bitcast(U32), in_=h_words.indirect(tokens))
+
+        def join_pairs(e):
+            h_slots = keep.tile([P, C, 2, 2], BF16, name="h_slots%d" % e, align_bytes=64)
+            nc.vector.tensor_copy(out=h_slots[:], in_=picked[e][:].rearrange("p u (c e) -> p c u e", e=2))
             return h_slots
 
         def expert_product(e, nt, acc, slots):
@@ -193,20 +209,24 @@ def tile_moe_sup_glu_sigmoid_kernel(
             expert_product(e, 0, acc, slots)
 
         pair_banks = [bank(0), bank(1), bank(4)]
-        picked = [gather_h(0), gather_h(1)]
+        for e in range(E):
+            gather_planes(e)
+        gather_pairs(0)
+        gather_pairs(1)
         for e in range(E - 1):
-            h_slots = join_pairs(e, picked[e], C)
+            h_slots = join_pairs(e)
             if e + 2 < E:
-                picked.append(gather_h(e + 2))
+                gather_pairs(e + 2)
+            else:
+                last_slots = join_pairs(E - 1)
             first_tile(e, h_slots, 0, C, pair_banks[e // 2][:, (e % 2) * C : (e % 2 + 1) * C])
         nc.scalar.copy(out=y[0][:, 0:BANK], in_=pair_banks[0][:])
         nc.scalar.copy(out=y[0][:, BANK : 2 * BANK], in_=pair_banks[1][:])
         nc.scalar.copy(out=y[0][:, 2 * BANK : 2 * BANK + C], in_=pair_banks[2][:, 0:C])
-        h_slots = join_pairs(E - 1, picked[E - 1], C // 2)
         for half in range(2):
             acc = bank(5 + half)
             c0 = half * C // 2
-            first_tile(E - 1, h_slots, c0, c0 + C // 2, acc[:, 0 : C // 2])
+            first_tile(E - 1, last_slots, c0, c0 + C // 2, acc[:, 0 : C // 2])
             nc.vector.tensor_copy(out=y[0][:, (E - 1) * C + c0 : (E - 1) * C + c0 + C // 2], in_=acc[:, 0 : C // 2])
 
         def slot_results(nt):
@@ -224,42 +244,46 @@ def tile_moe_sup_glu_sigmoid_kernel(
                 op=MULT,
             )
 
-        def sum_on_tensor(nt, products, t0, t1):
-            turned = bank(0)
+        def turn(turned, product, t0, t1, start, stop):
             for c in range(t0, t1, P):
-                for r in range(TOP):
-                    nc.tensor.matmul(
-                        out=turned[:, c : c + P], lhsT=products[r][:, c : c + P], rhs=ident[:],
-                        start=(r == 0), stop=(r == TOP - 1), is_transpose=True,
-                    )
+                nc.tensor.matmul(
+                    out=turned[:, c - t0 : c - t0 + P], lhsT=product[:, c : c + P], rhs=ident[:],
+                    start=(start and c == t0), stop=(stop and c == t1 - P), is_transpose=True,
+                )
+
+        def turn_back(turned, width, back):
             summed = ring.tile([P, T], F32)
-            nc.scalar.copy(out=summed[:, t0:t1], in_=turned[:, t0:t1])
-            back = bank(1 + nt % 2)
-            for c in range(t0, t1, P):
+            nc.scalar.copy(out=summed[:, 0:width], in_=turned[:, 0:width])
+            for c in range(0, width, P):
                 nc.tensor.transpose(back[:, c : c + P], summed[:, c : c + P], ident[:])
-            result = keep.tile([P, T], F32, name="result%d" % nt)
-            nc.scalar.copy(out=result[:, t0:t1], in_=back[:, t0:t1])
-            nc.scalar.dma_start(out=out[nt * P : (nt + 1) * P, t0:t1], in_=result[:, t0:t1])
+
+        def store(nt, back, t0, t1):
+            result = keep.tile([P, t1 - t0], F32, name="result%d_%d" % (nt, t0))
+            nc.scalar.copy(out=result[:], in_=back[:, 0 : t1 - t0])
+            nc.scalar.dma_start(out=out[nt * P : (nt + 1) * P, t0:t1], in_=result[:])
 
         for nt in range(1, N_TILES):
             slot_results(nt)
 
+        products = [[keep.tile([P, T], F32, name="product%d_%d" % (nt, r)) for r in range(TOP)] for nt in range(N_TILES)]
         for nt in range(N_TILES - 1):
-            products = [keep.tile([P, T], F32, name="product%d_%d" % (nt, r)) for r in range(TOP)]
+            turned = bank(6)
             for r in range(TOP):
-                weighted(nt, r, products[r], 0, T)
-            sum_on_tensor(nt, products, 0, T)
+                weighted(nt, r, products[nt][r], 0, T)
+                turn(turned, products[nt][r], 0, T, r == 0, r == TOP - 1)
+            back = bank(nt)
+            turn_back(turned, T, back)
+            store(nt, back, 0, T)
 
         nt = N_TILES - 1
-        products = [keep.tile([P, T], F32, name="product%d_%d" % (nt, r)) for r in range(TOP)]
         partial = keep.tile([P, T], F32)
         last = keep.tile([P, T], F32)
-        weighted(nt, 0, products[0], 0, T)
-        weighted(nt, 1, products[1], 0, T)
-        weighted(nt, 2, products[2], 0, T // 2)
-        nc.vector.tensor_tensor(out=partial[:], in0=products[0][:], in1=products[1][:], op=ADD)
-        weighted(nt, 2, products[2], T // 2, T)
+        weighted(nt, 0, products[nt][0], 0, T)
+        weighted(nt, 1, products[nt][1], 0, T)
+        weighted(nt, 2, products[nt][2], 0, T // 2)
+        nc.vector.tensor_tensor(out=partial[:], in0=products[nt][0][:], in1=products[nt][1][:], op=ADD)
+        weighted(nt, 2, products[nt][2], T // 2, T)
         for t0 in (0, T // 2):
             cols = slice(t0, t0 + T // 2)
-            nc.vector.tensor_tensor(out=last[:, cols], in0=partial[:, cols], in1=products[2][:, cols], op=ADD)
+            nc.vector.tensor_tensor(out=last[:, cols], in0=partial[:, cols], in1=products[nt][2][:, cols], op=ADD)
             nc.sync.dma_start(out=out[nt * P : (nt + 1) * P, cols], in_=last[:, cols])

@@ -26,13 +26,17 @@ K_PASS = P * PACK
 PASSES = K // K_PASS
 N_TILES = N // P
 BANK = 512
-SPLIT = 84
+LIST_ROWS = 16
+HALF = T // 2
+FIRST_SPLIT = 84
+SECOND_SPLIT = 48
 
 
 def tile_moe_sup_glu_sigmoid_kernel(
     tc, x_words, x_scales, w1, w3, w2_words, w2_scales, gate, offs, pos1, pos2, pos3, out
 ):
     nc = tc.nc
+    on_vector, on_scalar = nc.vector.tensor_copy, nc.scalar.copy
     with ExitStack() as ctx:
         keep = ctx.enter_context(tc.tile_pool(name="keep", bufs=1))
         ring = ctx.enter_context(tc.tile_pool(name="ring", bufs=2))
@@ -42,16 +46,16 @@ def tile_moe_sup_glu_sigmoid_kernel(
             return psum.tile([P, BANK], F32, name="bank%d" % b)
 
         x_codes = keep.tile([P, PASSES, T], U32, align_bytes=64)
-        x_plane = keep.tile([P, PASSES, T], U8, align_bytes=64)
+        x_bytes = keep.tile([P, T], U8, align_bytes=64)
         w2_codes = keep.tile([P, E, 2 * N], U8, align_bytes=64)
-        w2_plane = keep.tile([P, E, N], U8, align_bytes=64)
+        w2_bytes = keep.tile([P, E, N], U8, align_bytes=64)
         gates = keep.tile([P, TOP, T], F32)
-        slot_token = keep.tile([P, S // 16], U16)
-        token_slot = [keep.tile([P, T // 16], U16, name="token_slot%d" % r) for r in range(TOP)]
+        slot_token = keep.tile([P, S // LIST_ROWS], U16)
+        token_slot = [keep.tile([P, T // LIST_ROWS], U16, name="token_slot%d" % r) for r in range(TOP)]
         ident = keep.tile([P, P], F32)
 
-        nc.vector.memset(x_plane[:].rearrange("p s t -> p (s t)").bitcast(I32), 0)
-        nc.vector.memset(w2_plane[:].rearrange("p e n -> p (e n)").bitcast(I32), 0)
+        nc.vector.memset(x_bytes[:].bitcast(I32), 0)
+        nc.vector.memset(w2_bytes[:].rearrange("p e n -> p (e n)").bitcast(I32), 0)
         make_identity(nc, ident[:])
 
         raw = {}
@@ -67,22 +71,24 @@ def tile_moe_sup_glu_sigmoid_kernel(
                 in_=x_words[s].rearrange("p t d -> p (t d)").bitcast(I32),
             )
 
-        def load_plane(plane, rows):
-            for r in range(4):
-                nc.sync.dma_start(
-                    out=plane[r:P:32, :, :].bitcast(I32),
-                    in_=rows[:, r:16:4, :].rearrange("g q w -> q g w").bitcast(I32),
-                )
-
         load_w("w1", w1, 0)
-        load_plane(x_plane, x_scales)
+        for q in range(4):
+            nc.sync.dma_start(
+                out=x_bytes[32 * q : 32 * q + 4 * PASSES, :].bitcast(I32),
+                in_=x_scales[:, 4 * q : 4 * q + 4, :].bitcast(I32),
+            )
         load_x(0)
         load_w("w1", w1, 1)
         load_x(1)
         load_w("w3", w3, 0)
         load_w("w3", w3, 1)
         nc.sync.dma_start(slot_token[:], offs)
-        load_plane(w2_plane, w2_scales.rearrange("e s b n -> (e s) b n"))
+        w2_rows = w2_scales.rearrange("e s b n -> (e s) b n")
+        for r in range(4):
+            nc.sync.dma_start(
+                out=w2_bytes[r:P:32, :, :].bitcast(I32),
+                in_=w2_rows[:, r:16:4, :].rearrange("e q n -> q e n").bitcast(I32),
+            )
         nc.sync.dma_start(
             out=w2_codes[:].bitcast(I32),
             in_=w2_words.rearrange("e s p b -> p (e s) b").bitcast(I32),
@@ -91,199 +97,210 @@ def tile_moe_sup_glu_sigmoid_kernel(
             nc.sync.dma_start(token_slot[r][:], pos)
         nc.sync.dma_start(out=gates[:], in_=gate.rearrange("r p t -> p r t"))
 
-        on_vector, on_scalar = nc.vector.tensor_copy, nc.scalar.copy
+        codes, scales, grouped = {}, {}, {}
+        for name in ("w1", "w3"):
+            for s in range(PASSES):
+                codes[name, s] = keep.tile([P, H], U32, name="codes_%s%d" % (name, s), align_bytes=64)
+                scales[name, s] = keep.tile([P, H], U8, name="scales_%s%d" % (name, s), align_bytes=64)
 
-        def quantised(name, s):
-            grouped = keep.tile([P, PACK, P, PACK], BF16, name="grouped_%s%d" % (name, s), align_bytes=64)
-            codes = keep.tile([P, H], U32, name="codes_%s%d" % (name, s), align_bytes=64)
-            plane = keep.tile([P, H], U8, name="plane_%s%d" % (name, s), align_bytes=64)
-            return raw[name, s], grouped, codes, plane
+        def regroup(copy, name, s, t0, t1, m0=0, m1=P):
+            if (name, s, t0) not in grouped:
+                grouped[name, s, t0] = keep.tile(
+                    [P, t1 - t0, P, PACK], BF16, name="grouped_%s%d_%d" % (name, s, t0), align_bytes=64
+                )
+            source = raw[name, s][:].rearrange("p j (m t) -> p m j t", t=PACK)
+            target = grouped[name, s, t0][:].rearrange("p t m j -> p m j t")
+            copy(out=target[:, m0:m1], in_=source[:, m0:m1, :, t0:t1])
 
-        def regroup(tiles, t0, t1, split):
-            loaded, grouped = tiles[0], tiles[1]
-            source = loaded[:].rearrange("p j (m t) -> p m t j", t=PACK)
-            target = grouped[:].rearrange("p t m j -> p m t j")
-            on_vector(out=target[:, 0:split, t0:t1, :], in_=source[:, 0:split, t0:t1, :])
-            if split < P:
-                on_scalar(out=target[:, split:P, t0:t1, :], in_=source[:, split:P, t0:t1, :])
-
-        def quantise(tiles, t0, t1):
-            grouped, codes, plane = tiles[1], tiles[2], tiles[3]
+        def quantise_w(name, s, t0, t1):
             nc.vector.quantize_mx(
-                out=codes[:, t0 * P : t1 * P].bitcast(FP8X4),
-                scales=plane[:, t0 * P : t1 * P],
-                in_=grouped[:].rearrange("p t m j -> p (t m j)")[:, PACK * t0 * P : PACK * t1 * P],
+                out=codes[name, s][:, t0 * P : t1 * P].bitcast(FP8X4),
+                scales=scales[name, s][:, t0 * P : t1 * P],
+                in_=grouped[name, s, t0][:].rearrange("p t m j -> p (t m j)"),
             )
 
-        def first_product(acc, tiles, s, t, tokens=slice(0, T)):
-            codes, plane = tiles[2], tiles[3]
+        def shared_product(acc, name, s, t, tokens, start, stop):
             nc.tensor.matmul_mx(
                 out=acc,
-                lhsT=codes[:, t * P : (t + 1) * P].bitcast(FP8X4),
-                lhsT_scale=plane[:, t * P : (t + 1) * P],
+                lhsT=codes[name, s][:, t * P : (t + 1) * P].bitcast(FP8X4),
+                lhsT_scale=scales[name, s][:, t * P : (t + 1) * P],
                 rhs=x_codes[:, s, tokens].bitcast(FP8X4),
-                rhs_scale=x_plane[:, s, tokens],
-                start=(s == 0),
-                stop=(s == PASSES - 1),
+                rhs_scale=x_bytes[4 * s : P, tokens],
+                start=start,
+                stop=stop,
             )
 
-        w1q = [quantised("w1", s) for s in range(PASSES)]
-        a_banks = [bank(t) for t in range(PACK)]
-        for s in range(PASSES):
-            regroup(w1q[s], 0, PACK, P)
-            quantise(w1q[s], 0, PACK)
-            for t in (2, 3, 0, 1):
-                first_product(a_banks[t][:], w1q[s], s, t)
+        def plane_pass(acc, name, s, t):
+            shared_product(acc[:], name, s, t, slice(0, T), s == 0, s == PASSES - 1)
+
+        def pair_pass(acc, s, half):
+            tokens = slice(half * HALF, (half + 1) * HALF)
+            for t in range(2):
+                start, stop = s == 0 and t == 0, s == PASSES - 1 and t == 1
+                shared_product(acc[:, t * HALF : (t + 1) * HALF], "w3", s, t, tokens, start, stop)
+
+        gate_sums = [bank(t) for t in range(PACK)]
+        regroup(on_vector, "w1", 0, 0, PACK)
+        quantise_w("w1", 0, 0, PACK)
+        for t in range(PACK):
+            plane_pass(gate_sums[t], "w1", 0, t)
+        for t0 in (2, 0):
+            regroup(on_vector, "w1", 1, t0, t0 + 2)
+            quantise_w("w1", 1, t0, t0 + 2)
+            for t in (t0, t0 + 1):
+                plane_pass(gate_sums[t], "w1", 1, t)
         sig = keep.tile([P, PACK, T], F32)
         for t in (2, 3, 0, 1):
-            nc.scalar.activation(out=sig[:, t, :], in_=a_banks[t][:], func=SIGMOID)
+            nc.scalar.activation(out=sig[:, t, :], in_=gate_sums[t][:], func=SIGMOID)
 
-        w3q = [quantised("w3", s) for s in range(PASSES)]
-        b_banks = [bank(PACK + t) for t in range(PACK)]
-        h = keep.tile([P, 2, T], BF16)
-        h_pairs = keep.tile([P, T, 2], BF16)
-        regroup(w3q[0], 0, PACK, P)
-        quantise(w3q[0], 0, PACK)
+        plane_sums = {2: bank(4), 3: bank(5)}
+        pair_sums = [bank(6), bank(7)]
+        regroup(on_vector, "w3", 0, 2, 4)
+        quantise_w("w3", 0, 2, 4)
         for t in (2, 3):
-            first_product(b_banks[t - 2][:], w3q[0], 0, t)
-        regroup(w3q[1], 2, 4, SPLIT)
-        quantise(w3q[1], 2, 4)
-        for t in (2, 3):
-            first_product(b_banks[t - 2][:], w3q[1], 1, t)
-        regroup(w3q[1], 0, 2, P // 2)
-        nc.vector.tensor_tensor(out=h[:, 0, :], in0=b_banks[0][:], in1=sig[:, 2, :], op=MULT)
-        quantise(w3q[1], 0, 2)
-        nc.vector.tensor_tensor(out=h[:, 1, :], in0=b_banks[1][:], in1=sig[:, 3, :], op=MULT)
+            plane_pass(plane_sums[t], "w3", 0, t)
+        regroup(on_vector, "w3", 0, 0, 2)
+        quantise_w("w3", 0, 0, 2)
         for half in range(2):
-            tokens = slice(half * T // 2, (half + 1) * T // 2)
-            acc = b_banks[2 + half]
-            for t in range(2):
-                for s in range(PASSES):
-                    first_product(acc[:, t * T // 2 : (t + 1) * T // 2], w3q[s], s, t, tokens)
+            pair_pass(pair_sums[half], 0, half)
+
+        regroup(on_vector, "w3", 1, 2, 4, 0, FIRST_SPLIT)
+        regroup(on_scalar, "w3", 1, 2, 4, FIRST_SPLIT, P)
+        regroup(on_scalar, "w3", 1, 0, 2, SECOND_SPLIT, P)
+        quantise_w("w3", 1, 2, 4)
+        for t in (2, 3):
+            plane_pass(plane_sums[t], "w3", 1, t)
+        regroup(on_vector, "w3", 1, 0, 2, 0, SECOND_SPLIT)
+        quantise_w("w3", 1, 0, 2)
+
+        h = keep.tile([P, PACK * T], BF16)
+        for t in (2, 3):
+            nc.vector.tensor_tensor(out=h[:, t * T : (t + 1) * T], in0=plane_sums[t][:], in1=sig[:, t, :], op=MULT)
+        for half in range(2):
+            pair_pass(pair_sums[half], 1, half)
             nc.vector.tensor_tensor(
-                out=h_pairs[:, tokens, :],
-                in0=acc[:].rearrange("p (e t) -> p t e", e=2),
-                in1=sig[:, 0:2, tokens].rearrange("p e t -> p t e"),
+                out=h[:, half * T : (half + 1) * T].rearrange("p (t e) -> p t e", e=2),
+                in0=pair_sums[half][:].rearrange("p (e t) -> p t e", e=2),
+                in1=sig[:, 0:2, half * HALF : (half + 1) * HALF].rearrange("p e t -> p t e"),
                 op=MULT,
             )
-        h_words = h_pairs[:].rearrange("p t e -> p (t e)").bitcast(U32)
+        pair_window = h[:, 0 : 3 * T].bitcast(U32)
 
+        picked = [keep.tile([P, 2, 4 * C], BF16, name="picked%d" % g) for g in range(E // 2)]
+        joined = keep.tile([P, S, 2, 2], BF16, align_bytes=64)
         h_codes = keep.tile([P, S], U32, align_bytes=64)
-        h_plane = keep.tile([P, S], U8, align_bytes=64)
+        h_scales = keep.tile([P, S], U8, align_bytes=64)
         y = [keep.tile([P, S], F32, name="y%d" % nt) for nt in range(N_TILES)]
 
-        picked = [keep.tile([P, 2, 2 * C], BF16, name="picked%d" % e) for e in range(E)]
+        def tokens_of(e0, e1):
+            return slot_token[:, e0 * C // LIST_ROWS : e1 * C // LIST_ROWS]
 
-        def gather_planes(e):
-            tokens = slot_token[:, e * C // 16 : (e + 1) * C // 16]
-            for d in range(2):
-                nc.scalar.activation(out=picked[e][:, 1, d : 2 * C : 2], in_=h[:, d, :].indirect(tokens), func=COPY)
+        def gather_plane(e, t):
+            first = (e % 2) * 2 * C + t - 2
+            nc.scalar.activation(
+                out=picked[e // 2][:, 1, first : (e % 2 + 1) * 2 * C : 2],
+                in_=h[:, t * T : (t + 1) * T].indirect(tokens_of(e, e + 1)),
+                func=COPY,
+            )
 
-        def gather_pairs(e):
-            tokens = slot_token[:, e * C // 16 : (e + 1) * C // 16]
-            nc.vector.tensor_copy(out=picked[e][:, 0, :].bitcast(U32), in_=h_words.indirect(tokens))
+        def gather_pairs(g):
+            on_vector(out=picked[g][:, 0, :].bitcast(U32), in_=pair_window.indirect(tokens_of(2 * g, 2 * g + 2)))
 
-        def join_pairs(e):
-            h_slots = keep.tile([P, C, 2, 2], BF16, name="h_slots%d" % e, align_bytes=64)
-            nc.vector.tensor_copy(out=h_slots[:], in_=picked[e][:].rearrange("p u (c e) -> p c u e", e=2))
-            return h_slots
+        def join_pairs(e0, e1):
+            pairs = picked[e0 // 2][:].rearrange("p u (c e) -> p c u e", e=2)
+            first = (e0 % 2) * C
+            on_vector(out=joined[:, e0 * C : e1 * C], in_=pairs[:, first : first + (e1 - e0) * C])
 
-        def expert_product(e, nt, acc, slots):
+        def expert_product(nt, acc, s0, s1):
+            e = s0 // C
             nc.tensor.matmul_mx(
                 out=acc,
                 lhsT=w2_codes[:, e, 2 * nt * P : 2 * (nt + 1) * P].bitcast(FP4X4),
-                lhsT_scale=w2_plane[:, e, nt * P : (nt + 1) * P],
-                rhs=h_codes[:, slots].bitcast(FP8X4),
-                rhs_scale=h_plane[:, slots],
+                lhsT_scale=w2_bytes[:, e, nt * P : (nt + 1) * P],
+                rhs=h_codes[:, s0:s1].bitcast(FP8X4),
+                rhs_scale=h_scales[:, s0:s1],
                 start=True,
                 stop=True,
             )
 
-        def first_tile(e, h_slots, c0, c1, acc):
-            slots = slice(e * C + c0, e * C + c1)
+        def first_products(s0, s1, acc):
             nc.vector.quantize_mx(
-                out=h_codes[:, slots].bitcast(FP8X4),
-                scales=h_plane[:, slots],
-                in_=h_slots[:, c0:c1].rearrange("p c u e -> p (c u e)"),
+                out=h_codes[:, s0:s1].bitcast(FP8X4),
+                scales=h_scales[:, s0:s1],
+                in_=joined[:, s0:s1].rearrange("p c u e -> p (c u e)"),
             )
-            expert_product(e, 0, acc, slots)
+            for c in range(s0, s1, C):
+                end = min(c + C, s1)
+                expert_product(0, acc[:, c - s0 : end - s0], c, end)
 
-        pair_banks = [bank(0), bank(1), bank(4)]
         for e in range(E):
-            gather_planes(e)
+            for t in (2, 3):
+                gather_plane(e, t)
+
+        steps = [(0, 2 * C), (2 * C, 4 * C), (4 * C, 5 * C), (5 * C, S - C // 2), (S - C // 2, S)]
+        step_banks = [bank(b) for b in (0, 1, 4, 5, 6)]
         gather_pairs(0)
         gather_pairs(1)
-        for e in range(E - 1):
-            h_slots = join_pairs(e)
-            if e + 2 < E:
-                gather_pairs(e + 2)
-            else:
-                last_slots = join_pairs(E - 1)
-            first_tile(e, h_slots, 0, C, pair_banks[e // 2][:, (e % 2) * C : (e % 2 + 1) * C])
-        nc.scalar.copy(out=y[0][:, 0:BANK], in_=pair_banks[0][:])
-        nc.scalar.copy(out=y[0][:, BANK : 2 * BANK], in_=pair_banks[1][:])
-        nc.scalar.copy(out=y[0][:, 2 * BANK : 2 * BANK + C], in_=pair_banks[2][:, 0:C])
-        for half in range(2):
-            acc = bank(5 + half)
-            c0 = half * C // 2
-            first_tile(E - 1, last_slots, c0, c0 + C // 2, acc[:, 0 : C // 2])
-            nc.vector.tensor_copy(out=y[0][:, (E - 1) * C + c0 : (E - 1) * C + c0 + C // 2], in_=acc[:, 0 : C // 2])
+        join_pairs(0, 2)
+        gather_pairs(2)
+        first_products(*steps[0], step_banks[0])
+        join_pairs(2, 4)
+        join_pairs(4, 5)
+        first_products(*steps[1], step_banks[1])
+        join_pairs(5, 6)
+        for step in range(2, len(steps)):
+            first_products(*steps[step], step_banks[step])
+        for (s0, s1), acc, copy in zip(steps, step_banks, [on_scalar] * 3 + [on_vector] * 2):
+            copy(out=y[0][:, s0:s1], in_=acc[:, 0 : s1 - s0])
 
-        def slot_results(nt):
+        for nt in range(1, N_TILES):
             for g in range(E // 2):
-                acc = bank(E - g)
-                for e in (2 * g, 2 * g + 1):
-                    expert_product(e, nt, acc[:, (e % 2) * C : (e % 2 + 1) * C], slice(e * C, (e + 1) * C))
-                nc.scalar.copy(out=y[nt][:, g * BANK : (g + 1) * BANK], in_=acc[:])
+                acc = bank(6 - g)
+                for u in range(2):
+                    expert_product(nt, acc[:, u * C : (u + 1) * C], (2 * g + u) * C, (2 * g + u + 1) * C)
+                on_scalar(out=y[nt][:, g * BANK : (g + 1) * BANK], in_=acc[:])
 
-        def weighted(nt, r, product, t0, t1):
+        products = [[keep.tile([P, T], F32, name="product%d_%d" % (nt, r)) for r in range(TOP)] for nt in range(N_TILES)]
+
+        def weighted(nt, r, t0, t1):
             nc.vector.tensor_tensor(
-                out=product[:, t0:t1],
-                in0=y[nt][:].indirect(token_slot[r][:, t0 // 16 : t1 // 16]),
+                out=products[nt][r][:, t0:t1],
+                in0=y[nt][:].indirect(token_slot[r][:, t0 // LIST_ROWS : t1 // LIST_ROWS]),
                 in1=gates[:, r, t0:t1],
                 op=MULT,
             )
 
-        def turn(turned, product, t0, t1, start, stop):
-            for c in range(t0, t1, P):
-                nc.tensor.matmul(
-                    out=turned[:, c - t0 : c - t0 + P], lhsT=product[:, c : c + P], rhs=ident[:],
-                    start=(start and c == t0), stop=(stop and c == t1 - P), is_transpose=True,
-                )
-
-        def turn_back(turned, width, back):
-            summed = ring.tile([P, T], F32)
-            nc.scalar.copy(out=summed[:, 0:width], in_=turned[:, 0:width])
-            for c in range(0, width, P):
-                nc.tensor.transpose(back[:, c : c + P], summed[:, c : c + P], ident[:])
-
-        def store(nt, back, t0, t1):
-            result = keep.tile([P, t1 - t0], F32, name="result%d_%d" % (nt, t0))
-            nc.scalar.copy(out=result[:], in_=back[:, 0 : t1 - t0])
-            nc.scalar.dma_start(out=out[nt * P : (nt + 1) * P, t0:t1], in_=result[:])
-
-        for nt in range(1, N_TILES):
-            slot_results(nt)
-
-        products = [[keep.tile([P, T], F32, name="product%d_%d" % (nt, r)) for r in range(TOP)] for nt in range(N_TILES)]
+        blocks = [slice(c, c + P) for c in range(0, T, P)]
         for nt in range(N_TILES - 1):
             turned = bank(6)
             for r in range(TOP):
-                weighted(nt, r, products[nt][r], 0, T)
-                turn(turned, products[nt][r], 0, T, r == 0, r == TOP - 1)
+                weighted(nt, r, 0, T)
+                for c, cols in enumerate(blocks):
+                    nc.tensor.matmul(
+                        out=turned[:, cols],
+                        lhsT=products[nt][r][:, cols],
+                        rhs=ident[:],
+                        start=(r == 0 and c == 0),
+                        stop=(r == TOP - 1 and c == len(blocks) - 1),
+                        is_transpose=True,
+                    )
             back = bank(nt)
-            turn_back(turned, T, back)
-            store(nt, back, 0, T)
+            summed = ring.tile([P, T], F32)
+            on_scalar(out=summed[:], in_=turned[:])
+            for cols in blocks:
+                nc.tensor.transpose(back[:, cols], summed[:, cols], ident[:])
+            result = keep.tile([P, T], F32, name="result%d" % nt)
+            on_scalar(out=result[:], in_=back[:])
+            nc.scalar.dma_start(out=out[nt * P : (nt + 1) * P, :], in_=result[:])
 
         nt = N_TILES - 1
         partial = keep.tile([P, T], F32)
         last = keep.tile([P, T], F32)
-        weighted(nt, 0, products[nt][0], 0, T)
-        weighted(nt, 1, products[nt][1], 0, T)
-        weighted(nt, 2, products[nt][2], 0, T // 2)
+        weighted(nt, 0, 0, T)
+        weighted(nt, 1, 0, T)
+        weighted(nt, 2, 0, HALF)
         nc.vector.tensor_tensor(out=partial[:], in0=products[nt][0][:], in1=products[nt][1][:], op=ADD)
-        weighted(nt, 2, products[nt][2], T // 2, T)
-        for t0 in (0, T // 2):
-            cols = slice(t0, t0 + T // 2)
+        weighted(nt, 2, HALF, T)
+        for cols in (slice(0, HALF), slice(HALF, T)):
             nc.vector.tensor_tensor(out=last[:, cols], in0=partial[:, cols], in1=products[nt][2][:, cols], op=ADD)
             nc.sync.dma_start(out=out[nt * P : (nt + 1) * P, cols], in_=last[:, cols])

@@ -173,7 +173,8 @@ def tile_moe_sup_glu_sigmoid_kernel(
         regroup(on_vector, "w3", 1, 0, 2, 0, SECOND_SPLIT)
         quantise_w("w3", 1, 0, 2)
 
-        h = keep.tile([P, PACK * T], BF16)
+        h = keep.tile([P, PACK * T + HALF], BF16)
+        nc.vector.memset(h[:, PACK * T :], 0.0)
         for t in (2, 3):
             nc.vector.tensor_tensor(out=h[:, t * T : (t + 1) * T], in0=plane_sums[t][:], in1=sig[:, t, :], op=MULT)
         for half in range(2):
@@ -195,11 +196,12 @@ def tile_moe_sup_glu_sigmoid_kernel(
         def tokens_of(e0, e1):
             return slot_token[:, e0 * C // LIST_ROWS : e1 * C // LIST_ROWS]
 
-        def gather_plane(e, t):
-            first = (e % 2) * 2 * C + t - 2
+        def gather_plane(e0, e1, t):
+            first = (e0 % 2) * 2 * C
+            columns = T if e1 - e0 == 1 else T + HALF
             nc.scalar.activation(
-                out=picked[e // 2][:, 1, first : (e % 2 + 1) * 2 * C : 2],
-                in_=h[:, t * T : (t + 1) * T].indirect(tokens_of(e, e + 1)),
+                out=picked[e0 // 2][:, 1, first + t - 2 : first + (e1 - e0) * 2 * C : 2],
+                in_=h[:, t * T : t * T + columns].indirect(tokens_of(e0, e1)),
                 func=COPY,
             )
 
@@ -233,9 +235,14 @@ def tile_moe_sup_glu_sigmoid_kernel(
                 end = min(c + C, s1)
                 expert_product(0, acc[:, c - s0 : end - s0], c, end)
 
-        for e in range(E):
-            for t in (2, 3):
-                gather_plane(e, t)
+        gather_plane(0, 1, 2)
+        gather_plane(1, 2, 2)
+        gather_plane(0, 2, 3)
+        gather_plane(2, 4, 2)
+        gather_plane(2, 4, 3)
+        gather_plane(4, 6, 2)
+        gather_plane(4, 5, 3)
+        gather_plane(5, 6, 3)
 
         steps = [(0, 2 * C), (2 * C, 4 * C), (4 * C, 5 * C), (5 * C, S - C // 2), (S - C // 2, S)]
         step_banks = [bank(b) for b in (0, 1, 4, 5, 6)]
@@ -296,11 +303,11 @@ def tile_moe_sup_glu_sigmoid_kernel(
         nt = N_TILES - 1
         partial = keep.tile([P, T], F32)
         last = keep.tile([P, T], F32)
-        weighted(nt, 0, 0, T)
-        weighted(nt, 1, 0, T)
-        weighted(nt, 2, 0, HALF)
-        nc.vector.tensor_tensor(out=partial[:], in0=products[nt][0][:], in1=products[nt][1][:], op=ADD)
-        weighted(nt, 2, HALF, T)
-        for cols in (slice(0, HALF), slice(HALF, T)):
+        halves = (slice(0, HALF), slice(HALF, T))
+        for r in range(TOP):
+            weighted(nt, r, 0, T)
+        for cols in halves:
+            nc.vector.tensor_tensor(out=partial[:, cols], in0=products[nt][0][:, cols], in1=products[nt][1][:, cols], op=ADD)
+        for cols in halves:
             nc.vector.tensor_tensor(out=last[:, cols], in0=partial[:, cols], in1=products[nt][2][:, cols], op=ADD)
             nc.sync.dma_start(out=out[nt * P : (nt + 1) * P, cols], in_=last[:, cols])

@@ -187,8 +187,19 @@ def tile_moe_sup_glu_sigmoid_kernel(
             )
         pair_window = h[:, 0 : 3 * T].bitcast(U32)
 
-        picked = [keep.tile([P, 2, 4 * C], BF16, name="picked%d" % g) for g in range(E // 2)]
-        joined = keep.tile([P, S, 2, 2], BF16, align_bytes=64)
+        late_pairs = keep.tile([P, T], U32)
+        nc.gpsimd.tensor_copy(
+            out=late_pairs[:].bitcast(BF16).rearrange("p (t e) -> p t e", e=2),
+            in_=h[:, 2 * T : 4 * T].rearrange("p (e t) -> p t e", e=2),
+        )
+
+        row = keep.tile([P, 9 * C], U32, align_bytes=64)
+        early = [keep.tile([P, 2, 2 * C], U32, name="early%d" % g) for g in range(2)]
+        late_joined = keep.tile([P, 4 * C], U32, align_bytes=64)
+        picked = [early[e // 2][:, :, (e % 2) * C : (e % 2 + 1) * C] for e in range(4)]
+        picked.append(row[:, 0 : 8 * C].rearrange("p (u x) -> p u x", x=C)[:, 0:8:7, :])
+        picked.append(row[:, C : 3 * C].rearrange("p (u x) -> p u x", u=2))
+        joined = [row[:, 0 : 4 * C], row[:, 3 * C : 7 * C], late_joined[:]]
         h_codes = keep.tile([P, S], U32, align_bytes=64)
         h_scales = keep.tile([P, S], U8, align_bytes=64)
         y = [keep.tile([P, S], F32, name="y%d" % nt) for nt in range(N_TILES)]
@@ -197,21 +208,22 @@ def tile_moe_sup_glu_sigmoid_kernel(
             return slot_token[:, e0 * C // LIST_ROWS : e1 * C // LIST_ROWS]
 
         def gather_plane(e0, e1, t):
+            target = early[e0 // 2][:, 1, :] if e0 < 4 else row[:, 7 * C : 8 * C]
             first = (e0 % 2) * 2 * C
-            columns = T if e1 - e0 == 1 else T + HALF
+            columns = T if t == 2 and e0 < 2 else T + HALF
             nc.scalar.activation(
-                out=picked[e0 // 2][:, 1, first + t - 2 : first + (e1 - e0) * 2 * C : 2],
+                out=target.bitcast(BF16)[:, first + t - 2 : first + (e1 - e0) * 2 * C : 2],
                 in_=h[:, t * T : t * T + columns].indirect(tokens_of(e0, e1)),
                 func=COPY,
             )
 
-        def gather_pairs(g):
-            on_vector(out=picked[g][:, 0, :].bitcast(U32), in_=pair_window.indirect(tokens_of(2 * g, 2 * g + 2)))
+        def gather_pairs(e0, e1):
+            target = early[e0 // 2][:, 0, :] if e0 < 4 else row[:, 0 : 2 * C]
+            on_vector(out=target[:, (e0 % 2) * C : (e0 % 2 + e1 - e0) * C], in_=pair_window.indirect(tokens_of(e0, e1)))
 
-        def join_pairs(e0, e1):
-            pairs = picked[e0 // 2][:].rearrange("p u (c e) -> p c u e", e=2)
-            first = (e0 % 2) * C
-            on_vector(out=joined[:, e0 * C : e1 * C], in_=pairs[:, first : first + (e1 - e0) * C])
+        def join(e, copy):
+            target = joined[e // 2][:, (e % 2) * 2 * C : (e % 2 + 1) * 2 * C]
+            copy(out=target.rearrange("p (c u) -> p c u", u=2), in_=picked[e].rearrange("p u c -> p c u"))
 
         def expert_product(nt, acc, s0, s1):
             e = s0 // C
@@ -229,7 +241,7 @@ def tile_moe_sup_glu_sigmoid_kernel(
             nc.vector.quantize_mx(
                 out=h_codes[:, s0:s1].bitcast(FP8X4),
                 scales=h_scales[:, s0:s1],
-                in_=joined[:, s0:s1].rearrange("p c u e -> p (c u e)"),
+                in_=joined[s0 // (2 * C)][:, 2 * (s0 % (2 * C)) : 2 * (s0 % (2 * C) + s1 - s0)].bitcast(BF16),
             )
             for c in range(s0, s1, C):
                 end = min(c + C, s1)
@@ -240,25 +252,33 @@ def tile_moe_sup_glu_sigmoid_kernel(
         gather_plane(0, 2, 3)
         gather_plane(2, 4, 2)
         gather_plane(2, 4, 3)
-        gather_plane(4, 6, 2)
+        gather_plane(4, 5, 2)
         gather_plane(4, 5, 3)
-        gather_plane(5, 6, 3)
 
         steps = [(0, 2 * C), (2 * C, 4 * C), (4 * C, 5 * C), (5 * C, S - C // 2), (S - C // 2, S)]
         step_banks = [bank(b) for b in (0, 1, 4, 5, 6)]
-        gather_pairs(0)
-        gather_pairs(1)
-        join_pairs(0, 2)
-        gather_pairs(2)
+        def empty(step, copy):
+            s0, s1 = steps[step]
+            copy(out=y[0][:, s0:s1], in_=step_banks[step][:, 0 : s1 - s0])
+
+        on_gpsimd = nc.gpsimd.tensor_copy
+        gather_pairs(0, 1)
+        gather_pairs(1, 2)
+        gather_pairs(2, 4)
+        join(0, on_gpsimd)
+        join(1, on_gpsimd)
         first_products(*steps[0], step_banks[0])
-        join_pairs(2, 4)
-        join_pairs(4, 5)
+        gather_pairs(4, 6)
+        on_vector(out=row[:, 2 * C : 3 * C], in_=late_pairs[:].indirect(tokens_of(5, 6)))
+        join(2, on_gpsimd)
+        join(3, on_gpsimd)
+        join(4, on_scalar)
+        join(5, on_scalar)
         first_products(*steps[1], step_banks[1])
-        join_pairs(5, 6)
         for step in range(2, len(steps)):
             first_products(*steps[step], step_banks[step])
-        for (s0, s1), acc, copy in zip(steps, step_banks, [on_scalar] * 3 + [on_vector] * 2):
-            copy(out=y[0][:, s0:s1], in_=acc[:, 0 : s1 - s0])
+        for step, copy in ((0, on_scalar), (1, on_scalar), (2, on_scalar), (3, on_vector), (4, on_vector)):
+            empty(step, copy)
 
         for nt in range(1, N_TILES):
             for g in range(E // 2):

@@ -173,33 +173,26 @@ def tile_moe_sup_glu_sigmoid_kernel(
         regroup(on_vector, "w3", 1, 0, 2, 0, SECOND_SPLIT)
         quantise_w("w3", 1, 0, 2)
 
-        h = keep.tile([P, PACK * T + HALF], BF16)
-        nc.vector.memset(h[:, PACK * T :], 0.0)
+        h = keep.tile([P, 6 * T + HALF], BF16)
+        nc.vector.memset(h[:, 6 * T :], 0.0)
         for t in (2, 3):
-            nc.vector.tensor_tensor(out=h[:, t * T : (t + 1) * T], in0=plane_sums[t][:], in1=sig[:, t, :], op=MULT)
+            nc.vector.tensor_tensor(out=h[:, (t + 2) * T : (t + 3) * T], in0=plane_sums[t][:], in1=sig[:, t, :], op=MULT)
+        nc.gpsimd.tensor_copy(
+            out=h[:, 0 : 2 * T].rearrange("p (t e) -> p t e", e=2),
+            in_=h[:, 4 * T : 6 * T].rearrange("p (e t) -> p t e", e=2),
+        )
         for half in range(2):
             pair_pass(pair_sums[half], 1, half)
             nc.vector.tensor_tensor(
-                out=h[:, half * T : (half + 1) * T].rearrange("p (t e) -> p t e", e=2),
+                out=h[:, (half + 2) * T : (half + 3) * T].rearrange("p (t e) -> p t e", e=2),
                 in0=pair_sums[half][:].rearrange("p (e t) -> p t e", e=2),
                 in1=sig[:, 0:2, half * HALF : (half + 1) * HALF].rearrange("p e t -> p t e"),
                 op=MULT,
             )
-        pair_window = h[:, 0 : 3 * T].bitcast(U32)
+        pair_window = [h[:, 2 * T : 5 * T].bitcast(U32), h[:, 0 : 3 * T].bitcast(U32)]
 
-        late_pairs = keep.tile([P, T], U32)
-        nc.gpsimd.tensor_copy(
-            out=late_pairs[:].bitcast(BF16).rearrange("p (t e) -> p t e", e=2),
-            in_=h[:, 2 * T : 4 * T].rearrange("p (e t) -> p t e", e=2),
-        )
-
-        row = keep.tile([P, 9 * C], U32, align_bytes=64)
-        early = [keep.tile([P, 2, 2 * C], U32, name="early%d" % g) for g in range(2)]
-        late_joined = keep.tile([P, 4 * C], U32, align_bytes=64)
-        picked = [early[e // 2][:, :, (e % 2) * C : (e % 2 + 1) * C] for e in range(4)]
-        picked.append(row[:, 0 : 8 * C].rearrange("p (u x) -> p u x", x=C)[:, 0:8:7, :])
-        picked.append(row[:, C : 3 * C].rearrange("p (u x) -> p u x", u=2))
-        joined = [row[:, 0 : 4 * C], row[:, 3 * C : 7 * C], late_joined[:]]
+        picked = [keep.tile([P, 2, 2 * C], U32, name="picked%d" % g) for g in range(E // 2)]
+        joined = keep.tile([P, S, 2], U32, align_bytes=64)
         h_codes = keep.tile([P, S], U32, align_bytes=64)
         h_scales = keep.tile([P, S], U8, align_bytes=64)
         y = [keep.tile([P, S], F32, name="y%d" % nt) for nt in range(N_TILES)]
@@ -208,22 +201,20 @@ def tile_moe_sup_glu_sigmoid_kernel(
             return slot_token[:, e0 * C // LIST_ROWS : e1 * C // LIST_ROWS]
 
         def gather_plane(e0, e1, t):
-            target = early[e0 // 2][:, 1, :] if e0 < 4 else row[:, 7 * C : 8 * C]
             first = (e0 % 2) * 2 * C
-            columns = T if t == 2 and e0 < 2 else T + HALF
+            columns = T if e1 - e0 == 1 else T + HALF
             nc.scalar.activation(
-                out=target.bitcast(BF16)[:, first + t - 2 : first + (e1 - e0) * 2 * C : 2],
-                in_=h[:, t * T : t * T + columns].indirect(tokens_of(e0, e1)),
+                out=picked[e0 // 2][:, 1, :].bitcast(BF16)[:, first + t - 2 : first + (e1 - e0) * 2 * C : 2],
+                in_=h[:, (t + 2) * T : (t + 2) * T + columns].indirect(tokens_of(e0, e1)),
                 func=COPY,
             )
 
-        def gather_pairs(e0, e1):
-            target = early[e0 // 2][:, 0, :] if e0 < 4 else row[:, 0 : 2 * C]
-            on_vector(out=target[:, (e0 % 2) * C : (e0 % 2 + e1 - e0) * C], in_=pair_window.indirect(tokens_of(e0, e1)))
+        def gather_pairs(g, u):
+            on_vector(out=picked[g][:, u, :], in_=pair_window[u].indirect(tokens_of(2 * g, 2 * g + 2)))
 
-        def join(e, copy):
-            target = joined[e // 2][:, (e % 2) * 2 * C : (e % 2 + 1) * 2 * C]
-            copy(out=target.rearrange("p (c u) -> p c u", u=2), in_=picked[e].rearrange("p u c -> p c u"))
+        def join(e0, e1, copy):
+            pairs = picked[e0 // 2][:].rearrange("p u c -> p c u")
+            copy(out=joined[:, e0 * C : e1 * C], in_=pairs[:, (e0 % 2) * C : (e0 % 2 + e1 - e0) * C])
 
         def expert_product(nt, acc, s0, s1):
             e = s0 // C
@@ -241,7 +232,7 @@ def tile_moe_sup_glu_sigmoid_kernel(
             nc.vector.quantize_mx(
                 out=h_codes[:, s0:s1].bitcast(FP8X4),
                 scales=h_scales[:, s0:s1],
-                in_=joined[s0 // (2 * C)][:, 2 * (s0 % (2 * C)) : 2 * (s0 % (2 * C) + s1 - s0)].bitcast(BF16),
+                in_=joined[:, s0:s1].rearrange("p c u -> p (c u)").bitcast(BF16),
             )
             for c in range(s0, s1, C):
                 end = min(c + C, s1)
@@ -252,30 +243,22 @@ def tile_moe_sup_glu_sigmoid_kernel(
         gather_plane(0, 2, 3)
         gather_plane(2, 4, 2)
         gather_plane(2, 4, 3)
-        gather_plane(4, 5, 2)
-        gather_plane(4, 5, 3)
 
-        steps = [(0, 2 * C), (2 * C, 4 * C), (4 * C, 5 * C), (5 * C, S - C // 2), (S - C // 2, S)]
+        steps = [(4 * C, S), (0, 2 * C), (2 * C, 3 * C), (3 * C, 3 * C + C // 2), (3 * C + C // 2, 4 * C)]
         step_banks = [bank(b) for b in (0, 1, 4, 5, 6)]
         def empty(step, copy):
             s0, s1 = steps[step]
             copy(out=y[0][:, s0:s1], in_=step_banks[step][:, 0 : s1 - s0])
 
-        on_gpsimd = nc.gpsimd.tensor_copy
-        gather_pairs(0, 1)
-        gather_pairs(1, 2)
-        gather_pairs(2, 4)
-        join(0, on_gpsimd)
-        join(1, on_gpsimd)
-        first_products(*steps[0], step_banks[0])
-        gather_pairs(4, 6)
-        on_vector(out=row[:, 2 * C : 3 * C], in_=late_pairs[:].indirect(tokens_of(5, 6)))
-        join(2, on_gpsimd)
-        join(3, on_gpsimd)
-        join(4, on_scalar)
-        join(5, on_scalar)
-        first_products(*steps[1], step_banks[1])
-        for step in range(2, len(steps)):
+        gather_pairs(2, 0)
+        gather_pairs(2, 1)
+        gather_pairs(0, 0)
+        gather_pairs(1, 0)
+        join(4, 6, nc.gpsimd.tensor_copy)
+        join(0, 2, on_scalar)
+        join(2, 3, on_scalar)
+        join(3, 4, on_scalar)
+        for step in range(len(steps)):
             first_products(*steps[step], step_banks[step])
         for step, copy in ((0, on_scalar), (1, on_scalar), (2, on_scalar), (3, on_vector), (4, on_vector)):
             empty(step, copy)

@@ -197,20 +197,20 @@ def tile_moe_sup_glu_sigmoid_kernel(
         h_scales = keep.tile([P, S], U8, align_bytes=64)
         y = [keep.tile([P, S], F32, name="y%d" % nt) for nt in range(N_TILES)]
 
-        def tokens_of(e0, e1):
-            return slot_token[:, e0 * C // LIST_ROWS : e1 * C // LIST_ROWS]
+        def tokens_of(s0, s1):
+            return slot_token[:, s0 // LIST_ROWS : s1 // LIST_ROWS]
 
-        def gather_plane(e0, e1, t):
-            first = (e0 % 2) * 2 * C
-            columns = T if e1 - e0 == 1 else T + HALF
+        def gather_plane(s0, s1, t, columns=T + HALF):
+            first = 2 * (s0 % (2 * C))
             nc.scalar.activation(
-                out=picked[e0 // 2][:, 1, :].bitcast(BF16)[:, first + t - 2 : first + (e1 - e0) * 2 * C : 2],
-                in_=h[:, (t + 2) * T : (t + 2) * T + columns].indirect(tokens_of(e0, e1)),
+                out=picked[s0 // (2 * C)][:, 1, :].bitcast(BF16)[:, first + t - 2 : first + 2 * (s1 - s0) : 2],
+                in_=h[:, (t + 2) * T : (t + 2) * T + columns].indirect(tokens_of(s0, s1)),
                 func=COPY,
             )
 
-        def gather_pairs(g, u):
-            on_vector(out=picked[g][:, u, :], in_=pair_window[u].indirect(tokens_of(2 * g, 2 * g + 2)))
+        def gather_pairs(s0, s1, u):
+            first = s0 % (2 * C)
+            on_vector(out=picked[s0 // (2 * C)][:, u, first : first + s1 - s0], in_=pair_window[u].indirect(tokens_of(s0, s1)))
 
         def join(e0, e1, copy):
             pairs = picked[e0 // 2][:].rearrange("p u c -> p c u")
@@ -238,11 +238,14 @@ def tile_moe_sup_glu_sigmoid_kernel(
                 end = min(c + C, s1)
                 expert_product(0, acc[:, c - s0 : end - s0], c, end)
 
-        gather_plane(0, 1, 2)
-        gather_plane(1, 2, 2)
-        gather_plane(0, 2, 3)
-        gather_plane(2, 4, 2)
-        gather_plane(2, 4, 3)
+        shared_from = 4 * C + C // 2
+        gather_plane(4 * C, shared_from, 2, T)
+        gather_plane(0, C, 2, T)
+        gather_plane(4 * C, shared_from, 3)
+        gather_plane(C, 2 * C, 2)
+        gather_plane(0, 2 * C, 3)
+        gather_plane(2 * C, 4 * C, 2)
+        gather_plane(2 * C, 4 * C, 3)
 
         steps = [(4 * C, S), (0, 2 * C), (2 * C, 3 * C), (3 * C, 3 * C + C // 2), (3 * C + C // 2, 4 * C)]
         step_banks = [bank(b) for b in (0, 1, 4, 5, 6)]
@@ -250,12 +253,13 @@ def tile_moe_sup_glu_sigmoid_kernel(
             s0, s1 = steps[step]
             copy(out=y[0][:, s0:s1], in_=step_banks[step][:, 0 : s1 - s0])
 
-        gather_pairs(2, 0)
-        gather_pairs(2, 1)
-        gather_pairs(0, 0)
-        gather_pairs(1, 0)
+        gather_pairs(4 * C, S, 0)
+        gather_pairs(shared_from, S, 1)
+        gather_pairs(0, 2 * C, 0)
+        gather_pairs(2 * C, 4 * C, 0)
         join(4, 6, nc.gpsimd.tensor_copy)
-        join(0, 2, on_scalar)
+        join(0, 1, nc.gpsimd.tensor_copy)
+        join(1, 2, on_scalar)
         join(2, 3, on_scalar)
         join(3, 4, on_scalar)
         for step in range(len(steps)):

@@ -284,11 +284,13 @@ def tile_moe_sup_glu_sigmoid_kernel(
                 op=MULT,
             )
 
-        blocks = [slice(c, c + P) for c in range(0, T, P)]
-        for nt in range(N_TILES - 1):
-            turned = bank(6)
+        last_tile = N_TILES - 1
+        parts = [(nt, T) for nt in range(last_tile)] + [(last_tile, HALF)]
+        for nt, tokens in parts:
+            blocks = [slice(c, c + P) for c in range(0, tokens, P)]
+            turned = bank(7 if tokens == T else 1)
             for r in range(TOP):
-                weighted(nt, r, 0, T)
+                weighted(nt, r, 0, tokens)
                 for c, cols in enumerate(blocks):
                     nc.tensor.matmul(
                         out=turned[:, cols],
@@ -300,21 +302,21 @@ def tile_moe_sup_glu_sigmoid_kernel(
                     )
             back = bank(nt)
             summed = ring.tile([P, T], F32)
-            on_scalar(out=summed[:], in_=turned[:])
+            on_scalar(out=summed[:, 0:tokens], in_=turned[:, 0:tokens])
             for cols in blocks:
                 nc.tensor.transpose(back[:, cols], summed[:, cols], ident[:])
             result = keep.tile([P, T], F32, name="result%d" % nt)
-            on_scalar(out=result[:], in_=back[:])
-            nc.scalar.dma_start(out=out[nt * P : (nt + 1) * P, :], in_=result[:])
+            on_scalar(out=result[:, 0:tokens], in_=back[:, 0:tokens])
+            nc.scalar.dma_start(out=out[nt * P : (nt + 1) * P, 0:tokens], in_=result[:, 0:tokens])
 
-        nt = N_TILES - 1
+        nt = last_tile
         partial = keep.tile([P, T], F32)
         last = keep.tile([P, T], F32)
-        halves = (slice(0, HALF), slice(HALF, T))
+        quarters = (slice(HALF, HALF + P), slice(HALF + P, T))
         for r in range(TOP):
-            weighted(nt, r, 0, T)
-        for cols in halves:
+            weighted(nt, r, HALF, T)
+        for cols in quarters:
             nc.vector.tensor_tensor(out=partial[:, cols], in0=products[nt][0][:, cols], in1=products[nt][1][:, cols], op=ADD)
-        for cols in halves:
+        for cols in quarters:
             nc.vector.tensor_tensor(out=last[:, cols], in0=partial[:, cols], in1=products[nt][2][:, cols], op=ADD)
             nc.sync.dma_start(out=out[nt * P : (nt + 1) * P, cols], in_=last[:, cols])

@@ -39,7 +39,6 @@ def tile_moe_sup_glu_sigmoid_kernel(
     on_vector, on_scalar = nc.vector.tensor_copy, nc.scalar.copy
     with ExitStack() as ctx:
         keep = ctx.enter_context(tc.tile_pool(name="keep", bufs=1))
-        ring = ctx.enter_context(tc.tile_pool(name="ring", bufs=2))
         psum = ctx.enter_context(tc.psum_pool(name="psum", bufs=1))
 
         def bank(b):
@@ -96,6 +95,11 @@ def tile_moe_sup_glu_sigmoid_kernel(
         for r, pos in enumerate((pos1, pos2, pos3)):
             nc.sync.dma_start(token_slot[r][:], pos)
         nc.sync.dma_start(out=gates[:], in_=gate.rearrange("r p t -> p r t"))
+        gate_columns = {}
+        with nc.allow_non_contiguous_dma(reason="one weight a partition"):
+            for r in (1, 2):
+                gate_columns[r] = keep.tile([P, T // P], F32, name="gate_column%d" % r)
+                nc.sync.dma_start(out=gate_columns[r][:], in_=gate[r, 0, :].rearrange("(c p) -> p c", p=P))
 
         codes, scales, grouped = {}, {}, {}
         for name in ("w1", "w3"):
@@ -267,56 +271,113 @@ def tile_moe_sup_glu_sigmoid_kernel(
         for step, copy in ((0, on_scalar), (1, on_scalar), (2, on_scalar), (3, on_vector), (4, on_vector)):
             empty(step, copy)
 
-        for nt in range(1, N_TILES):
+        filled = {}
+
+        def multiply(nt, g):
+            filled[nt, g] = bank(6 - g)
+            for u in range(2):
+                expert_product(nt, filled[nt, g][:, u * C : (u + 1) * C], (2 * g + u) * C, (2 * g + u + 1) * C)
+
+        def fill(nt):
             for g in range(E // 2):
-                acc = bank(6 - g)
-                for u in range(2):
-                    expert_product(nt, acc[:, u * C : (u + 1) * C], (2 * g + u) * C, (2 * g + u + 1) * C)
-                on_scalar(out=y[nt][:, g * BANK : (g + 1) * BANK], in_=acc[:])
+                on_scalar(out=y[nt][:, g * BANK : (g + 1) * BANK], in_=filled[nt, g][:])
+                if nt + 1 < N_TILES:
+                    multiply(nt + 1, g)
 
-        products = [[keep.tile([P, T], F32, name="product%d_%d" % (nt, r)) for r in range(TOP)] for nt in range(N_TILES)]
+        def row(name):
+            return keep.tile([P, T], F32, name=name)
 
-        def weighted(nt, r, t0, t1):
-            nc.vector.tensor_tensor(
-                out=products[nt][r][:, t0:t1],
-                in0=y[nt][:].indirect(token_slot[r][:, t0 // LIST_ROWS : t1 // LIST_ROWS]),
-                in1=gates[:, r, t0:t1],
-                op=MULT,
-            )
+        def slots_of(r, t0, t1):
+            return token_slot[r][:, t0 // LIST_ROWS : t1 // LIST_ROWS]
 
-        last_tile = N_TILES - 1
-        parts = [(nt, T) for nt in range(last_tile)] + [(last_tile, HALF)]
-        for nt, tokens in parts:
-            blocks = [slice(c, c + P) for c in range(0, tokens, P)]
-            turned = bank(7 if tokens == T else 1)
-            for r in range(TOP):
-                weighted(nt, r, 0, tokens)
-                for c, cols in enumerate(blocks):
-                    nc.tensor.matmul(
-                        out=turned[:, cols],
-                        lhsT=products[nt][r][:, cols],
-                        rhs=ident[:],
-                        start=(r == 0 and c == 0),
-                        stop=(r == TOP - 1 and c == len(blocks) - 1),
-                        is_transpose=True,
-                    )
-            back = bank(nt)
-            summed = ring.tile([P, T], F32)
-            on_scalar(out=summed[:, 0:tokens], in_=turned[:, 0:tokens])
-            for cols in blocks:
-                nc.tensor.transpose(back[:, cols], summed[:, cols], ident[:])
-            result = keep.tile([P, T], F32, name="result%d" % nt)
+        def weighted(target, nt, r, t0, t1):
+            nc.vector.tensor_tensor(out=target, in0=y[nt][:].indirect(slots_of(r, t0, t1)), in1=gates[:, r, t0:t1], op=MULT)
+
+        def turn(acc, source, tokens, start, stop):
+            for c in range(0, tokens, P):
+                nc.tensor.matmul(
+                    out=acc[:, c : c + P],
+                    lhsT=source[:, c : c + P],
+                    rhs=ident[:],
+                    start=start and c == 0,
+                    stop=stop and c + P == tokens,
+                    is_transpose=True,
+                )
+
+        def term(acc, nt, r, tokens):
+            product = row("product%d_%d" % (nt, r))
+            weighted(product[:, 0:tokens], nt, r, 0, tokens)
+            turn(acc, product, tokens, r == 0, r == TOP - 1)
+
+        def turn_back(nt, acc, b, tokens):
+            summed = row("summed%d" % nt)
+            on_scalar(out=summed[:, 0:tokens], in_=acc[:, 0:tokens])
+            back = bank(b)
+            turn(back, summed, tokens, True, True)
+            return back
+
+        def store(nt, back, tokens):
+            result = row("result%d" % nt)
             on_scalar(out=result[:, 0:tokens], in_=back[:, 0:tokens])
             nc.scalar.dma_start(out=out[nt * P : (nt + 1) * P, 0:tokens], in_=result[:, 0:tokens])
 
-        nt = last_tile
-        partial = keep.tile([P, T], F32)
-        last = keep.tile([P, T], F32)
-        quarters = (slice(HALF, HALF + P), slice(HALF + P, T))
+        def fetch(nt, r, b):
+            fetched = row("fetched%d" % r)
+            nc.scalar.activation(out=fetched[:], in_=y[nt][:].indirect(token_slot[r][:]), func=COPY)
+            acc = bank(b)
+            turn(acc, fetched, T, True, True)
+            return acc
+
+        def scale_back(acc, r, back, start, stop):
+            scaled = row("scaled%d" % r)
+            for c in range(T // P):
+                cols = slice(c * P, (c + 1) * P)
+                nc.scalar.activation(out=scaled[:, cols], in_=acc[:, cols], func=COPY, scale=gate_columns[r][:, c : c + 1])
+            turn(back, scaled, T, start, stop)
+            return scaled
+
+        for g in range(E // 2):
+            multiply(1, g)
+        fill(1)
+        fill(2)
+        fetched1 = fetch(1, 1, 2)
+        fetched2 = fetch(1, 2, 3)
+        sum0 = bank(7)
         for r in range(TOP):
-            weighted(nt, r, HALF, T)
+            term(sum0, 0, r, T)
+        direct = row("direct")
+        weighted(direct[:], 1, 0, 0, T)
+        sum2 = bank(1)
+        for r in range(TOP):
+            term(sum2, 2, r, T)
+        fill(3)
+        back1 = bank(0)
+        scale_back(fetched1, 1, back1, True, False)
+        sum3 = bank(6)
+        term(sum3, 3, 0, HALF)
+        sc2 = scale_back(fetched2, 2, back1, False, True)
+        term(sum3, 3, 1, HALF)
+        back0 = turn_back(0, sum0, 2, T)
+        term(sum3, 3, 2, HALF)
+        back2 = turn_back(2, sum2, 3, T)
+        store(0, back0, T)
+        back3 = turn_back(3, sum3, 5, HALF)
+        store(2, back2, T)
+        store(3, back3, HALF)
+
+        late = keep.tile([P, HALF], F32)
+        weighted(late[:], 3, 2, HALF, T)
+        result1 = row("result1")
+        for cols in (slice(0, HALF), slice(HALF, T)):
+            nc.vector.tensor_tensor(out=result1[:, cols], in0=back1[:, cols], in1=direct[:, cols], op=ADD)
+        nc.sync.dma_start(out=out[P : 2 * P, :], in_=result1[:])
+        for r in range(2):
+            weighted(direct[:, r * HALF : (r + 1) * HALF], 3, r, HALF, T)
+        partial = keep.tile([P, HALF], F32)
+        last = keep.tile([P, HALF], F32)
+        quarters = (slice(0, P), slice(P, HALF))
         for cols in quarters:
-            nc.vector.tensor_tensor(out=partial[:, cols], in0=products[nt][0][:, cols], in1=products[nt][1][:, cols], op=ADD)
+            nc.vector.tensor_tensor(out=partial[:, cols], in0=direct[:, cols], in1=late[:, cols], op=ADD)
         for cols in quarters:
-            nc.vector.tensor_tensor(out=last[:, cols], in0=partial[:, cols], in1=products[nt][2][:, cols], op=ADD)
-            nc.sync.dma_start(out=out[nt * P : (nt + 1) * P, cols], in_=last[:, cols])
+            nc.vector.tensor_tensor(out=last[:, cols], in0=partial[:, cols], in1=direct[:, HALF + cols.start : HALF + cols.stop], op=ADD)
+            nc.sync.dma_start(out=out[3 * P : 4 * P, HALF + cols.start : HALF + cols.stop], in_=last[:, cols])

@@ -272,17 +272,15 @@ def tile_moe_sup_glu_sigmoid_kernel(
             empty(step, copy)
 
         filled = {}
+        y_banks = {1: (5, 0, 6), 2: (0, 1, 5), 3: (6, 0, 1)}
 
         def multiply(nt, g):
-            filled[nt, g] = bank(6 - g)
-            for u in range(2):
+            filled[nt, g] = bank(y_banks[nt][g])
+            for u in (1, 0):
                 expert_product(nt, filled[nt, g][:, u * C : (u + 1) * C], (2 * g + u) * C, (2 * g + u + 1) * C)
 
-        def fill(nt):
-            for g in range(E // 2):
-                on_scalar(out=y[nt][:, g * BANK : (g + 1) * BANK], in_=filled[nt, g][:])
-                if nt + 1 < N_TILES:
-                    multiply(nt + 1, g)
+        def fill(nt, g):
+            on_scalar(out=y[nt][:, g * BANK : (g + 1) * BANK], in_=filled[nt, g][:])
 
         def row(name):
             return keep.tile([P, T], F32, name=name)
@@ -308,9 +306,9 @@ def tile_moe_sup_glu_sigmoid_kernel(
             product = row("product%d_%d" % (nt, r))
             weighted(product[:, 0:tokens], nt, r, 0, tokens)
             turn(acc, product, tokens, r == 0, r == TOP - 1)
+            return product
 
-        def turn_back(nt, acc, b, tokens):
-            summed = row("summed%d" % nt)
+        def turn_back(summed, acc, b, tokens):
             on_scalar(out=summed[:, 0:tokens], in_=acc[:, 0:tokens])
             back = bank(b)
             turn(back, summed, tokens, True, True)
@@ -321,8 +319,7 @@ def tile_moe_sup_glu_sigmoid_kernel(
             on_scalar(out=result[:, 0:tokens], in_=back[:, 0:tokens])
             nc.scalar.dma_start(out=out[nt * P : (nt + 1) * P, 0:tokens], in_=result[:, 0:tokens])
 
-        def fetch(nt, r, b):
-            fetched = row("fetched%d" % r)
+        def fetch(fetched, nt, r, b):
             nc.scalar.activation(out=fetched[:], in_=y[nt][:].indirect(token_slot[r][:]), func=COPY)
             acc = bank(b)
             turn(acc, fetched, T, True, True)
@@ -336,43 +333,55 @@ def tile_moe_sup_glu_sigmoid_kernel(
             turn(back, scaled, T, start, stop)
             return scaled
 
-        for g in range(E // 2):
+        for g in (1, 0, 2):
             multiply(1, g)
-        fill(1)
-        fill(2)
-        fetched1 = fetch(1, 1, 2)
-        fetched2 = fetch(1, 2, 3)
+        multiply(2, 1)
+        fill(1, 1)
+        multiply(2, 0)
+        fill(1, 0)
+        multiply(2, 2)
+        fill(1, 2)
+        multiply(3, 0)
+        fill(2, 1)
+        multiply(3, 2)
+        fill(2, 0)
+        multiply(3, 1)
+        fill(2, 2)
+        fetched1 = fetch(row("fetched1"), 1, 1, 2)
         sum0 = bank(7)
         for r in range(TOP):
-            term(sum0, 0, r, T)
+            spent = term(sum0, 0, r, T)
+        back0 = turn_back(row("summed0"), sum0, 4, T)
+        for g in (0, 2, 1):
+            fill(3, g)
+        fetched2 = fetch(spent, 1, 2, 3)
         direct = row("direct")
         weighted(direct[:], 1, 0, 0, T)
-        sum2 = bank(1)
+        sum2 = bank(5)
         for r in range(TOP):
             term(sum2, 2, r, T)
-        fill(3)
-        back1 = bank(0)
+        back1 = bank(7)
         scale_back(fetched1, 1, back1, True, False)
-        sum3 = bank(6)
-        term(sum3, 3, 0, HALF)
         sc2 = scale_back(fetched2, 2, back1, False, True)
-        term(sum3, 3, 1, HALF)
-        back0 = turn_back(0, sum0, 2, T)
-        term(sum3, 3, 2, HALF)
-        back2 = turn_back(2, sum2, 3, T)
+        sum3 = bank(2)
+        for r in range(TOP):
+            term(sum3, 3, r, HALF)
+        back2 = turn_back(row("summed2"), sum2, 3, T)
         store(0, back0, T)
-        back3 = turn_back(3, sum3, 5, HALF)
+        plain = keep.tile([P, HALF], F32)
+        nc.scalar.activation(out=plain[:], in_=y[3][:].indirect(slots_of(2, HALF, T)), func=COPY)
         store(2, back2, T)
+        back3 = turn_back(row("summed3"), sum3, 6, HALF)
         store(3, back3, HALF)
 
         late = keep.tile([P, HALF], F32)
-        weighted(late[:], 3, 2, HALF, T)
+        weighted(late[:], 3, 0, HALF, T)
         result1 = row("result1")
         for cols in (slice(0, HALF), slice(HALF, T)):
             nc.vector.tensor_tensor(out=result1[:, cols], in0=back1[:, cols], in1=direct[:, cols], op=ADD)
         nc.sync.dma_start(out=out[P : 2 * P, :], in_=result1[:])
-        for r in range(2):
-            weighted(direct[:, r * HALF : (r + 1) * HALF], 3, r, HALF, T)
+        weighted(direct[:, 0:HALF], 3, 1, HALF, T)
+        nc.vector.tensor_tensor(out=direct[:, HALF:T], in0=plain[:], in1=gates[:, 2, HALF:T], op=MULT)
         partial = keep.tile([P, HALF], F32)
         last = keep.tile([P, HALF], F32)
         quarters = (slice(0, P), slice(P, HALF))

@@ -314,10 +314,6 @@ def tile_moe_sup_glu_sigmoid_kernel(
             turn(back, summed, tokens, True, True)
             return back
 
-        def store(nt, back, tokens):
-            result = row("result%d" % nt)
-            on_scalar(out=result[:, 0:tokens], in_=back[:, 0:tokens])
-            nc.scalar.dma_start(out=out[nt * P : (nt + 1) * P, 0:tokens], in_=result[:, 0:tokens])
 
         def fetch(fetched, nt, r, b):
             nc.scalar.activation(out=fetched[:], in_=y[nt][:].indirect(token_slot[r][:]), func=COPY)
@@ -361,18 +357,23 @@ def tile_moe_sup_glu_sigmoid_kernel(
         for r in range(TOP):
             term(sum2, 2, r, T)
         back1 = bank(7)
-        scale_back(fetched1, 1, back1, True, False)
+        result0 = scale_back(fetched1, 1, back1, True, False)
         sc2 = scale_back(fetched2, 2, back1, False, True)
         sum3 = bank(2)
         for r in range(TOP):
             term(sum3, 3, r, HALF)
         back2 = turn_back(row("summed2"), sum2, 3, T)
-        store(0, back0, T)
+        on_scalar(out=result0[:], in_=back0[:])
+        nc.sync.dma_start(out=out[0:P, :], in_=result0[:])
         plain = keep.tile([P, HALF], F32)
         nc.scalar.activation(out=plain[:], in_=y[3][:].indirect(slots_of(2, HALF, T)), func=COPY)
-        store(2, back2, T)
         back3 = turn_back(row("summed3"), sum3, 6, HALF)
-        store(3, back3, HALF)
+        result2 = row("result2")
+        result3 = keep.tile([P, HALF], F32)
+        on_scalar(out=result2[:], in_=back2[:])
+        on_scalar(out=result3[:], in_=back3[:, 0:HALF])
+        nc.scalar.dma_start(out=out[2 * P : 3 * P, :], in_=result2[:])
+        nc.scalar.dma_start(out=out[3 * P : 4 * P, 0:HALF], in_=result3[:])
 
         late = keep.tile([P, HALF], F32)
         weighted(late[:], 3, 0, HALF, T)

@@ -30,6 +30,7 @@ LIST_ROWS = 16
 HALF = T // 2
 FIRST_SPLIT = 84
 SECOND_SPLIT = 48
+VECTOR_FROM = 4 * C + C // 2
 
 
 def tile_moe_sup_glu_sigmoid_kernel(
@@ -242,10 +243,9 @@ def tile_moe_sup_glu_sigmoid_kernel(
                 end = min(c + C, s1)
                 expert_product(0, acc[:, c - s0 : end - s0], c, end)
 
-        shared_from = 4 * C + C // 2
-        gather_plane(4 * C, shared_from, 2, T)
+        gather_plane(4 * C, VECTOR_FROM, 2, T)
         gather_plane(0, C, 2, T)
-        gather_plane(4 * C, shared_from, 3)
+        gather_plane(4 * C, VECTOR_FROM, 3)
         gather_plane(C, 2 * C, 2)
         gather_plane(0, 2 * C, 3)
         gather_plane(2 * C, 4 * C, 2)
@@ -253,12 +253,13 @@ def tile_moe_sup_glu_sigmoid_kernel(
 
         steps = [(4 * C, S), (0, 2 * C), (2 * C, 3 * C), (3 * C, 3 * C + C // 2), (3 * C + C // 2, 4 * C)]
         step_banks = [bank(b) for b in (0, 1, 4, 5, 6)]
+
         def empty(step, copy):
             s0, s1 = steps[step]
             copy(out=y[0][:, s0:s1], in_=step_banks[step][:, 0 : s1 - s0])
 
         gather_pairs(4 * C, S, 0)
-        gather_pairs(shared_from, S, 1)
+        gather_pairs(VECTOR_FROM, S, 1)
         gather_pairs(0, 2 * C, 0)
         gather_pairs(2 * C, 4 * C, 0)
         join(4, 6, nc.gpsimd.tensor_copy)
@@ -268,19 +269,30 @@ def tile_moe_sup_glu_sigmoid_kernel(
         join(3, 4, on_scalar)
         for step in range(len(steps)):
             first_products(*steps[step], step_banks[step])
-        for step, copy in ((0, on_scalar), (1, on_scalar), (2, on_scalar), (3, on_vector), (4, on_vector)):
+        for step, copy in enumerate((on_scalar, on_scalar, on_vector, on_vector, on_scalar)):
             empty(step, copy)
 
-        filled = {}
-        y_banks = {1: (5, 0, 6), 2: (0, 1, 5), 3: (6, 0, 1)}
+        groups = [(nt, g) for nt in range(1, N_TILES) for g in (1, 0, 2)]
+        ring = (0, 5, 6, 1)
+        group_banks = {}
 
-        def multiply(nt, g):
-            filled[nt, g] = bank(y_banks[nt][g])
+        def multiply(i):
+            nt, g = groups[i]
+            group_banks[i] = bank(ring[i % len(ring)])
             for u in (1, 0):
-                expert_product(nt, filled[nt, g][:, u * C : (u + 1) * C], (2 * g + u) * C, (2 * g + u + 1) * C)
+                expert_product(nt, group_banks[i][:, u * C : (u + 1) * C], (2 * g + u) * C, (2 * g + u + 1) * C)
 
-        def fill(nt, g):
-            on_scalar(out=y[nt][:, g * BANK : (g + 1) * BANK], in_=filled[nt, g][:])
+        def fill(i):
+            nt, g = groups[i]
+            on_scalar(out=y[nt][:, g * BANK : (g + 1) * BANK], in_=group_banks[i][:])
+
+        early_groups = 2 * (E // 2)
+        for i in range(len(ring)):
+            multiply(i)
+        for i in range(early_groups):
+            fill(i)
+            if i + len(ring) < len(groups):
+                multiply(i + len(ring))
 
         def row(name):
             return keep.tile([P, T], F32, name=name)
@@ -291,7 +303,10 @@ def tile_moe_sup_glu_sigmoid_kernel(
         def weighted(target, nt, r, t0, t1):
             nc.vector.tensor_tensor(out=target, in0=y[nt][:].indirect(slots_of(r, t0, t1)), in1=gates[:, r, t0:t1], op=MULT)
 
-        def turn(acc, source, tokens, start, stop):
+        def plain(target, nt, r, t0, t1):
+            nc.scalar.activation(out=target, in_=y[nt][:].indirect(slots_of(r, t0, t1)), func=COPY)
+
+        def turn(acc, source, tokens, start=True, stop=True):
             for c in range(0, tokens, P):
                 nc.tensor.matmul(
                     out=acc[:, c : c + P],
@@ -302,23 +317,25 @@ def tile_moe_sup_glu_sigmoid_kernel(
                     is_transpose=True,
                 )
 
-        def term(acc, nt, r, tokens):
-            product = row("product%d_%d" % (nt, r))
-            weighted(product[:, 0:tokens], nt, r, 0, tokens)
-            turn(acc, product, tokens, r == 0, r == TOP - 1)
-            return product
+        def turned_sum(nt, b, tokens):
+            acc = bank(b)
+            for r in range(TOP):
+                product = row("product%d_%d" % (nt, r))
+                weighted(product[:, 0:tokens], nt, r, 0, tokens)
+                turn(acc, product, tokens, r == 0, r == TOP - 1)
+            return acc, product
 
-        def turn_back(summed, acc, b, tokens):
+        def turn_back(nt, acc, b, tokens):
+            summed = row("summed%d" % nt)
             on_scalar(out=summed[:, 0:tokens], in_=acc[:, 0:tokens])
             back = bank(b)
-            turn(back, summed, tokens, True, True)
+            turn(back, summed, tokens)
             return back
 
-
-        def fetch(fetched, nt, r, b):
-            nc.scalar.activation(out=fetched[:], in_=y[nt][:].indirect(token_slot[r][:]), func=COPY)
+        def turned_plain(target, r, b):
+            plain(target[:], 1, r, 0, T)
             acc = bank(b)
-            turn(acc, fetched, T, True, True)
+            turn(acc, target, T)
             return acc
 
         def scale_back(acc, r, back, start, stop):
@@ -329,45 +346,25 @@ def tile_moe_sup_glu_sigmoid_kernel(
             turn(back, scaled, T, start, stop)
             return scaled
 
-        for g in (1, 0, 2):
-            multiply(1, g)
-        multiply(2, 1)
-        fill(1, 1)
-        multiply(2, 0)
-        fill(1, 0)
-        multiply(2, 2)
-        fill(1, 2)
-        multiply(3, 0)
-        fill(2, 1)
-        multiply(3, 2)
-        fill(2, 0)
-        multiply(3, 1)
-        fill(2, 2)
-        fetched1 = fetch(row("fetched1"), 1, 1, 2)
-        sum0 = bank(7)
-        for r in range(TOP):
-            spent = term(sum0, 0, r, T)
-        back0 = turn_back(row("summed0"), sum0, 4, T)
-        for g in (0, 2, 1):
-            fill(3, g)
-        fetched2 = fetch(spent, 1, 2, 3)
+        turned1 = turned_plain(row("plain1"), 1, 2)
+        sum0, spent_product = turned_sum(0, 7, T)
+        back0 = turn_back(0, sum0, 4, T)
+        for i in range(early_groups, len(groups)):
+            fill(i)
+        turned2 = turned_plain(spent_product, 2, 3)
         direct = row("direct")
         weighted(direct[:], 1, 0, 0, T)
-        sum2 = bank(5)
-        for r in range(TOP):
-            term(sum2, 2, r, T)
+        sum2 = turned_sum(2, 5, T)[0]
         back1 = bank(7)
-        result0 = scale_back(fetched1, 1, back1, True, False)
-        sc2 = scale_back(fetched2, 2, back1, False, True)
-        sum3 = bank(2)
-        for r in range(TOP):
-            term(sum3, 3, r, HALF)
-        back2 = turn_back(row("summed2"), sum2, 3, T)
+        result0 = scale_back(turned1, 1, back1, True, False)
+        scale_back(turned2, 2, back1, False, True)
+        sum3 = turned_sum(3, 2, HALF)[0]
+        back2 = turn_back(2, sum2, 3, T)
         on_scalar(out=result0[:], in_=back0[:])
         nc.sync.dma_start(out=out[0:P, :], in_=result0[:])
-        plain = keep.tile([P, HALF], F32)
-        nc.scalar.activation(out=plain[:], in_=y[3][:].indirect(slots_of(2, HALF, T)), func=COPY)
-        back3 = turn_back(row("summed3"), sum3, 6, HALF)
+        late_plain = keep.tile([P, HALF], F32)
+        plain(late_plain[:], 3, 2, HALF, T)
+        back3 = turn_back(3, sum3, 6, HALF)
         result2 = row("result2")
         result3 = keep.tile([P, HALF], F32)
         on_scalar(out=result2[:], in_=back2[:])
@@ -375,19 +372,20 @@ def tile_moe_sup_glu_sigmoid_kernel(
         nc.scalar.dma_start(out=out[2 * P : 3 * P, :], in_=result2[:])
         nc.scalar.dma_start(out=out[3 * P : 4 * P, 0:HALF], in_=result3[:])
 
-        late = keep.tile([P, HALF], F32)
-        weighted(late[:], 3, 0, HALF, T)
+        late_first = keep.tile([P, HALF], F32)
+        weighted(late_first[:], 3, 0, HALF, T)
         result1 = row("result1")
         for cols in (slice(0, HALF), slice(HALF, T)):
             nc.vector.tensor_tensor(out=result1[:, cols], in0=back1[:, cols], in1=direct[:, cols], op=ADD)
         nc.sync.dma_start(out=out[P : 2 * P, :], in_=result1[:])
-        weighted(direct[:, 0:HALF], 3, 1, HALF, T)
-        nc.vector.tensor_tensor(out=direct[:, HALF:T], in0=plain[:], in1=gates[:, 2, HALF:T], op=MULT)
+        late_second, late_third = direct[:, 0:HALF], direct[:, HALF:T]
+        weighted(late_second, 3, 1, HALF, T)
+        nc.vector.tensor_tensor(out=late_third, in0=late_plain[:], in1=gates[:, 2, HALF:T], op=MULT)
         partial = keep.tile([P, HALF], F32)
         last = keep.tile([P, HALF], F32)
         quarters = (slice(0, P), slice(P, HALF))
         for cols in quarters:
-            nc.vector.tensor_tensor(out=partial[:, cols], in0=direct[:, cols], in1=late[:, cols], op=ADD)
+            nc.vector.tensor_tensor(out=partial[:, cols], in0=late_second[:, cols], in1=late_first[:, cols], op=ADD)
         for cols in quarters:
-            nc.vector.tensor_tensor(out=last[:, cols], in0=partial[:, cols], in1=direct[:, HALF + cols.start : HALF + cols.stop], op=ADD)
+            nc.vector.tensor_tensor(out=last[:, cols], in0=partial[:, cols], in1=late_third[:, cols], op=ADD)
             nc.sync.dma_start(out=out[3 * P : 4 * P, HALF + cols.start : HALF + cols.stop], in_=last[:, cols])

@@ -30,7 +30,6 @@ LIST_ROWS = 16
 HALF = T // 2
 FIRST_SPLIT = 84
 SECOND_SPLIT = 48
-VECTOR_FROM = 4 * C + C // 2
 
 
 def tile_moe_sup_glu_sigmoid_kernel(
@@ -180,8 +179,10 @@ def tile_moe_sup_glu_sigmoid_kernel(
 
         h = keep.tile([P, 6 * T + HALF], BF16)
         nc.vector.memset(h[:, 6 * T :], 0.0)
-        for t in (2, 3):
-            nc.vector.tensor_tensor(out=h[:, (t + 2) * T : (t + 3) * T], in0=plane_sums[t][:], in1=sig[:, t, :], op=MULT)
+        nc.vector.tensor_tensor(out=h[:, 4 * T : 5 * T], in0=plane_sums[2][:], in1=sig[:, 2, :], op=MULT)
+        plane3 = keep.tile([P, T], F32)
+        on_scalar(out=plane3[:], in_=plane_sums[3][:])
+        nc.gpsimd.tensor_tensor(out=h[:, 5 * T : 6 * T], in0=plane3[:], in1=sig[:, 3, :], op=MULT)
         nc.gpsimd.tensor_copy(
             out=h[:, 0 : 2 * T].rearrange("p (t e) -> p t e", e=2),
             in_=h[:, 4 * T : 6 * T].rearrange("p (e t) -> p t e", e=2),
@@ -196,196 +197,212 @@ def tile_moe_sup_glu_sigmoid_kernel(
             )
         pair_window = [h[:, 2 * T : 5 * T].bitcast(U32), h[:, 0 : 3 * T].bitcast(U32)]
 
-        picked = [keep.tile([P, 2, 2 * C], U32, name="picked%d" % g) for g in range(E // 2)]
-        joined = keep.tile([P, S, 2], U32, align_bytes=64)
+        steps = [(0, C, C), (C, 5 * P, 3 * C), (3 * C, 9 * P, 5 * C), (5 * C, 5 * C, S)]
+        y = [keep.tile([P, S], F32, name="y%d" % nt, align_bytes=64) for nt in range(N_TILES)]
+        even = keep.tile([P, 8 * C], U32)
+        odd = keep.tile([P, 4 * C], U32, align_bytes=64)
+        joined_odd = keep.tile([P, 4 * C], U32, align_bytes=64)
+        joined = [y[2][:, C : 5 * C].bitcast(U32), joined_odd[:]]
         h_codes = keep.tile([P, S], U32, align_bytes=64)
         h_scales = keep.tile([P, S], U8, align_bytes=64)
-        y = [keep.tile([P, S], F32, name="y%d" % nt) for nt in range(N_TILES)]
+        staged = [(even, 2 * C), (odd, 2 * C), (even, 4 * C)]
 
         def tokens_of(s0, s1):
             return slot_token[:, s0 // LIST_ROWS : s1 // LIST_ROWS]
 
-        def gather_plane(s0, s1, t, columns=T + HALF):
-            first = 2 * (s0 % (2 * C))
+        def gather_plane(step, t, columns=T + HALF):
+            s0, s1 = steps[step][0:2]
+            tile, far = staged[step]
             nc.scalar.activation(
-                out=picked[s0 // (2 * C)][:, 1, :].bitcast(BF16)[:, first + t - 2 : first + 2 * (s1 - s0) : 2],
+                out=tile[:, far : far + s1 - s0].bitcast(BF16)[:, t - 2 : 2 * (s1 - s0) : 2],
                 in_=h[:, (t + 2) * T : (t + 2) * T + columns].indirect(tokens_of(s0, s1)),
                 func=COPY,
             )
 
-        def gather_pairs(s0, s1, u):
-            first = s0 % (2 * C)
-            on_vector(out=picked[s0 // (2 * C)][:, u, first : first + s1 - s0], in_=pair_window[u].indirect(tokens_of(s0, s1)))
+        def gather_pairs(target, s0, s1, u):
+            on_vector(out=target, in_=pair_window[u].indirect(tokens_of(s0, s1)))
 
-        def join(e0, e1, copy):
-            pairs = picked[e0 // 2][:].rearrange("p u c -> p c u")
-            copy(out=joined[:, e0 * C : e1 * C], in_=pairs[:, (e0 % 2) * C : (e0 % 2 + e1 - e0) * C])
+        def gather(step):
+            s0, mid, s1 = steps[step]
+            if step == len(staged):
+                for u in range(2):
+                    gather_pairs(odd[:, u : 2 * (s1 - s0) : 2], s0, s1, u)
+            else:
+                tile, far = staged[step]
+                gather_pairs(tile[:, 0 : s1 - s0], s0, s1, 0)
+                if mid < s1:
+                    gather_pairs(tile[:, far + mid - s0 : far + s1 - s0], mid, s1, 1)
 
-        def expert_product(nt, acc, s0, s1):
-            e = s0 // C
-            nc.tensor.matmul_mx(
-                out=acc,
-                lhsT=w2_codes[:, e, 2 * nt * P : 2 * (nt + 1) * P].bitcast(FP4X4),
-                lhsT_scale=w2_bytes[:, e, nt * P : (nt + 1) * P],
-                rhs=h_codes[:, s0:s1].bitcast(FP8X4),
-                rhs_scale=h_scales[:, s0:s1],
-                start=True,
-                stop=True,
+        def join(step, c0=0, c1=None):
+            c1 = c1 or steps[step][2] - steps[step][0]
+            tile, far = staged[step]
+            nc.gpsimd.tensor_copy(
+                out=joined[step % 2][:, 2 * c0 : 2 * c1].rearrange("p (c u) -> p c u", u=2),
+                in_=tile[:, 0 : 2 * far].rearrange("p (u c) -> p c u", u=2)[:, c0:c1],
             )
 
-        def first_products(s0, s1, acc):
+        def quantise(step, s0, s1):
+            words = odd[:] if step == len(staged) else joined[step % 2]
+            first = steps[step][0]
             nc.vector.quantize_mx(
                 out=h_codes[:, s0:s1].bitcast(FP8X4),
                 scales=h_scales[:, s0:s1],
-                in_=joined[:, s0:s1].rearrange("p c u -> p (c u)").bitcast(BF16),
+                in_=words[:, 2 * (s0 - first) : 2 * (s1 - first)].bitcast(BF16),
             )
-            for c in range(s0, s1, C):
-                end = min(c + C, s1)
-                expert_product(0, acc[:, c - s0 : end - s0], c, end)
 
-        gather_plane(4 * C, VECTOR_FROM, 2, T)
-        gather_plane(0, C, 2, T)
-        gather_plane(4 * C, VECTOR_FROM, 3)
-        gather_plane(C, 2 * C, 2)
-        gather_plane(0, 2 * C, 3)
-        gather_plane(2 * C, 4 * C, 2)
-        gather_plane(2 * C, 4 * C, 3)
+        def multiply(nt, s0, s1, b):
+            acc = bank(b)
+            cuts = [s0] + list(range((s0 // C + 1) * C, s1, C)) + [s1]
+            for c0, c1 in zip(cuts, cuts[1:]):
+                nc.tensor.matmul_mx(
+                    out=acc[:, c0 - s0 : c1 - s0],
+                    lhsT=w2_codes[:, c0 // C, 2 * nt * P : 2 * (nt + 1) * P].bitcast(FP4X4),
+                    lhsT_scale=w2_bytes[:, c0 // C, nt * P : (nt + 1) * P],
+                    rhs=h_codes[:, c0:c1].bitcast(FP8X4),
+                    rhs_scale=h_scales[:, c0:c1],
+                    start=True,
+                    stop=True,
+                )
+            return lambda copy: copy(out=y[nt][:, s0:s1], in_=acc[:, 0 : s1 - s0])
 
-        steps = [(4 * C, S), (0, 2 * C), (2 * C, 3 * C), (3 * C, 3 * C + C // 2), (3 * C + C // 2, 4 * C)]
-        step_banks = [bank(b) for b in (0, 1, 4, 5, 6)]
+        gather_plane(0, 2, T)
+        gather_plane(0, 3)
+        gather_plane(1, 2, T)
+        gather_plane(1, 3)
+        for t in (2, 3):
+            gather_plane(2, t)
 
-        def empty(step, copy):
-            s0, s1 = steps[step]
-            copy(out=y[0][:, s0:s1], in_=step_banks[step][:, 0 : s1 - s0])
+        gather(0)
+        join(0)
+        gather(1)
+        quantise(0, 0, C)
+        join(1)
+        for nt in range(N_TILES):
+            multiply(nt, 0, C, nt)(on_scalar)
+        gather(2)
+        quantise(1, C, 3 * C)
+        join(2, 0, C)
+        join(2, C, 2 * C)
+        for nt in range(2):
+            multiply(nt, C, 3 * C, 4 + nt)(on_scalar)
+        waiting = [multiply(2, C, 3 * C, 6)]
+        gather(3)
+        for b, (step, s0, s1) in enumerate(((2, 3 * C, 4 * C), (3, 5 * C, S), (2, 4 * C, 9 * P), (2, 9 * P, 5 * C))):
+            quantise(step, s0, s1)
+            multiply(0, s0, s1, b)(on_scalar)
+            if b == 0:
+                waiting.append(multiply(1, s0, s1, 7))
+        for empty in waiting:
+            empty(on_vector)
+        multiply(1, 4 * C, S, 4)(on_scalar)
+        rest2 = [multiply(2, 3 * C, 5 * C, 5), multiply(2, 5 * C, S, 0)]
+        rest3 = [multiply(3, C, 3 * C, 1), multiply(3, 3 * C, 5 * C, 2), multiply(3, 5 * C, S, 3)]
 
-        gather_pairs(4 * C, S, 0)
-        gather_pairs(VECTOR_FROM, S, 1)
-        gather_pairs(0, 2 * C, 0)
-        gather_pairs(2 * C, 4 * C, 0)
-        join(4, 6, nc.gpsimd.tensor_copy)
-        join(0, 1, nc.gpsimd.tensor_copy)
-        join(1, 2, on_scalar)
-        join(2, 3, on_scalar)
-        join(3, 4, on_scalar)
-        for step in range(len(steps)):
-            first_products(*steps[step], step_banks[step])
-        for step, copy in enumerate((on_scalar, on_scalar, on_vector, on_vector, on_scalar)):
-            empty(step, copy)
-
-        groups = [(nt, g) for nt in range(1, N_TILES) for g in (1, 0, 2)]
-        ring = (0, 5, 6, 1)
-        group_banks = {}
-
-        def multiply(i):
-            nt, g = groups[i]
-            group_banks[i] = bank(ring[i % len(ring)])
-            for u in (1, 0):
-                expert_product(nt, group_banks[i][:, u * C : (u + 1) * C], (2 * g + u) * C, (2 * g + u + 1) * C)
-
-        def fill(i):
-            nt, g = groups[i]
-            on_scalar(out=y[nt][:, g * BANK : (g + 1) * BANK], in_=group_banks[i][:])
-
-        early_groups = 2 * (E // 2)
-        for i in range(len(ring)):
-            multiply(i)
-        for i in range(early_groups):
-            fill(i)
-            if i + len(ring) < len(groups):
-                multiply(i + len(ring))
-
-        def row(name):
-            return keep.tile([P, T], F32, name=name)
+        def row(name, columns=T):
+            return keep.tile([P, columns], F32, name=name)
 
         def slots_of(r, t0, t1):
             return token_slot[r][:, t0 // LIST_ROWS : t1 // LIST_ROWS]
 
-        def weighted(target, nt, r, t0, t1):
+        def weighted(target, nt, r, t0=0, t1=T):
             nc.vector.tensor_tensor(out=target, in0=y[nt][:].indirect(slots_of(r, t0, t1)), in1=gates[:, r, t0:t1], op=MULT)
 
-        def plain(target, nt, r, t0, t1):
+        def plain(target, nt, r, t0=0, t1=T):
             nc.scalar.activation(out=target, in_=y[nt][:].indirect(slots_of(r, t0, t1)), func=COPY)
 
-        def turn(acc, source, tokens, start=True, stop=True):
-            for c in range(0, tokens, P):
+        def turn(acc, source, c0, c1, start=True, stop=True):
+            for c in range(c0, c1):
                 nc.tensor.matmul(
-                    out=acc[:, c : c + P],
-                    lhsT=source[:, c : c + P],
+                    out=acc[:, (c - c0) * P : (c - c0 + 1) * P],
+                    lhsT=source[:, c * P : (c + 1) * P],
                     rhs=ident[:],
-                    start=start and c == 0,
-                    stop=stop and c + P == tokens,
+                    start=start and c == c0,
+                    stop=stop and c + 1 == c1,
                     is_transpose=True,
                 )
 
-        def turned_sum(nt, b, tokens):
-            acc = bank(b)
-            for r in range(TOP):
-                product = row("product%d_%d" % (nt, r))
-                weighted(product[:, 0:tokens], nt, r, 0, tokens)
-                turn(acc, product, tokens, r == 0, r == TOP - 1)
-            return acc, product
-
-        def turn_back(nt, acc, b, tokens):
-            summed = row("summed%d" % nt)
-            on_scalar(out=summed[:, 0:tokens], in_=acc[:, 0:tokens])
-            back = bank(b)
-            turn(back, summed, tokens)
-            return back
-
-        def turned_plain(target, r, b):
-            plain(target[:], 1, r, 0, T)
-            acc = bank(b)
-            turn(acc, target, T)
-            return acc
-
-        def scale_back(acc, r, back, start, stop):
-            scaled = row("scaled%d" % r)
-            for c in range(T // P):
+        def scale(target, acc, r, c0, c1):
+            for c in range(c0, c1):
                 cols = slice(c * P, (c + 1) * P)
-                nc.scalar.activation(out=scaled[:, cols], in_=acc[:, cols], func=COPY, scale=gate_columns[r][:, c : c + 1])
-            turn(back, scaled, T, start, stop)
-            return scaled
+                nc.scalar.activation(out=target[:, cols], in_=acc[:, cols], func=COPY, scale=gate_columns[r][:, c : c + 1])
 
-        turned1 = turned_plain(row("plain1"), 1, 2)
-        sum0, spent_product = turned_sum(0, 7, T)
-        back0 = turn_back(0, sum0, 4, T)
-        for i in range(early_groups, len(groups)):
-            fill(i)
-        turned2 = turned_plain(spent_product, 2, 3)
-        direct = row("direct")
-        weighted(direct[:], 1, 0, 0, T)
-        sum2 = turned_sum(2, 5, T)[0]
-        back1 = bank(7)
-        result0 = scale_back(turned1, 1, back1, True, False)
-        scale_back(turned2, 2, back1, False, True)
-        sum3 = turned_sum(3, 2, HALF)[0]
-        back2 = turn_back(2, sum2, 3, T)
+        def add(target, a, b):
+            nc.vector.tensor_tensor(out=target, in0=a, in1=b, op=ADD)
+
+        product = [row("product%d" % r) for r in range(TOP)]
+        summed0 = row("summed0")
+        picked = {(1, 1): row("picked1"), (1, 2): row("picked2"), (2, 1): product[2], (2, 2): summed0}
+        scaled = {(nt, r): row("scaled%d_%d" % (nt, r)) for nt in (1, 2) for r in (1, 2)}
+        direct = {nt: row("direct%d" % nt) for nt in (1, 2)}
+        turned = {}
+
+        def turned_plain(nt, r, b):
+            plain(picked[nt, r][:], nt, r)
+            turned[nt, r] = bank(b)
+            turn(turned[nt, r], picked[nt, r], 0, 4)
+
+        sum0 = bank(6)
+        weighted(product[0][:], 0, 0)
+        turn(sum0, product[0], 0, 4, True, False)
+        turned_plain(1, 1, 7)
+        for empty in rest2:
+            empty(on_scalar)
+        weighted(product[1][:], 0, 1)
+        turn(sum0, product[1], 0, 4, False, False)
+        turned_plain(1, 2, 4)
+        for empty in rest3:
+            empty(on_scalar)
+        weighted(product[2][:], 0, 2)
+        turn(sum0, product[2], 0, 4, False, True)
+        scale(scaled[1, 1], turned[1, 1], 1, 0, 4)
+        back1 = bank(5)
+        turn(back1, scaled[1, 1], 0, 4, True, False)
+        weighted(direct[1][:], 1, 0)
+        on_scalar(out=summed0[:], in_=sum0[:])
+        back0 = bank(0)
+        turn(back0, summed0, 0, 4)
+        weighted(direct[2][:], 2, 0)
+        turned_plain(2, 1, 1)
+        scale(scaled[1, 2], turned[1, 2], 2, 0, 4)
+        turn(back1, scaled[1, 2], 0, 4, False, True)
+        sum3 = bank(6)
+        early = [row("early%d" % r, HALF) for r in range(TOP)]
+        for r in range(TOP):
+            weighted(early[r][:], 3, r, 0, HALF)
+            turn(sum3, early[r], 0, 2, r == 0, r == TOP - 1)
+        result0 = row("result0")
         on_scalar(out=result0[:], in_=back0[:])
         nc.sync.dma_start(out=out[0:P, :], in_=result0[:])
-        late_plain = keep.tile([P, HALF], F32)
-        plain(late_plain[:], 3, 2, HALF, T)
-        back3 = turn_back(3, sum3, 6, HALF)
-        result2 = row("result2")
-        result3 = keep.tile([P, HALF], F32)
-        on_scalar(out=result2[:], in_=back2[:])
-        on_scalar(out=result3[:], in_=back3[:, 0:HALF])
-        nc.scalar.dma_start(out=out[2 * P : 3 * P, :], in_=result2[:])
-        nc.scalar.dma_start(out=out[3 * P : 4 * P, 0:HALF], in_=result3[:])
-
-        late_first = keep.tile([P, HALF], F32)
-        weighted(late_first[:], 3, 0, HALF, T)
+        turned_plain(2, 2, 7)
         result1 = row("result1")
-        for cols in (slice(0, HALF), slice(HALF, T)):
-            nc.vector.tensor_tensor(out=result1[:, cols], in0=back1[:, cols], in1=direct[:, cols], op=ADD)
+        add(result1[:], back1[:], direct[1][:])
         nc.sync.dma_start(out=out[P : 2 * P, :], in_=result1[:])
-        late_second, late_third = direct[:, 0:HALF], direct[:, HALF:T]
-        weighted(late_second, 3, 1, HALF, T)
-        nc.vector.tensor_tensor(out=late_third, in0=late_plain[:], in1=gates[:, 2, HALF:T], op=MULT)
-        partial = keep.tile([P, HALF], F32)
-        last = keep.tile([P, HALF], F32)
+        late = [direct[1][:, 0:HALF], direct[1][:, HALF:T], row("late2", HALF)[:]]
+        for r in range(TOP):
+            weighted(late[r], 3, r, HALF, T)
+        scale(scaled[2, 1], turned[2, 1], 1, 0, 4)
+        back2 = [bank(2), bank(4)]
+        result2 = row("result2")
+        partial = row("partial", HALF)
+        last = direct[2][:, HALF:T]
+        for half in range(2):
+            turn(back2[half], scaled[2, 1], 2 * half, 2 * half + 2, True, False)
+        for half in range(2):
+            scale(scaled[2, 2], turned[2, 2], 2, 2 * half, 2 * half + 2)
+            turn(back2[half], scaled[2, 2], 2 * half, 2 * half + 2, False, True)
+        summed3 = row("summed3", HALF)
+        on_scalar(out=summed3[:], in_=sum3[:, 0:HALF])
+        back3 = bank(3)
+        turn(back3, summed3, 0, 2)
+        result3 = row("result3", HALF)
+        on_scalar(out=result3[:], in_=back3[:, 0:HALF])
+        nc.scalar.dma_start(out=out[3 * P : 4 * P, 0:HALF], in_=result3[:])
         quarters = (slice(0, P), slice(P, HALF))
+        add(partial[:], late[0], late[1])
+        for half in range(2):
+            cols = slice(half * HALF, (half + 1) * HALF)
+            add(result2[:, cols], back2[half][:, 0:HALF], direct[2][:, cols])
+            nc.sync.dma_start(out=out[2 * P : 3 * P, cols], in_=result2[:, cols])
         for cols in quarters:
-            nc.vector.tensor_tensor(out=partial[:, cols], in0=late_second[:, cols], in1=late_first[:, cols], op=ADD)
-        for cols in quarters:
-            nc.vector.tensor_tensor(out=last[:, cols], in0=partial[:, cols], in1=late_third[:, cols], op=ADD)
+            add(last[:, cols], partial[:, cols], late[2][:, cols])
             nc.sync.dma_start(out=out[3 * P : 4 * P, HALF + cols.start : HALF + cols.stop], in_=last[:, cols])

@@ -333,7 +333,9 @@ def tile_moe_sup_glu_sigmoid_kernel(
         summed0 = row("summed0")
         picked = {(1, 1): row("picked1"), (1, 2): row("picked2"), (2, 1): product[2], (2, 2): summed0}
         scaled = {(nt, r): row("scaled%d_%d" % (nt, r)) for nt in (1, 2) for r in (1, 2)}
-        direct = {nt: row("direct%d" % nt) for nt in (1, 2)}
+        late_row = row("late")
+        direct_row = row("direct", T + HALF)
+        direct = {1: direct_row[:, 0:T], 2: direct_row[:, HALF : HALF + T]}
         turned = {}
 
         def turned_plain(nt, r, b):
@@ -345,64 +347,63 @@ def tile_moe_sup_glu_sigmoid_kernel(
         weighted(product[0][:], 0, 0)
         turn(sum0, product[0], 0, 4, True, False)
         turned_plain(1, 1, 7)
-        for empty in rest2:
+        for empty in rest3:
             empty(on_scalar)
         weighted(product[1][:], 0, 1)
         turn(sum0, product[1], 0, 4, False, False)
         turned_plain(1, 2, 4)
-        for empty in rest3:
+        for empty in rest2:
             empty(on_scalar)
         weighted(product[2][:], 0, 2)
         turn(sum0, product[2], 0, 4, False, True)
         scale(scaled[1, 1], turned[1, 1], 1, 0, 4)
         back1 = bank(5)
         turn(back1, scaled[1, 1], 0, 4, True, False)
-        weighted(direct[1][:], 1, 0)
+        scale(scaled[1, 2], turned[1, 2], 2, 0, 4)
+        turn(back1, scaled[1, 2], 0, 4, False, True)
+        weighted(direct[1], 1, 0)
         on_scalar(out=summed0[:], in_=sum0[:])
         back0 = bank(0)
         turn(back0, summed0, 0, 4)
-        weighted(direct[2][:], 2, 0)
         turned_plain(2, 1, 1)
-        scale(scaled[1, 2], turned[1, 2], 2, 0, 4)
-        turn(back1, scaled[1, 2], 0, 4, False, True)
         sum3 = bank(6)
-        early = [row("early%d" % r, HALF) for r in range(TOP)]
+        early_row = row("early", TOP * HALF)
+        early = [early_row[:, r * HALF : (r + 1) * HALF] for r in range(TOP)]
         for r in range(TOP):
-            weighted(early[r][:], 3, r, 0, HALF)
+            weighted(early[r], 3, r, 0, HALF)
             turn(sum3, early[r], 0, 2, r == 0, r == TOP - 1)
-        result0 = row("result0")
-        on_scalar(out=result0[:], in_=back0[:])
-        nc.sync.dma_start(out=out[0:P, :], in_=result0[:])
+        summed3 = row("summed3", HALF)
+        on_scalar(out=summed3[:], in_=sum3[:, 0:HALF])
+        back3 = bank(3)
+        turn(back3, summed3, 0, 2)
         turned_plain(2, 2, 7)
-        result1 = row("result1")
-        add(result1[:], back1[:], direct[1][:])
-        nc.sync.dma_start(out=out[P : 2 * P, :], in_=result1[:])
-        late = [direct[1][:, 0:HALF], direct[1][:, HALF:T], row("late2", HALF)[:]]
-        for r in range(TOP):
+        result3 = row("result3", HALF)
+        on_scalar(out=result3[:], in_=back3[:, 0:HALF])
+        result0 = row("result0")
+        on_vector(out=result0[:], in_=back0[:])
+        nc.sync.dma_start(out=out[0:P, :], in_=result0[:])
+        late = [late_row[:, 0:HALF], late_row[:, HALF:T], direct[1][:, 0:HALF]]
+        for r in range(2):
             weighted(late[r], 3, r, HALF, T)
+        partial = row("partial", HALF)
+        nc.gpsimd.tensor_tensor(out=partial[:], in0=late[0], in1=late[1], op=ADD)
+        result1 = row("result1")
+        add(result1[:], back1[:], direct[1])
+        nc.sync.dma_start(out=out[P : 2 * P, :], in_=result1[:])
+        nc.sync.dma_start(out=out[3 * P : 4 * P, 0:HALF], in_=result3[:])
+        weighted(late[2], 3, 2, HALF, T)
+        last = row("last", HALF)
+        nc.gpsimd.tensor_tensor(out=last[:], in0=partial[:], in1=late[2], op=ADD)
+        nc.sync.dma_start(out=out[3 * P : 4 * P, HALF:T], in_=last[:])
+        weighted(direct[2], 2, 0)
         scale(scaled[2, 1], turned[2, 1], 1, 0, 4)
         back2 = [bank(2), bank(4)]
         result2 = row("result2")
-        partial = row("partial", HALF)
-        last = direct[2][:, HALF:T]
         for half in range(2):
             turn(back2[half], scaled[2, 1], 2 * half, 2 * half + 2, True, False)
         for half in range(2):
             scale(scaled[2, 2], turned[2, 2], 2, 2 * half, 2 * half + 2)
             turn(back2[half], scaled[2, 2], 2 * half, 2 * half + 2, False, True)
-        summed3 = row("summed3", HALF)
-        on_scalar(out=summed3[:], in_=sum3[:, 0:HALF])
-        back3 = bank(3)
-        turn(back3, summed3, 0, 2)
-        result3 = row("result3", HALF)
-        on_scalar(out=result3[:], in_=back3[:, 0:HALF])
-        nc.scalar.dma_start(out=out[3 * P : 4 * P, 0:HALF], in_=result3[:])
-        quarters = (slice(0, P), slice(P, HALF))
-        add(partial[:], late[0], late[1])
-        for half in range(2):
-            cols = slice(half * HALF, (half + 1) * HALF)
-            add(result2[:, cols], back2[half][:, 0:HALF], direct[2][:, cols])
-            nc.sync.dma_start(out=out[2 * P : 3 * P, cols], in_=result2[:, cols])
-        for cols in quarters:
-            add(last[:, cols], partial[:, cols], late[2][:, cols])
-            nc.sync.dma_start(out=out[3 * P : 4 * P, HALF + cols.start : HALF + cols.stop], in_=last[:, cols])
+        for c0, c1 in ((0, HALF), (HALF, 3 * P), (3 * P, T)):
+            add(result2[:, c0:c1], back2[c0 // HALF][:, c0 % HALF : c0 % HALF + c1 - c0], direct[2][:, c0:c1])
+            nc.sync.dma_start(out=out[2 * P : 3 * P, c0:c1], in_=result2[:, c0:c1])

@@ -48,7 +48,8 @@ def tile_moe_sup_glu_sigmoid_kernel(
         x_bytes = keep.tile([P, T], U8, align_bytes=64)
         w2_codes = keep.tile([P, E, 2 * N], U8, align_bytes=64)
         w2_bytes = keep.tile([P, E, N], U8, align_bytes=64)
-        gates = keep.tile([P, TOP, T], F32)
+        closing = keep.tile([P, 1 + TOP, T], F32)
+        gates = closing[:, 1:]
         slot_token = keep.tile([P, S // LIST_ROWS], U16)
         token_slot = [keep.tile([P, T // LIST_ROWS], U16, name="token_slot%d" % r) for r in range(TOP)]
         ident = keep.tile([P, P], F32)
@@ -94,7 +95,7 @@ def tile_moe_sup_glu_sigmoid_kernel(
         )
         for r, pos in enumerate((pos1, pos2, pos3)):
             nc.sync.dma_start(token_slot[r][:], pos)
-        nc.sync.dma_start(out=gates[:], in_=gate.rearrange("r p t -> p r t"))
+        nc.sync.dma_start(out=gates, in_=gate.rearrange("r p t -> p r t"))
         gate_columns = {}
         with nc.allow_non_contiguous_dma(reason="one weight a partition"):
             for r in (1, 2):
@@ -366,7 +367,7 @@ def tile_moe_sup_glu_sigmoid_kernel(
         back0 = bank(0)
         turn(back0, summed0, 0, 4)
         turned_plain(2, 1, 1)
-        sum3 = bank(6)
+        sum3 = bank(7)
         early_row = row("early", TOP * HALF)
         early = [early_row[:, r * HALF : (r + 1) * HALF] for r in range(TOP)]
         for r in range(TOP):
@@ -376,7 +377,7 @@ def tile_moe_sup_glu_sigmoid_kernel(
         on_scalar(out=summed3[:], in_=sum3[:, 0:HALF])
         back3 = bank(3)
         turn(back3, summed3, 0, 2)
-        turned_plain(2, 2, 7)
+        turned_plain(2, 2, 6)
         result3 = row("result3", HALF)
         on_scalar(out=result3[:], in_=back3[:, 0:HALF])
         result0 = row("result0")
@@ -392,18 +393,19 @@ def tile_moe_sup_glu_sigmoid_kernel(
         nc.sync.dma_start(out=out[P : 2 * P, :], in_=result1[:])
         nc.sync.dma_start(out=out[3 * P : 4 * P, 0:HALF], in_=result3[:])
         weighted(late[2], 3, 2, HALF, T)
-        last = row("last", HALF)
-        nc.gpsimd.tensor_tensor(out=last[:], in0=partial[:], in1=late[2], op=ADD)
-        nc.sync.dma_start(out=out[3 * P : 4 * P, HALF:T], in_=last[:])
         weighted(direct[2], 2, 0)
         scale(scaled[2, 1], turned[2, 1], 1, 0, 4)
         back2 = [bank(2), bank(4)]
-        result2 = row("result2")
         for half in range(2):
             turn(back2[half], scaled[2, 1], 2 * half, 2 * half + 2, True, False)
         for half in range(2):
             scale(scaled[2, 2], turned[2, 2], 2, 2 * half, 2 * half + 2)
             turn(back2[half], scaled[2, 2], 2 * half, 2 * half + 2, False, True)
-        for c0, c1 in ((0, HALF), (HALF, 3 * P), (3 * P, T)):
-            add(result2[:, c0:c1], back2[c0 // HALF][:, c0 % HALF : c0 % HALF + c1 - c0], direct[2][:, c0:c1])
-            nc.sync.dma_start(out=out[2 * P : 3 * P, c0:c1], in_=result2[:, c0:c1])
+        add(closing[:, 0, 0:HALF], back2[0][:, 0:HALF], direct[2][:, 0:HALF])
+        nc.sync.dma_start(out=out[2 * P : 3 * P, 0:HALF], in_=closing[:, 0, 0:HALF])
+        both = out[2 * P : 4 * P, :].rearrange("(b p) t -> p b t", p=P)
+        for c0 in (0, P):
+            part, cols = slice(c0, c0 + P), slice(HALF + c0, HALF + c0 + P)
+            nc.gpsimd.tensor_tensor(out=closing[:, 1, cols], in0=partial[:, part], in1=late[2][:, part], op=ADD)
+            add(closing[:, 0, cols], back2[1][:, part], direct[2][:, cols])
+            nc.sync.dma_start(out=both[:, :, cols], in_=closing[:, 0:2, cols])

@@ -332,8 +332,8 @@ def tile_moe_sup_glu_sigmoid_kernel(
 
         product = [row("product%d" % r) for r in range(TOP)]
         summed0 = row("summed0")
-        picked = {(1, 1): row("picked1"), (1, 2): row("picked2"), (2, 1): product[2], (2, 2): summed0}
         scaled = {(nt, r): row("scaled%d_%d" % (nt, r)) for nt in (1, 2) for r in (1, 2)}
+        picked = {(1, 1): row("picked1"), (1, 2): row("picked2"), (2, 1): product[2], (2, 2): scaled[1, 2]}
         late_row = row("late")
         direct_row = row("direct", T + HALF)
         direct = {1: direct_row[:, 0:T], 2: direct_row[:, HALF : HALF + T]}
@@ -353,19 +353,19 @@ def tile_moe_sup_glu_sigmoid_kernel(
         weighted(product[1][:], 0, 1)
         turn(sum0, product[1], 0, 4, False, False)
         turned_plain(1, 2, 4)
-        for empty in rest2:
-            empty(on_scalar)
         weighted(product[2][:], 0, 2)
         turn(sum0, product[2], 0, 4, False, True)
+        on_scalar(out=summed0[:], in_=sum0[:])
+        back0 = bank(2)
+        turn(back0, summed0, 0, 4)
+        for empty in rest2:
+            empty(on_scalar)
         scale(scaled[1, 1], turned[1, 1], 1, 0, 4)
         back1 = bank(5)
         turn(back1, scaled[1, 1], 0, 4, True, False)
         scale(scaled[1, 2], turned[1, 2], 2, 0, 4)
         turn(back1, scaled[1, 2], 0, 4, False, True)
         weighted(direct[1], 1, 0)
-        on_scalar(out=summed0[:], in_=sum0[:])
-        back0 = bank(0)
-        turn(back0, summed0, 0, 4)
         turned_plain(2, 1, 1)
         sum3 = bank(7)
         early_row = row("early", TOP * HALF)
@@ -389,23 +389,25 @@ def tile_moe_sup_glu_sigmoid_kernel(
         partial = row("partial", HALF)
         nc.gpsimd.tensor_tensor(out=partial[:], in0=late[0], in1=late[1], op=ADD)
         result1 = row("result1")
-        add(result1[:], back1[:], direct[1])
+        for cols in (slice(0, HALF), slice(HALF, T)):
+            add(result1[:, cols], back1[:, cols], direct[1][:, cols])
         nc.sync.dma_start(out=out[P : 2 * P, :], in_=result1[:])
         nc.sync.dma_start(out=out[3 * P : 4 * P, 0:HALF], in_=result3[:])
         weighted(late[2], 3, 2, HALF, T)
         weighted(direct[2], 2, 0)
         scale(scaled[2, 1], turned[2, 1], 1, 0, 4)
-        back2 = [bank(2), bank(4)]
-        for half in range(2):
-            turn(back2[half], scaled[2, 1], 2 * half, 2 * half + 2, True, False)
-        for half in range(2):
-            scale(scaled[2, 2], turned[2, 2], 2, 2 * half, 2 * half + 2)
-            turn(back2[half], scaled[2, 2], 2 * half, 2 * half + 2, False, True)
+        pieces = ((0, 2), (2, 3), (3, 4))
+        back2 = [bank(0), bank(4), bank(5)]
+        for acc, (c0, c1) in zip(back2, pieces):
+            turn(acc, scaled[2, 1], c0, c1, True, False)
+        for acc, (c0, c1) in zip(back2, pieces):
+            scale(scaled[2, 2], turned[2, 2], 2, c0, c1)
+            turn(acc, scaled[2, 2], c0, c1, False, True)
         add(closing[:, 0, 0:HALF], back2[0][:, 0:HALF], direct[2][:, 0:HALF])
         nc.sync.dma_start(out=out[2 * P : 3 * P, 0:HALF], in_=closing[:, 0, 0:HALF])
         both = out[2 * P : 4 * P, :].rearrange("(b p) t -> p b t", p=P)
         for c0 in (0, P):
             part, cols = slice(c0, c0 + P), slice(HALF + c0, HALF + c0 + P)
             nc.gpsimd.tensor_tensor(out=closing[:, 1, cols], in0=partial[:, part], in1=late[2][:, part], op=ADD)
-            add(closing[:, 0, cols], back2[1][:, part], direct[2][:, cols])
+            add(closing[:, 0, cols], back2[1 + c0 // P][:, 0:P], direct[2][:, cols])
             nc.sync.dma_start(out=both[:, :, cols], in_=closing[:, 0:2, cols])

@@ -333,10 +333,10 @@ def tile_moe_sup_glu_sigmoid_kernel(
         product = [row("product%d" % r) for r in range(TOP)]
         summed0 = row("summed0")
         scaled = {(nt, r): row("scaled%d_%d" % (nt, r)) for nt in (1, 2) for r in (1, 2)}
-        picked = {(1, 1): row("picked1"), (1, 2): row("picked2"), (2, 1): product[2], (2, 2): scaled[1, 2]}
+        picked = {(1, 1): row("picked1"), (1, 2): row("picked2"), (2, 1): product[2], (2, 2): scaled[1, 1]}
         late_row = row("late")
         direct_row = row("direct", T + HALF)
-        direct = {1: direct_row[:, 0:T], 2: direct_row[:, HALF : HALF + T]}
+        direct = {1: direct_row[:, HALF : HALF + T], 2: direct_row[:, 0:T]}
         turned = {}
 
         def turned_plain(nt, r, b):
@@ -367,24 +367,24 @@ def tile_moe_sup_glu_sigmoid_kernel(
         turn(back1, scaled[1, 2], 0, 4, False, True)
         weighted(direct[1], 1, 0)
         turned_plain(2, 1, 1)
-        sum3 = bank(7)
+        sum3 = bank(4)
         early_row = row("early", TOP * HALF)
         early = [early_row[:, r * HALF : (r + 1) * HALF] for r in range(TOP)]
         for r in range(TOP):
             weighted(early[r], 3, r, 0, HALF)
             turn(sum3, early[r], 0, 2, r == 0, r == TOP - 1)
+        turned_plain(2, 2, 6)
         summed3 = row("summed3", HALF)
         on_scalar(out=summed3[:], in_=sum3[:, 0:HALF])
         back3 = bank(3)
         turn(back3, summed3, 0, 2)
-        turned_plain(2, 2, 6)
-        result3 = row("result3", HALF)
-        on_scalar(out=result3[:], in_=back3[:, 0:HALF])
+        result3 = row("result3", 3 * P)
+        on_scalar(out=result3[:, 0:HALF], in_=back3[:, 0:HALF])
         result0 = row("result0")
         on_vector(out=result0[:], in_=back0[:])
         nc.sync.dma_start(out=out[0:P, :], in_=result0[:])
-        late = [late_row[:, 0:HALF], late_row[:, HALF:T], direct[1][:, 0:HALF]]
-        for r in range(2):
+        late = [late_row[:, 0:HALF], late_row[:, HALF:T], row("late2", HALF)[:]]
+        for r in range(TOP):
             weighted(late[r], 3, r, HALF, T)
         partial = row("partial", HALF)
         nc.gpsimd.tensor_tensor(out=partial[:], in0=late[0], in1=late[1], op=ADD)
@@ -392,12 +392,12 @@ def tile_moe_sup_glu_sigmoid_kernel(
         for cols in (slice(0, HALF), slice(HALF, T)):
             add(result1[:, cols], back1[:, cols], direct[1][:, cols])
         nc.sync.dma_start(out=out[P : 2 * P, :], in_=result1[:])
-        nc.sync.dma_start(out=out[3 * P : 4 * P, 0:HALF], in_=result3[:])
-        weighted(late[2], 3, 2, HALF, T)
+        nc.gpsimd.tensor_tensor(out=result3[:, HALF : 3 * P], in0=partial[:, 0:P], in1=late[2][:, 0:P], op=ADD)
+        nc.sync.dma_start(out=out[3 * P : 4 * P, 0 : 3 * P], in_=result3[:])
         weighted(direct[2], 2, 0)
         scale(scaled[2, 1], turned[2, 1], 1, 0, 4)
-        pieces = ((0, 2), (2, 3), (3, 4))
-        back2 = [bank(0), bank(4), bank(5)]
+        pieces = ((0, 2), (3, 4), (2, 3))
+        back2 = [bank(0), bank(7), bank(5)]
         for acc, (c0, c1) in zip(back2, pieces):
             turn(acc, scaled[2, 1], c0, c1, True, False)
         for acc, (c0, c1) in zip(back2, pieces):
@@ -406,8 +406,8 @@ def tile_moe_sup_glu_sigmoid_kernel(
         add(closing[:, 0, 0:HALF], back2[0][:, 0:HALF], direct[2][:, 0:HALF])
         nc.sync.dma_start(out=out[2 * P : 3 * P, 0:HALF], in_=closing[:, 0, 0:HALF])
         both = out[2 * P : 4 * P, :].rearrange("(b p) t -> p b t", p=P)
-        for c0 in (0, P):
-            part, cols = slice(c0, c0 + P), slice(HALF + c0, HALF + c0 + P)
-            nc.gpsimd.tensor_tensor(out=closing[:, 1, cols], in0=partial[:, part], in1=late[2][:, part], op=ADD)
-            add(closing[:, 0, cols], back2[1 + c0 // P][:, 0:P], direct[2][:, cols])
-            nc.sync.dma_start(out=both[:, :, cols], in_=closing[:, 0:2, cols])
+        nc.gpsimd.tensor_tensor(out=closing[:, 1, 3 * P : T], in0=partial[:, P:HALF], in1=late[2][:, P:HALF], op=ADD)
+        add(closing[:, 0, 3 * P : T], back2[1][:, 0:P], direct[2][:, 3 * P : T])
+        nc.sync.dma_start(out=both[:, :, 3 * P : T], in_=closing[:, 0:2, 3 * P : T])
+        add(closing[:, 0, HALF : 3 * P], back2[2][:, 0:P], direct[2][:, HALF : 3 * P])
+        nc.sync.dma_start(out=out[2 * P : 3 * P, HALF : 3 * P], in_=closing[:, 0, HALF : 3 * P])

@@ -29,7 +29,9 @@ BANK = 512
 LIST_ROWS = 16
 HALF = T // 2
 FIRST_SPLIT = 84
-SECOND_SPLIT = 48
+SECOND_SPLIT = 64
+STEPS = ((0, C, C), (C, 5 * P, 3 * C), (3 * C, 9 * P, 5 * C), (5 * C, 5 * C, S))
+LAST_STEP = len(STEPS) - 1
 
 
 def tile_moe_sup_glu_sigmoid_kernel(
@@ -173,13 +175,12 @@ def tile_moe_sup_glu_sigmoid_kernel(
         regroup(on_scalar, "w3", 1, 2, 4, FIRST_SPLIT, P)
         regroup(on_scalar, "w3", 1, 0, 2, SECOND_SPLIT, P)
         quantise_w("w3", 1, 2, 4)
-        for t in (2, 3):
+        for t in (3, 2):
             plane_pass(plane_sums[t], "w3", 1, t)
         regroup(on_vector, "w3", 1, 0, 2, 0, SECOND_SPLIT)
         quantise_w("w3", 1, 0, 2)
 
-        h = keep.tile([P, 6 * T + HALF], BF16)
-        nc.vector.memset(h[:, 6 * T :], 0.0)
+        h = keep.tile([P, 6 * T], BF16)
         nc.vector.tensor_tensor(out=h[:, 4 * T : 5 * T], in0=plane_sums[2][:], in1=sig[:, 2, :], op=MULT)
         plane3 = keep.tile([P, T], F32)
         on_scalar(out=plane3[:], in_=plane_sums[3][:])
@@ -198,7 +199,6 @@ def tile_moe_sup_glu_sigmoid_kernel(
             )
         pair_window = [h[:, 2 * T : 5 * T].bitcast(U32), h[:, 0 : 3 * T].bitcast(U32)]
 
-        steps = [(0, C, C), (C, 5 * P, 3 * C), (3 * C, 9 * P, 5 * C), (5 * C, 5 * C, S)]
         y = [keep.tile([P, S], F32, name="y%d" % nt, align_bytes=64) for nt in range(N_TILES)]
         even = keep.tile([P, 8 * C], U32)
         odd = keep.tile([P, 4 * C], U32, align_bytes=64)
@@ -211,8 +211,8 @@ def tile_moe_sup_glu_sigmoid_kernel(
         def tokens_of(s0, s1):
             return slot_token[:, s0 // LIST_ROWS : s1 // LIST_ROWS]
 
-        def gather_plane(step, t, columns=T + HALF):
-            s0, s1 = steps[step][0:2]
+        def gather_plane(step, t, columns=T):
+            s0, s1 = STEPS[step][0:2]
             tile, far = staged[step]
             nc.scalar.activation(
                 out=tile[:, far : far + s1 - s0].bitcast(BF16)[:, t - 2 : 2 * (s1 - s0) : 2],
@@ -224,8 +224,8 @@ def tile_moe_sup_glu_sigmoid_kernel(
             on_vector(out=target, in_=pair_window[u].indirect(tokens_of(s0, s1)))
 
         def gather(step):
-            s0, mid, s1 = steps[step]
-            if step == len(staged):
+            s0, mid, s1 = STEPS[step]
+            if step == LAST_STEP:
                 for u in range(2):
                     gather_pairs(odd[:, u : 2 * (s1 - s0) : 2], s0, s1, u)
             else:
@@ -234,8 +234,7 @@ def tile_moe_sup_glu_sigmoid_kernel(
                 if mid < s1:
                     gather_pairs(tile[:, far + mid - s0 : far + s1 - s0], mid, s1, 1)
 
-        def join(step, c0=0, c1=None):
-            c1 = c1 or steps[step][2] - steps[step][0]
+        def join(step, c0, c1):
             tile, far = staged[step]
             nc.gpsimd.tensor_copy(
                 out=joined[step % 2][:, 2 * c0 : 2 * c1].rearrange("p (c u) -> p c u", u=2),
@@ -243,8 +242,8 @@ def tile_moe_sup_glu_sigmoid_kernel(
             )
 
         def quantise(step, s0, s1):
-            words = odd[:] if step == len(staged) else joined[step % 2]
-            first = steps[step][0]
+            words = odd[:] if step == LAST_STEP else joined[step % 2]
+            first = STEPS[step][0]
             nc.vector.quantize_mx(
                 out=h_codes[:, s0:s1].bitcast(FP8X4),
                 scales=h_scales[:, s0:s1],
@@ -266,18 +265,15 @@ def tile_moe_sup_glu_sigmoid_kernel(
                 )
             return lambda copy: copy(out=y[nt][:, s0:s1], in_=acc[:, 0 : s1 - s0])
 
-        gather_plane(0, 2, T)
-        gather_plane(0, 3)
-        gather_plane(1, 2, T)
-        gather_plane(1, 3)
-        for t in (2, 3):
-            gather_plane(2, t)
+        for step in range(LAST_STEP):
+            gather_plane(step, 2, T if step < 2 else T + HALF)
+            gather_plane(step, 3)
 
         gather(0)
-        join(0)
+        join(0, 0, C)
         gather(1)
         quantise(0, 0, C)
-        join(1)
+        join(1, 0, 2 * C)
         for nt in range(N_TILES):
             multiply(nt, 0, C, nt)(on_scalar)
         gather(2)
@@ -286,14 +282,19 @@ def tile_moe_sup_glu_sigmoid_kernel(
         join(2, C, 2 * C)
         for nt in range(2):
             multiply(nt, C, 3 * C, 4 + nt)(on_scalar)
-        waiting = [multiply(2, C, 3 * C, 6)]
-        gather(3)
-        for b, (step, s0, s1) in enumerate(((2, 3 * C, 4 * C), (3, 5 * C, S), (2, 4 * C, 9 * P), (2, 9 * P, 5 * C))):
+        for_vector = [multiply(2, C, 3 * C, 6)]
+        gather(LAST_STEP)
+
+        def first_tile(step, s0, s1, b):
             quantise(step, s0, s1)
             multiply(0, s0, s1, b)(on_scalar)
-            if b == 0:
-                waiting.append(multiply(1, s0, s1, 7))
-        for empty in waiting:
+
+        first_tile(2, 3 * C, 4 * C, 0)
+        for_vector.append(multiply(1, 3 * C, 4 * C, 7))
+        first_tile(LAST_STEP, 5 * C, S, 1)
+        first_tile(2, 4 * C, 4 * C + P, 2)
+        first_tile(2, 4 * C + P, 5 * C, 3)
+        for empty in for_vector:
             empty(on_vector)
         multiply(1, 4 * C, S, 4)(on_scalar)
         rest2 = [multiply(2, 3 * C, 5 * C, 5), multiply(2, 5 * C, S, 0)]
@@ -308,8 +309,8 @@ def tile_moe_sup_glu_sigmoid_kernel(
         def weighted(target, nt, r, t0=0, t1=T):
             nc.vector.tensor_tensor(out=target, in0=y[nt][:].indirect(slots_of(r, t0, t1)), in1=gates[:, r, t0:t1], op=MULT)
 
-        def plain(target, nt, r, t0=0, t1=T):
-            nc.scalar.activation(out=target, in_=y[nt][:].indirect(slots_of(r, t0, t1)), func=COPY)
+        def plain(target, nt, r):
+            nc.scalar.activation(out=target, in_=y[nt][:].indirect(slots_of(r, 0, T)), func=COPY)
 
         def turn(acc, source, c0, c1, start=True, stop=True):
             for c in range(c0, c1):
@@ -327,8 +328,8 @@ def tile_moe_sup_glu_sigmoid_kernel(
                 cols = slice(c * P, (c + 1) * P)
                 nc.scalar.activation(out=target[:, cols], in_=acc[:, cols], func=COPY, scale=gate_columns[r][:, c : c + 1])
 
-        def add(target, a, b):
-            nc.vector.tensor_tensor(out=target, in0=a, in1=b, op=ADD)
+        def add(engine, target, a, b):
+            engine.tensor_tensor(out=target, in0=a, in1=b, op=ADD)
 
         product = [row("product%d" % r) for r in range(TOP)]
         summed0 = row("summed0")
@@ -338,48 +339,51 @@ def tile_moe_sup_glu_sigmoid_kernel(
         direct_row = row("direct", T + HALF)
         direct = {1: direct_row[:, HALF : HALF + T], 2: direct_row[:, 0:T]}
         turned = {}
+        blocks = T // P
 
         def turned_plain(nt, r, b):
             plain(picked[nt, r][:], nt, r)
             turned[nt, r] = bank(b)
-            turn(turned[nt, r], picked[nt, r], 0, 4)
+            turn(turned[nt, r], picked[nt, r], 0, blocks)
 
         sum0 = bank(6)
         weighted(product[0][:], 0, 0)
-        turn(sum0, product[0], 0, 4, True, False)
+        turn(sum0, product[0], 0, blocks, True, False)
         turned_plain(1, 1, 7)
         for empty in rest3:
             empty(on_scalar)
         weighted(product[1][:], 0, 1)
-        turn(sum0, product[1], 0, 4, False, False)
+        turn(sum0, product[1], 0, blocks, False, False)
         turned_plain(1, 2, 4)
         weighted(product[2][:], 0, 2)
-        turn(sum0, product[2], 0, 4, False, True)
+        turn(sum0, product[2], 0, blocks, False, True)
         on_scalar(out=summed0[:], in_=sum0[:])
         back0 = bank(2)
-        turn(back0, summed0, 0, 4)
+        turn(back0, summed0, 0, blocks)
         for empty in rest2:
             empty(on_scalar)
-        scale(scaled[1, 1], turned[1, 1], 1, 0, 4)
+        scale(scaled[1, 1], turned[1, 1], 1, 0, blocks)
         back1 = bank(5)
-        turn(back1, scaled[1, 1], 0, 4, True, False)
-        scale(scaled[1, 2], turned[1, 2], 2, 0, 4)
-        turn(back1, scaled[1, 2], 0, 4, False, True)
+        turn(back1, scaled[1, 1], 0, blocks, True, False)
+        scale(scaled[1, 2], turned[1, 2], 2, 0, blocks)
+        turn(back1, scaled[1, 2], 0, blocks, False, True)
         weighted(direct[1], 1, 0)
         turned_plain(2, 1, 1)
+
         sum3 = bank(4)
         early_row = row("early", TOP * HALF)
-        early = [early_row[:, r * HALF : (r + 1) * HALF] for r in range(TOP)]
         for r in range(TOP):
-            weighted(early[r], 3, r, 0, HALF)
-            turn(sum3, early[r], 0, 2, r == 0, r == TOP - 1)
+            early = early_row[:, r * HALF : (r + 1) * HALF]
+            weighted(early, 3, r, 0, HALF)
+            turn(sum3, early, 0, HALF // P, r == 0, r == TOP - 1)
         turned_plain(2, 2, 6)
         summed3 = row("summed3", HALF)
         on_scalar(out=summed3[:], in_=sum3[:, 0:HALF])
         back3 = bank(3)
-        turn(back3, summed3, 0, 2)
+        turn(back3, summed3, 0, HALF // P)
         result3 = row("result3", 3 * P)
         on_scalar(out=result3[:, 0:HALF], in_=back3[:, 0:HALF])
+
         result0 = row("result0")
         on_vector(out=result0[:], in_=back0[:])
         nc.sync.dma_start(out=out[0:P, :], in_=result0[:])
@@ -387,15 +391,16 @@ def tile_moe_sup_glu_sigmoid_kernel(
         for r in range(TOP):
             weighted(late[r], 3, r, HALF, T)
         partial = row("partial", HALF)
-        nc.gpsimd.tensor_tensor(out=partial[:], in0=late[0], in1=late[1], op=ADD)
+        add(nc.gpsimd, partial[:], late[0], late[1])
         result1 = row("result1")
         for cols in (slice(0, HALF), slice(HALF, T)):
-            add(result1[:, cols], back1[:, cols], direct[1][:, cols])
+            add(nc.vector, result1[:, cols], back1[:, cols], direct[1][:, cols])
         nc.sync.dma_start(out=out[P : 2 * P, :], in_=result1[:])
-        nc.gpsimd.tensor_tensor(out=result3[:, HALF : 3 * P], in0=partial[:, 0:P], in1=late[2][:, 0:P], op=ADD)
+        add(nc.gpsimd, result3[:, HALF : 3 * P], partial[:, 0:P], late[2][:, 0:P])
         nc.sync.dma_start(out=out[3 * P : 4 * P, 0 : 3 * P], in_=result3[:])
+
         weighted(direct[2], 2, 0)
-        scale(scaled[2, 1], turned[2, 1], 1, 0, 4)
+        scale(scaled[2, 1], turned[2, 1], 1, 0, blocks)
         pieces = ((0, 2), (3, 4), (2, 3))
         back2 = [bank(0), bank(7), bank(5)]
         for acc, (c0, c1) in zip(back2, pieces):
@@ -403,11 +408,12 @@ def tile_moe_sup_glu_sigmoid_kernel(
         for acc, (c0, c1) in zip(back2, pieces):
             scale(scaled[2, 2], turned[2, 2], 2, c0, c1)
             turn(acc, scaled[2, 2], c0, c1, False, True)
-        add(closing[:, 0, 0:HALF], back2[0][:, 0:HALF], direct[2][:, 0:HALF])
-        nc.sync.dma_start(out=out[2 * P : 3 * P, 0:HALF], in_=closing[:, 0, 0:HALF])
-        both = out[2 * P : 4 * P, :].rearrange("(b p) t -> p b t", p=P)
-        nc.gpsimd.tensor_tensor(out=closing[:, 1, 3 * P : T], in0=partial[:, P:HALF], in1=late[2][:, P:HALF], op=ADD)
-        add(closing[:, 0, 3 * P : T], back2[1][:, 0:P], direct[2][:, 3 * P : T])
-        nc.sync.dma_start(out=both[:, :, 3 * P : T], in_=closing[:, 0:2, 3 * P : T])
-        add(closing[:, 0, HALF : 3 * P], back2[2][:, 0:P], direct[2][:, HALF : 3 * P])
-        nc.sync.dma_start(out=out[2 * P : 3 * P, HALF : 3 * P], in_=closing[:, 0, HALF : 3 * P])
+        first_half, third, fourth = slice(0, HALF), slice(HALF, 3 * P), slice(3 * P, T)
+        add(nc.vector, closing[:, 0, first_half], back2[0][:, 0:HALF], direct[2][:, first_half])
+        nc.sync.dma_start(out=out[2 * P : 3 * P, first_half], in_=closing[:, 0, first_half])
+        both_tiles = out[2 * P : 4 * P, :].rearrange("(b p) t -> p b t", p=P)
+        add(nc.gpsimd, closing[:, 1, fourth], partial[:, P:HALF], late[2][:, P:HALF])
+        add(nc.vector, closing[:, 0, fourth], back2[1][:, 0:P], direct[2][:, fourth])
+        nc.sync.dma_start(out=both_tiles[:, :, fourth], in_=closing[:, 0:2, fourth])
+        add(nc.vector, closing[:, 0, third], back2[2][:, 0:P], direct[2][:, third])
+        nc.sync.dma_start(out=out[2 * P : 3 * P, third], in_=closing[:, 0, third])

from contextlib import ExitStack

import concourse.mybir as mybir
from concourse.masks import make_identity

K, T, E, C, H, N, TOP = 1024, 512, 6, 256, 512, 512, 3
S = E * C
FLOPS = 2 * (2 * K * H * T + H * N * S)

F32 = mybir.dt.float32
BF16 = mybir.dt.bfloat16
I32 = mybir.dt.int32
U32 = mybir.dt.uint32
U16 = mybir.dt.uint16
U8 = mybir.dt.uint8
FP8X4 = mybir.dt.float8_e4m3fn_x4
FP4X4 = mybir.dt.float4_e2m1fn_x4
MULT = mybir.AluOpType.mult
ADD = mybir.AluOpType.add
SIGMOID = mybir.ActivationFunctionType.Sigmoid
COPY = mybir.ActivationFunctionType.Copy

P = 128
PACK = 4
K_PASS = P * PACK
PASSES = K // K_PASS
N_TILES = N // P
BANK = 512
LIST_ROWS = 16
HALF = T // 2
FIRST_SPLIT = 84
SECOND_SPLIT = 64
STEPS = ((0, C, C), (C, 5 * P, 3 * C), (3 * C, 9 * P, 5 * C), (5 * C, 5 * C, S))
LAST_STEP = len(STEPS) - 1


def tile_moe_sup_glu_sigmoid_kernel(
    tc, x_words, x_scales, w1, w3, w2_words, w2_scales, gate, offs, pos1, pos2, pos3, out
):
    nc = tc.nc
    on_vector, on_scalar = nc.vector.tensor_copy, nc.scalar.copy
    with ExitStack() as ctx:
        keep = ctx.enter_context(tc.tile_pool(name="keep", bufs=1))
        psum = ctx.enter_context(tc.psum_pool(name="psum", bufs=1))

        def bank(b):
            return psum.tile([P, BANK], F32, name="bank%d" % b)

        x_codes = keep.tile([P, PASSES, T], U32, align_bytes=64)
        x_bytes = keep.tile([P, T], U8, align_bytes=64)
        w2_codes = keep.tile([P, E, 2 * N], U8, align_bytes=64)
        w2_bytes = keep.tile([P, E, N], U8, align_bytes=64)
        closing = keep.tile([P, 1 + TOP, T], F32)
        gates = closing[:, 1:]
        slot_token = keep.tile([P, S // LIST_ROWS], U16)
        token_slot = [keep.tile([P, T // LIST_ROWS], U16, name="token_slot%d" % r) for r in range(TOP)]
        ident = keep.tile([P, P], F32)

        nc.vector.memset(x_bytes[:].bitcast(I32), 0)
        nc.vector.memset(w2_bytes[:].rearrange("p e n -> p (e n)").bitcast(I32), 0)
        make_identity(nc, ident[:])

        raw = {}

        def load_w(name, w, s):
            raw[name, s] = keep.tile([P, PACK, H], F32, name="raw_%s%d" % (name, s))
            rows = w[s * K_PASS : (s + 1) * K_PASS, :].rearrange("(p j) c -> p j c", j=PACK)
            nc.sync.dma_start(out=raw[name, s][:], in_=rows)

        def load_x(s):
            nc.sync.dma_start(
                out=x_codes[:, s, :].bitcast(I32),
                in_=x_words[s].rearrange("p t d -> p (t d)").bitcast(I32),
            )

        load_w("w1", w1, 0)
        for q in range(4):
            nc.sync.dma_start(
                out=x_bytes[32 * q : 32 * q + 4 * PASSES, :].bitcast(I32),
                in_=x_scales[:, 4 * q : 4 * q + 4, :].bitcast(I32),
            )
        load_x(0)
        load_w("w1", w1, 1)
        load_x(1)
        load_w("w3", w3, 0)
        load_w("w3", w3, 1)
        nc.sync.dma_start(slot_token[:], offs)
        w2_rows = w2_scales.rearrange("e s b n -> (e s) b n")
        for r in range(4):
            nc.sync.dma_start(
                out=w2_bytes[r:P:32, :, :].bitcast(I32),
                in_=w2_rows[:, r:16:4, :].rearrange("e q n -> q e n").bitcast(I32),
            )
        nc.sync.dma_start(
            out=w2_codes[:].bitcast(I32),
            in_=w2_words.rearrange("e s p b -> p (e s) b").bitcast(I32),
        )
        for r, pos in enumerate((pos1, pos2, pos3)):
            nc.sync.dma_start(token_slot[r][:], pos)
        nc.sync.dma_start(out=gates, in_=gate.rearrange("r p t -> p r t"))
        gate_columns = {}
        with nc.allow_non_contiguous_dma(reason="one weight a partition"):
            for r in (1, 2):
                gate_columns[r] = keep.tile([P, T // P], F32, name="gate_column%d" % r)
                nc.sync.dma_start(out=gate_columns[r][:], in_=gate[r, 0, :].rearrange("(c p) -> p c", p=P))

        codes, scales, grouped = {}, {}, {}
        for name in ("w1", "w3"):
            for s in range(PASSES):
                codes[name, s] = keep.tile([P, H], U32, name="codes_%s%d" % (name, s), align_bytes=64)
                scales[name, s] = keep.tile([P, H], U8, name="scales_%s%d" % (name, s), align_bytes=64)

        def regroup(copy, name, s, t0, t1, m0=0, m1=P):
            if (name, s, t0) not in grouped:
                grouped[name, s, t0] = keep.tile(
                    [P, t1 - t0, P, PACK], BF16, name="grouped_%s%d_%d" % (name, s, t0), align_bytes=64
                )
            source = raw[name, s][:].rearrange("p j (m t) -> p m j t", t=PACK)
            target = grouped[name, s, t0][:].rearrange("p t m j -> p m j t")
            copy(out=target[:, m0:m1], in_=source[:, m0:m1, :, t0:t1])

        def quantise_w(name, s, t0, t1):
            nc.vector.quantize_mx(
                out=codes[name, s][:, t0 * P : t1 * P].bitcast(FP8X4),
                scales=scales[name, s][:, t0 * P : t1 * P],
                in_=grouped[name, s, t0][:].rearrange("p t m j -> p (t m j)"),
            )

        def shared_product(acc, name, s, t, tokens, start, stop):
            nc.tensor.matmul_mx(
                out=acc,
                lhsT=codes[name, s][:, t * P : (t + 1) * P].bitcast(FP8X4),
                lhsT_scale=scales[name, s][:, t * P : (t + 1) * P],
                rhs=x_codes[:, s, tokens].bitcast(FP8X4),
                rhs_scale=x_bytes[4 * s : P, tokens],
                start=start,
                stop=stop,
            )

        def plane_pass(acc, name, s, t):
            shared_product(acc[:], name, s, t, slice(0, T), s == 0, s == PASSES - 1)

        def pair_pass(acc, s, half):
            tokens = slice(half * HALF, (half + 1) * HALF)
            for t in range(2):
                start, stop = s == 0 and t == 0, s == PASSES - 1 and t == 1
                shared_product(acc[:, t * HALF : (t + 1) * HALF], "w3", s, t, tokens, start, stop)

        gate_sums = [bank(t) for t in range(PACK)]
        regroup(on_vector, "w1", 0, 0, PACK)
        quantise_w("w1", 0, 0, PACK)
        for t in range(PACK):
            plane_pass(gate_sums[t], "w1", 0, t)
        for t0 in (2, 0):
            regroup(on_vector, "w1", 1, t0, t0 + 2)
            quantise_w("w1", 1, t0, t0 + 2)
            for t in (t0, t0 + 1):
                plane_pass(gate_sums[t], "w1", 1, t)
        sig = keep.tile([P, PACK, T], F32)
        for t in (2, 3, 0, 1):
            nc.scalar.activation(out=sig[:, t, :], in_=gate_sums[t][:], func=SIGMOID)

        plane_sums = {2: bank(4), 3: bank(5)}
        pair_sums = [bank(6), bank(7)]
        regroup(on_vector, "w3", 0, 2, 4)
        quantise_w("w3", 0, 2, 4)
        for t in (2, 3):
            plane_pass(plane_sums[t], "w3", 0, t)
        regroup(on_vector, "w3", 0, 0, 2)
        quantise_w("w3", 0, 0, 2)
        for half in range(2):
            pair_pass(pair_sums[half], 0, half)

        regroup(on_vector, "w3", 1, 2, 4, 0, FIRST_SPLIT)
        regroup(on_scalar, "w3", 1, 2, 4, FIRST_SPLIT, P)
        regroup(on_scalar, "w3", 1, 0, 2, SECOND_SPLIT, P)
        quantise_w("w3", 1, 2, 4)
        for t in (3, 2):
            plane_pass(plane_sums[t], "w3", 1, t)
        regroup(on_vector, "w3", 1, 0, 2, 0, SECOND_SPLIT)
        quantise_w("w3", 1, 0, 2)

        h = keep.tile([P, 6 * T], BF16)
        nc.vector.tensor_tensor(out=h[:, 4 * T : 5 * T], in0=plane_sums[2][:], in1=sig[:, 2, :], op=MULT)
        plane3 = keep.tile([P, T], F32)
        on_scalar(out=plane3[:], in_=plane_sums[3][:])
        nc.gpsimd.tensor_tensor(out=h[:, 5 * T : 6 * T], in0=plane3[:], in1=sig[:, 3, :], op=MULT)
        nc.gpsimd.tensor_copy(
            out=h[:, 0 : 2 * T].rearrange("p (t e) -> p t e", e=2),
            in_=h[:, 4 * T : 6 * T].rearrange("p (e t) -> p t e", e=2),
        )
        for half in range(2):
            pair_pass(pair_sums[half], 1, half)
            nc.vector.tensor_tensor(
                out=h[:, (half + 2) * T : (half + 3) * T].rearrange("p (t e) -> p t e", e=2),
                in0=pair_sums[half][:].rearrange("p (e t) -> p t e", e=2),
                in1=sig[:, 0:2, half * HALF : (half + 1) * HALF].rearrange("p e t -> p t e"),
                op=MULT,
            )
        pair_window = [h[:, 2 * T : 5 * T].bitcast(U32), h[:, 0 : 3 * T].bitcast(U32)]

        y = [keep.tile([P, S], F32, name="y%d" % nt, align_bytes=64) for nt in range(N_TILES)]
        even = keep.tile([P, 8 * C], U32)
        odd = keep.tile([P, 4 * C], U32, align_bytes=64)
        joined_odd = keep.tile([P, 4 * C], U32, align_bytes=64)
        joined = [y[2][:, C : 5 * C].bitcast(U32), joined_odd[:]]
        h_codes = keep.tile([P, S], U32, align_bytes=64)
        h_scales = keep.tile([P, S], U8, align_bytes=64)
        staged = [(even, 2 * C), (odd, 2 * C), (even, 4 * C)]

        def tokens_of(s0, s1):
            return slot_token[:, s0 // LIST_ROWS : s1 // LIST_ROWS]

        def gather_plane(step, t, columns=T):
            s0, s1 = STEPS[step][0:2]
            tile, far = staged[step]
            nc.scalar.activation(
                out=tile[:, far : far + s1 - s0].bitcast(BF16)[:, t - 2 : 2 * (s1 - s0) : 2],
                in_=h[:, (t + 2) * T : (t + 2) * T + columns].indirect(tokens_of(s0, s1)),
                func=COPY,
            )

        def gather_pairs(target, s0, s1, u):
            on_vector(out=target, in_=pair_window[u].indirect(tokens_of(s0, s1)))

        def gather(step):
            s0, mid, s1 = STEPS[step]
            if step == LAST_STEP:
                for u in range(2):
                    gather_pairs(odd[:, u : 2 * (s1 - s0) : 2], s0, s1, u)
            else:
                tile, far = staged[step]
                gather_pairs(tile[:, 0 : s1 - s0], s0, s1, 0)
                if mid < s1:
                    gather_pairs(tile[:, far + mid - s0 : far + s1 - s0], mid, s1, 1)

        def join(step, c0, c1):
            tile, far = staged[step]
            nc.gpsimd.tensor_copy(
                out=joined[step % 2][:, 2 * c0 : 2 * c1].rearrange("p (c u) -> p c u", u=2),
                in_=tile[:, 0 : 2 * far].rearrange("p (u c) -> p c u", u=2)[:, c0:c1],
            )

        def quantise(step, s0, s1):
            words = odd[:] if step == LAST_STEP else joined[step % 2]
            first = STEPS[step][0]
            nc.vector.quantize_mx(
                out=h_codes[:, s0:s1].bitcast(FP8X4),
                scales=h_scales[:, s0:s1],
                in_=words[:, 2 * (s0 - first) : 2 * (s1 - first)].bitcast(BF16),
            )

        def multiply(nt, s0, s1, b):
            acc = bank(b)
            cuts = [s0] + list(range((s0 // C + 1) * C, s1, C)) + [s1]
            for c0, c1 in zip(cuts, cuts[1:]):
                nc.tensor.matmul_mx(
                    out=acc[:, c0 - s0 : c1 - s0],
                    lhsT=w2_codes[:, c0 // C, 2 * nt * P : 2 * (nt + 1) * P].bitcast(FP4X4),
                    lhsT_scale=w2_bytes[:, c0 // C, nt * P : (nt + 1) * P],
                    rhs=h_codes[:, c0:c1].bitcast(FP8X4),
                    rhs_scale=h_scales[:, c0:c1],
                    start=True,
                    stop=True,
                )
            return lambda copy: copy(out=y[nt][:, s0:s1], in_=acc[:, 0 : s1 - s0])

        for step in range(LAST_STEP):
            gather_plane(step, 2, T if step < 2 else T + HALF)
            gather_plane(step, 3)

        gather(0)
        join(0, 0, C)
        gather(1)
        quantise(0, 0, C)
        join(1, 0, 2 * C)
        for nt in range(N_TILES):
            multiply(nt, 0, C, nt)(on_scalar)
        gather(2)
        quantise(1, C, 3 * C)
        join(2, 0, C)
        join(2, C, 2 * C)
        for nt in range(2):
            multiply(nt, C, 3 * C, 4 + nt)(on_scalar)
        for_vector = [multiply(2, C, 3 * C, 6)]
        gather(LAST_STEP)

        def first_tile(step, s0, s1, b):
            quantise(step, s0, s1)
            multiply(0, s0, s1, b)(on_scalar)

        first_tile(2, 3 * C, 4 * C, 0)
        for_vector.append(multiply(1, 3 * C, 4 * C, 7))
        first_tile(LAST_STEP, 5 * C, S, 1)
        first_tile(2, 4 * C, 4 * C + P, 2)
        first_tile(2, 4 * C + P, 5 * C, 3)
        for empty in for_vector:
            empty(on_vector)
        multiply(1, 4 * C, S, 4)(on_scalar)
        rest2 = [multiply(2, 3 * C, 5 * C, 5), multiply(2, 5 * C, S, 0)]
        rest3 = [multiply(3, C, 3 * C, 1), multiply(3, 3 * C, 5 * C, 2), multiply(3, 5 * C, S, 3)]

        def row(name, columns=T):
            return keep.tile([P, columns], F32, name=name)

        def slots_of(r, t0, t1):
            return token_slot[r][:, t0 // LIST_ROWS : t1 // LIST_ROWS]

        def weighted(target, nt, r, t0=0, t1=T):
            nc.vector.tensor_tensor(out=target, in0=y[nt][:].indirect(slots_of(r, t0, t1)), in1=gates[:, r, t0:t1], op=MULT)

        def plain(target, nt, r):
            nc.scalar.activation(out=target, in_=y[nt][:].indirect(slots_of(r, 0, T)), func=COPY)

        def turn(acc, source, c0, c1, start=True, stop=True):
            for c in range(c0, c1):
                nc.tensor.matmul(
                    out=acc[:, (c - c0) * P : (c - c0 + 1) * P],
                    lhsT=source[:, c * P : (c + 1) * P],
                    rhs=ident[:],
                    start=start and c == c0,
                    stop=stop and c + 1 == c1,
                    is_transpose=True,
                )

        def scale(target, acc, r, c0, c1):
            for c in range(c0, c1):
                cols = slice(c * P, (c + 1) * P)
                nc.scalar.activation(out=target[:, cols], in_=acc[:, cols], func=COPY, scale=gate_columns[r][:, c : c + 1])

        def add(engine, target, a, b):
            engine.tensor_tensor(out=target, in0=a, in1=b, op=ADD)

        product = [row("product%d" % r) for r in range(TOP)]
        summed0 = row("summed0")
        scaled = {(nt, r): row("scaled%d_%d" % (nt, r)) for nt in (1, 2) for r in (1, 2)}
        picked = {(1, 1): row("picked1"), (1, 2): row("picked2"), (2, 1): product[2], (2, 2): scaled[1, 1]}
        late_row = row("late")
        direct_row = row("direct", T + HALF)
        direct = {1: direct_row[:, HALF : HALF + T], 2: direct_row[:, 0:T]}
        turned = {}
        blocks = T // P

        def turned_plain(nt, r, b):
            plain(picked[nt, r][:], nt, r)
            turned[nt, r] = bank(b)
            turn(turned[nt, r], picked[nt, r], 0, blocks)

        sum0 = bank(6)
        weighted(product[0][:], 0, 0)
        turn(sum0, product[0], 0, blocks, True, False)
        turned_plain(1, 1, 7)
        for empty in rest3:
            empty(on_scalar)
        weighted(product[1][:], 0, 1)
        turn(sum0, product[1], 0, blocks, False, False)
        turned_plain(1, 2, 4)
        weighted(product[2][:], 0, 2)
        turn(sum0, product[2], 0, blocks, False, True)
        on_scalar(out=summed0[:], in_=sum0[:])
        back0 = bank(2)
        turn(back0, summed0, 0, blocks)
        for empty in rest2:
            empty(on_scalar)
        scale(scaled[1, 1], turned[1, 1], 1, 0, blocks)
        back1 = bank(5)
        turn(back1, scaled[1, 1], 0, blocks, True, False)
        scale(scaled[1, 2], turned[1, 2], 2, 0, blocks)
        turn(back1, scaled[1, 2], 0, blocks, False, True)
        weighted(direct[1], 1, 0)
        turned_plain(2, 1, 1)

        sum3 = bank(4)
        early_row = row("early", TOP * HALF)
        for r in range(TOP):
            early = early_row[:, r * HALF : (r + 1) * HALF]
            weighted(early, 3, r, 0, HALF)
            turn(sum3, early, 0, HALF // P, r == 0, r == TOP - 1)
        turned_plain(2, 2, 6)
        summed3 = row("summed3", HALF)
        on_scalar(out=summed3[:], in_=sum3[:, 0:HALF])
        back3 = bank(3)
        turn(back3, summed3, 0, HALF // P)
        result3 = row("result3", 3 * P)
        on_scalar(out=result3[:, 0:HALF], in_=back3[:, 0:HALF])

        result0 = row("result0")
        on_vector(out=result0[:], in_=back0[:])
        nc.sync.dma_start(out=out[0:P, :], in_=result0[:])
        late = [late_row[:, 0:HALF], late_row[:, HALF:T], row("late2", HALF)[:]]
        for r in range(TOP):
            weighted(late[r], 3, r, HALF, T)
        partial = row("partial", HALF)
        add(nc.gpsimd, partial[:], late[0], late[1])
        result1 = row("result1")
        for cols in (slice(0, HALF), slice(HALF, T)):
            add(nc.vector, result1[:, cols], back1[:, cols], direct[1][:, cols])
        nc.sync.dma_start(out=out[P : 2 * P, :], in_=result1[:])
        add(nc.gpsimd, result3[:, HALF : 3 * P], partial[:, 0:P], late[2][:, 0:P])
        nc.sync.dma_start(out=out[3 * P : 4 * P, 0 : 3 * P], in_=result3[:])

        weighted(direct[2], 2, 0)
        scale(scaled[2, 1], turned[2, 1], 1, 0, blocks)
        pieces = ((0, 2), (3, 4), (2, 3))
        back2 = [bank(0), bank(7), bank(5)]
        for acc, (c0, c1) in zip(back2, pieces):
            turn(acc, scaled[2, 1], c0, c1, True, False)
        for acc, (c0, c1) in zip(back2, pieces):
            scale(scaled[2, 2], turned[2, 2], 2, c0, c1)
            turn(acc, scaled[2, 2], c0, c1, False, True)
        first_half, third, fourth = slice(0, HALF), slice(HALF, 3 * P), slice(3 * P, T)
        add(nc.vector, closing[:, 0, first_half], back2[0][:, 0:HALF], direct[2][:, first_half])
        nc.sync.dma_start(out=out[2 * P : 3 * P, first_half], in_=closing[:, 0, first_half])
        both_tiles = out[2 * P : 4 * P, :].rearrange("(b p) t -> p b t", p=P)
        add(nc.gpsimd, closing[:, 1, fourth], partial[:, P:HALF], late[2][:, P:HALF])
        add(nc.vector, closing[:, 0, fourth], back2[1][:, 0:P], direct[2][:, fourth])
        nc.sync.dma_start(out=both_tiles[:, :, fourth], in_=closing[:, 0:2, fourth])
        add(nc.vector, closing[:, 0, third], back2[2][:, 0:P], direct[2][:, third])
        nc.sync.dma_start(out=out[2 * P : 3 * P, third], in_=closing[:, 0, third])
